import numpy as np
import ml_dtypes


def mxq(x, axis, fmt="e4m3"):
    dtype, down = {"e4m3": (ml_dtypes.float8_e4m3fn, 7), "e5m2": (ml_dtypes.float8_e5m2, 14)}[fmt]
    v = np.moveaxis(np.asarray(x, np.float32).astype(ml_dtypes.bfloat16).astype(np.float64), axis, -1)
    blocks = v.reshape(v.shape[:-1] + (-1, 32))
    amax = np.abs(blocks).max(-1, keepdims=True)
    byte = np.maximum(np.where(amax > 0, np.frexp(amax)[1] - 1 + 127, 0) - down, 1)
    scale = np.exp2(byte - 127.0)
    codes = (blocks / scale).astype(np.float32).astype(dtype).astype(np.float64)
    return np.moveaxis((codes * scale).reshape(v.shape), -1, axis)


WIDE = False


def mx_kscale(k):
    if not WIDE:
        return np.ones(k)
    levels = np.array([10, -10, 5, -5, 0])
    if k % 512:
        return np.exp2(np.random.permutation(np.resize(levels, k // 32))).repeat(32)
    a = np.empty((k // 512, 16))
    for p in range(k // 512):
        a[p, :8] = np.random.permutation(np.resize(levels, 8))
        for g in range(8):
            far = levels[np.abs(levels - a[p, g]) >= 10]
            a[p, g + 8] = far[np.random.randint(len(far))]
    return np.exp2(a.ravel()).repeat(32)


def f64(x):
    return np.asarray(x).astype(np.float64)


def striped(idx):
    return np.tile(idx.reshape(-1, 16).T, (8, 1)).astype(np.uint16)


def unstriped(offs):
    return offs[:16].T.reshape(-1).astype(np.int64)


E2M1 = np.array([0.0, 0.5, 1.0, 1.5, 2.0, 3.0, 4.0, 6.0, -0.0, -0.5, -1.0, -1.5, -2.0, -3.0, -4.0, -6.0])


def pack_weight(w, fmt):
    k, n = w.shape
    w = f64(np.asarray(w, np.float32).astype(ml_dtypes.bfloat16)).reshape(k // 32, 32, n)
    amax = np.abs(w).max(1)
    if fmt == "e4m3":
        byte = np.frexp(amax)[1] - 1 + 127 - 7
    else:
        mant, ex = np.frexp(amax / 6.0)
        byte = np.where(mant > 0.5, ex, ex - 1) + 127
    byte = np.clip(np.where(amax > 0, byte, 1), 1, 254)
    scaled = (w * np.exp2(127.0 - byte)[:, None, :]).reshape(k, n).astype(np.float32)
    by_word = np.ascontiguousarray(scaled.reshape(k // 512, 128, 4, n).transpose(0, 1, 3, 2))
    if fmt == "e4m3":
        words = by_word.astype(ml_dtypes.float8_e4m3fn).view(np.uint8)
    else:
        c = by_word.astype(ml_dtypes.float4_e2m1fn).view(np.uint8) & 0xF
        words = (c[..., 0::2] | (c[..., 1::2] << 4)).reshape(k // 512, 128, 2 * n)
    return np.ascontiguousarray(words), np.ascontiguousarray(byte.astype(np.uint8).reshape(k // 512, 16, n))


def unpack_weight(words, scales, fmt):
    g, _, n = scales.shape
    words = np.ascontiguousarray(words).reshape(g, 128, n, -1)
    if fmt == "e4m3":
        vals = words.view(ml_dtypes.float8_e4m3fn).astype(np.float64)
    else:
        nib = np.empty((g, 128, n, 4), np.uint8)
        nib[..., 0::2] = words & 0xF
        nib[..., 1::2] = words >> 4
        vals = E2M1[nib]
    vals = vals * np.repeat(np.exp2(scales.astype(np.float64) - 127.0), 8, axis=1)[..., None]
    return vals.transpose(0, 1, 3, 2).reshape(g * 512, n)


def gelu(v):
    return 0.5 * v * (1.0 + np.tanh(np.sqrt(2.0 / np.pi) * (v + 0.044715 * v**3)))


def striped8(idx):
    return np.concatenate([v.reshape(-1, 16).T for v in idx]).astype(np.uint16)


def unstriped8(offs):
    return np.stack([offs[16 * g:16 * g + 16].T.reshape(-1) for g in range(8)]).astype(np.int64)


def put_heads(h, wgs, idx8, t2):
    r = np.arange(h.shape[0])
    page = np.zeros((h.shape[0], t2))
    page[r[:, None], idx8[r % 512 // 64]] = wgs[r // 4 % 128] * h
    return page


K, T, S, T2, H, N = 1024, 2048, 512, 1024, 1024, 512

def setup_inputs():
    n = np.random.standard_normal
    s = mx_kscale(K)[:, None]
    u = mx_kscale(H)[:, None]
    tab_words, tab_scales = pack_weight(n((K, T)) * s, "e4m3")
    w1_words, w1_scales = pack_weight(n((K, H)) / np.sqrt(K) / s * u.T, "e2m1")
    w2 = (n((K, H)) / np.sqrt(K) / s * u.T).astype(np.float32)
    w3_words, w3_scales = pack_weight(n((H, N)) / np.sqrt(H) / u, "e4m3")
    return {
        "tab_words": tab_words, "tab_scales": tab_scales,
        "offs": striped(np.random.permutation(T)[:S]),
        "w1_words": w1_words, "w1_scales": w1_scales,
        "w2": w2,
        "offs2": striped8(np.stack([np.random.permutation(T2)[:S] for _ in range(8)])),
        "wgs": np.repeat(np.random.uniform(0.5, 2.0, (8, S)), 16, axis=0).astype(np.float32),
        "lim": ((1.0 + 0.5 * n((H, T2))) * u).astype(np.float32),
        "w3_words": w3_words, "w3_scales": w3_scales,
    }

def reference(tab_words, tab_scales, offs, w1_words, w1_scales, w2, offs2, wgs, lim, w3_words, w3_scales):
    v = unpack_weight(tab_words, tab_scales, "e4m3")[:, unstriped(offs)]
    w1 = unpack_weight(w1_words, w1_scales, "e2m1")
    w3 = unpack_weight(w3_words, w3_scales, "e4m3")
    d1 = w1.T @ v
    d2 = mxq(f64(w2), 0, "e4m3").T @ v
    h = np.maximum(d1, d2)
    page = put_heads(h, f64(wgs), unstriped8(offs2), T2)
    z = f64(lim) - page
    y = w3.T @ mxq(z, 0, "e4m3")
    return np.square(y)

@@ -1,0 +1,346 @@
+from contextlib import ExitStack
+
+import concourse.mybir as mybir
+from concourse.masks import make_identity
+
+K, T, S, T2, H, N = 1024, 2048, 512, 1024, 1024, 512
+FLOPS = 2 * (2 * K * H * S + H * N * T2)
+
+F32 = mybir.dt.float32
+BF16 = mybir.dt.bfloat16
+I32 = mybir.dt.int32
+U32 = mybir.dt.uint32
+U16 = mybir.dt.uint16
+U8 = mybir.dt.uint8
+FP8X4 = mybir.dt.float8_e4m3fn_x4
+FP4X4 = mybir.dt.float4_e2m1fn_x4
+ALU = mybir.AluOpType
+ACT = mybir.ActivationFunctionType
+
+P = 128
+PASS = 512
+CH = 256
+NCH = T2 // CH
+
+
+def tile_list_stowage_bay_score_kernel(tc, tab_words, tab_scales, offs, w1_words, w1_scales, w2, offs2, wgs, lim, w3_words, w3_scales, out):
+    nc = tc.nc
+    with ExitStack() as ctx:
+        lists = ctx.enter_context(tc.tile_pool(name="lists", bufs=1))
+        keep = ctx.enter_context(tc.tile_pool(name="keep", bufs=1))
+        ring = ctx.enter_context(tc.tile_pool(name="ring", bufs=2))
+        psum = ctx.enter_context(tc.psum_pool(name="psum", bufs=2))
+
+        def held(shape, dtype, name, tag=None):
+            return keep.tile(shape, dtype, name=name, tag=tag or name, align_bytes=64)
+
+        def load_scales(tile, src):
+            for q in range(4):
+                nc.sync.dma_start(
+                    out=tile[32 * q : 32 * q + 4, :].bitcast(I32).rearrange("r (a c) -> r a c", a=2),
+                    in_=src[:, 4 * q : 4 * q + 4, :].rearrange("a r c -> r a c").bitcast(I32),
+                )
+
+        tab_s = held([P, 2 * T], U8, "tab_s")
+        w1_s_raw = held([P, 2 * H], U8, "w1_s_raw")
+        w3_s = held([P, 2 * N], U8, "w3_s")
+        nc.vector.memset(tab_s[:].bitcast(I32), 0)
+        nc.gpsimd.memset(w1_s_raw[:].bitcast(I32), 0)
+        nc.vector.memset(w3_s[:].bitcast(I32), 0)
+
+        warm = held([P, 8], F32, "warm")
+        warm2 = held([P, 8], F32, "warm2")
+        nc.vector.memset(warm[:], 0.0)
+        nc.scalar.activation(warm2[:], warm[:], ACT.Square)
+
+        ident = held([P, P], F32, "ident")
+        make_identity(nc, ident[:])
+        pages = [held([P, T2], F32, "page%d" % i) for i in range(4)]
+        for page in pages:
+            nc.gpsimd.memset(page[:], 0.0)
+
+        idx = lists.tile([P, S // 16], U16, name="idx")
+        idx2 = lists.tile([P, S // 16], U16, name="idx2")
+        nc.sync.dma_start(idx[:], offs)
+        w1_w_raw = held([P, H], I32, "w1_w_raw")
+        nc.sync.dma_start(
+            out=w1_w_raw[:].rearrange("p (a c) -> p a c", a=2),
+            in_=w1_words.rearrange("a p c -> p a c").bitcast(I32),
+        )
+        tab_w = [held([P, T], I32, "tab_w%d" % a) for a in range(2)]
+        load_scales(tab_s, tab_scales)
+        nc.sync.dma_start(out=tab_w[0][:], in_=tab_words[0].rearrange("p t i -> p (t i)").bitcast(I32))
+        nc.sync.dma_start(out=tab_w[1][:], in_=tab_words[1].rearrange("p t i -> p (t i)").bitcast(I32))
+        load_scales(w1_s_raw, w1_scales)
+
+        w2_raw = {}
+
+        def load_w2(b, a, c0, c1):
+            raw = held([P, 4, c1 - c0], F32, "w2_raw%d%d_%d" % (b, a, c0))
+            nc.sync.dma_start(
+                out=raw[:],
+                in_=w2[PASS * a : PASS * (a + 1), PASS * b + c0 : PASS * b + c1].rearrange("(p j) c -> p j c", j=4),
+            )
+            w2_raw[(b, a, c0)] = raw
+
+        lim_t = {}
+
+        def load_lim(b, u):
+            tile = held([P, 2, T2], F32, "lim%d%d" % (b, u))
+            nc.sync.dma_start(
+                out=tile[:],
+                in_=lim[PASS * b : PASS * (b + 1), :].rearrange("(p i) m -> p i m", i=4)[:, 2 * u : 2 * u + 2, :],
+            )
+            lim_t[(b, u)] = tile
+
+        load_w2(0, 0, 0, 512)
+        load_w2(0, 1, 0, 256)
+        load_w2(0, 1, 256, 512)
+        nc.sync.dma_start(idx2[:], offs2)
+        wgt = held([P, S], F32, "wgt")
+        nc.sync.dma_start(out=wgt[:], in_=wgs)
+        load_w2(1, 0, 0, 512)
+        load_w2(1, 1, 0, 512)
+        load_lim(0, 0)
+        load_lim(0, 1)
+        w3_w = held([P, 2 * N], I32, "w3_w")
+        nc.sync.dma_start(
+            out=w3_w[:].rearrange("p (b c) -> p b c", b=2),
+            in_=w3_words.rearrange("b p c i -> p b (c i)").bitcast(I32),
+        )
+        load_scales(w3_s, w3_scales)
+        load_lim(1, 0)
+        load_lim(1, 1)
+
+        w1_w = held([P, 4 * H], U8, "w1_w")
+        w1_s = held([P, 2 * H], U8, "w1_s")
+        nc.vector.tensor_copy(
+            out=w1_w[:].bitcast(U16).rearrange("p (g t m) -> p g m t", g=4, t=4),
+            in_=w1_w_raw[:].bitcast(U16).rearrange("p (g m t) -> p g m t", g=4, t=4),
+        )
+
+        v_w = [held([P, S], U32, "v_w%d" % a) for a in range(2)]
+        v_s = [held([P, S], U8, "v_s%d" % a) for a in range(2)]
+        for a in range(2):
+            nc.vector.tensor_copy(v_s[a][:], tab_s[:, a * T : (a + 1) * T].indirect(idx[:]))
+        for a in range(2):
+            nc.vector.tensor_copy(v_w[a][:], tab_w[a][:].bitcast(U32).indirect(idx[:]))
+
+        nc.vector.tensor_copy(
+            out=w1_s[:].rearrange("p (g t m) -> p g m t", g=4, t=4),
+            in_=w1_s_raw[:].rearrange("p (g m t) -> p g m t", g=4, t=4),
+        )
+
+        w2_g = {}
+        w2_w = {}
+        w2_s = {}
+
+        def cast_w2(b, a, c0, lo, hi, on_vector):
+            if (b, a) not in w2_g:
+                w2_g[(b, a)] = held([P, 4 * PASS], BF16, "w2_g%d%d" % (b, a))
+            dst = w2_g[(b, a)][:].rearrange("p (t m j) -> p m j t", t=4, j=4)[:, lo // 4 : hi // 4]
+            src = w2_raw[(b, a, c0)][:, :, lo - c0 : hi - c0].rearrange("p j (m t) -> p m j t", t=4)
+            if on_vector:
+                nc.vector.tensor_copy(out=dst, in_=src)
+            else:
+                nc.scalar.copy(out=dst, in_=src)
+
+        def quantize_w2(b, a, t0, t1):
+            if (b, a) not in w2_w:
+                w2_w[(b, a)] = held([P, PASS], U32, "w2_w%d%d" % (b, a))
+                w2_s[(b, a)] = held([P, PASS], U8, "w2_s%d%d" % (b, a))
+            nc.vector.quantize_mx(
+                out=w2_w[(b, a)][:, P * t0 : P * t1].bitcast(FP8X4),
+                scales=w2_s[(b, a)][:, P * t0 : P * t1],
+                in_=w2_g[(b, a)][:, 4 * P * t0 : 4 * P * t1],
+            )
+
+        cast_w2(0, 0, 0, 0, 256, False)
+        cast_w2(0, 0, 0, 256, 512, True)
+        cast_w2(0, 1, 0, 0, 256, True)
+        quantize_w2(0, 0, 0, 4)
+        cast_w2(0, 1, 256, 256, 512, True)
+        quantize_w2(0, 1, 0, 2)
+        quantize_w2(0, 1, 2, 4)
+
+        neg_h = {}
+
+        d2 = {}
+        neg_d1 = {}
+
+        def products(k):
+            pair = (2 * k, 2 * k + 1)
+            for s in pair:
+                b, i = divmod(s, 4)
+                d1 = psum.tile([P, S], F32, name="d1", tag="d1")
+                for a in range(2):
+                    col = (2 * a + b) * PASS + i * P
+                    nc.tensor.matmul_mx(
+                        out=d1[:],
+                        lhsT=w1_w[:, 2 * col : 2 * (col + P)].bitcast(FP4X4),
+                        lhsT_scale=w1_s[:, col : col + P],
+                        rhs=v_w[a][:].bitcast(FP8X4),
+                        rhs_scale=v_s[a][:],
+                        start=(a == 0),
+                        stop=(a == 1),
+                    )
+                if s < 2:
+                    neg_d1[s] = held([P, S], F32, "neg_d1_%d" % s, tag="w2_raw0%d_0" % s)
+                else:
+                    neg_d1[s] = ring.tile([P, S], F32, name="neg_d1")
+                nc.scalar.activation(neg_d1[s][:], d1[:], ACT.Copy, scale=-1.0)
+                d2[s] = psum.tile([P, S], F32, name="d2", tag="d2")
+            for a in range(2):
+                for s in pair:
+                    b, i = divmod(s, 4)
+                    nc.tensor.matmul_mx(
+                        out=d2[s][:],
+                        lhsT=w2_w[(b, a)][:, i * P : (i + 1) * P].bitcast(FP8X4),
+                        lhsT_scale=w2_s[(b, a)][:, i * P : (i + 1) * P],
+                        rhs=v_w[a][:].bitcast(FP8X4),
+                        rhs_scale=v_s[a][:],
+                        start=(a == 0),
+                        stop=(a == 1),
+                    )
+
+        def larger(s):
+            if s == 2:
+                neg_h[s] = held([P, S], F32, "neg_h2", tag="w2_g11")
+            elif s == 3:
+                neg_h[s] = held([P, S], F32, "neg_h3", tag="w2_g10")
+            elif s == 7:
+                neg_h[s] = held([P, S], F32, "neg_h7", tag="z03")
+            else:
+                neg_h[s] = ring.tile([P, S], F32, name="neg_h")
+            nc.vector.scalar_tensor_tensor(
+                out=neg_h[s][:], in0=d2[s][:], scalar=-1.0, in1=neg_d1[s][:], op0=ALU.mult, op1=ALU.min
+            )
+
+        def scatter(s):
+            nc.vector.tensor_tensor(pages[s % 4][:].indirect(idx2[:]), neg_h[s][:], wgt[:], ALU.mult)
+
+        z_t = [held([P, 512], F32, "z_t%d" % c) for c in range(NCH)]
+
+        def turned_sum(bank, terms):
+            n = len(terms)
+            for k, (slot, src) in enumerate(terms):
+                nc.tensor.matmul(
+                    out=bank[:, slot * P : (slot + 1) * P], lhsT=src, rhs=ident[:],
+                    is_transpose=True, start=(k == 0), stop=(k == n - 1),
+                )
+
+        def subtract_pair(b, u):
+            for c in range(NCH):
+                bank = psum.tile([P, 512], F32, name="t1", tag="t1")
+                terms = []
+                for e in range(2):
+                    for mb in range(2):
+                        m0 = c * CH + mb * P
+                        terms.append((2 * mb + e, lim_t[(b, u)][:, e, m0 : m0 + P]))
+                for e in range(2):
+                    for mb in range(2):
+                        m0 = c * CH + mb * P
+                        terms.append((2 * mb + e, pages[2 * u + e][:, m0 : m0 + P]))
+                turned_sum(bank, terms)
+                nc.scalar.copy(
+                    out=z_t[c][:].bitcast(BF16).rearrange("m (mb u q e) -> m mb u q e", mb=2, u=2, e=2)[:, :, u],
+                    in_=bank[:].rearrange("m (mb e q) -> m mb q e", mb=2, e=2),
+                )
+
+        def subtract_single(b, u):
+            for half in range(2):
+                bank = psum.tile([P, 512], F32, name="t1", tag="t1")
+                terms = []
+                for mb in range(4):
+                    m0 = half * 2 * CH + mb * P
+                    terms.append((mb, lim_t[(b, u)][:, 0, m0 : m0 + P]))
+                for mb in range(4):
+                    m0 = half * 2 * CH + mb * P
+                    terms.append((mb, pages[2 * u][:, m0 : m0 + P]))
+                turned_sum(bank, terms)
+                for cc in range(2):
+                    c = 2 * half + cc
+                    nc.scalar.copy(
+                        out=z_t[c][:].bitcast(BF16).rearrange("m (mb u q e) -> m mb u q e", mb=2, u=2, e=2)[:, :, u, :, 0],
+                        in_=bank[:, cc * CH : (cc + 1) * CH].rearrange("m (mb q) -> m mb q", mb=2),
+                    )
+
+        z = {}
+        z_w = {}
+        z_s = {}
+
+        def turn_back(b):
+            for c in range(NCH):
+                bank = psum.tile([P, 512], F32, name="t2", tag="t2")
+                for u in range(2):
+                    for mb in range(2):
+                        w0 = (2 * mb + u) * P
+                        nc.tensor.transpose(bank[:, u * CH + mb * P : u * CH + (mb + 1) * P], z_t[c][:, w0 : w0 + P], ident[:])
+                z[(b, c)] = held([P, 4 * CH], BF16, "z%d%d" % (b, c))
+                nc.scalar.copy(
+                    out=z[(b, c)][:].bitcast(F32).rearrange("p (m u) -> p m u", u=2),
+                    in_=bank[:].rearrange("p (u m) -> p m u", u=2),
+                )
+
+        def quantize_z(b, c):
+            z_w[(b, c)] = held([P, CH], U32, "z_w%d%d" % (b, c))
+            z_s[(b, c)] = held([P, CH], U8, "z_s%d%d" % (b, c))
+            nc.vector.quantize_mx(out=z_w[(b, c)][:].bitcast(FP8X4), scales=z_s[(b, c)][:], in_=z[(b, c)][:])
+
+        y = {}
+
+        def score(b, c):
+            for hf in range(2):
+                if b == 0:
+                    y[(c, hf)] = psum.tile([P, 512], F32, name="y", tag=(("d1", "d2"), ("d1", "d2"), ("t1", "t1"), ("t2", "t2"))[c][hf])
+                for nt in range(2):
+                    col = b * N + (2 * hf + nt) * P
+                    nc.tensor.matmul_mx(
+                        out=y[(c, hf)][:, nt * CH : (nt + 1) * CH],
+                        lhsT=w3_w[:, col : col + P].bitcast(FP8X4),
+                        lhsT_scale=w3_s[:, col : col + P],
+                        rhs=z_w[(b, c)][:].bitcast(FP8X4),
+                        rhs_scale=z_s[(b, c)][:],
+                        start=(b == 0 and nt == 0),
+                        stop=(b == 1 and nt == 1),
+                    )
+
+        products(0)
+        for k in range(4):
+            if k == 1:
+                for a in range(2):
+                    cast_w2(1, a, 0, 0, 256, False)
+                    cast_w2(1, a, 0, 256, 512, False)
+                    quantize_w2(1, a, 0, 4)
+            if k == 3:
+                for c in range(NCH):
+                    quantize_z(0, c)
+            larger(2 * k)
+            larger(2 * k + 1)
+            if k < 3:
+                products(k + 1)
+            if k > 0:
+                subtract_pair((k - 1) // 2, (k - 1) % 2)
+            if k == 2:
+                turn_back(0)
+            scatter(2 * k)
+            if k == 3:
+                subtract_single(1, 1)
+                turn_back(1)
+            scatter(2 * k + 1)
+        for c in range(NCH):
+            score(0, c)
+        for c in range(NCH):
+            cols = slice(c * CH, (c + 1) * CH)
+            nc.vector.tensor_tensor(
+                z[(1, c)][:].rearrange("p (m i) -> p m i", i=4)[:, :, 3], lim_t[(1, 1)][:, 1, cols], pages[3][:, cols], ALU.add
+            )
+            quantize_z(1, c)
+            score(1, c)
+            for hf in range(2):
+                res = held([P, 2 * CH], F32, "res%d%d" % (c, hf))
+                nc.scalar.activation(res[:], y[(c, hf)][:], ACT.Square)
+                nc.sync.dma_start(
+                    out=out[2 * P * hf : 2 * P * (hf + 1), cols].rearrange("(n p) m -> p n m", p=P),
+                    in_=res[:].rearrange("p (n m) -> p n m", n=2),
+                )

@@ -62,11 +62,15 @@ def tile_list_stowage_bay_score_kernel(tc, tab_words, tab_scales, offs, w1_words
         idx = lists.tile([P, S // 16], U16, name="idx")
         idx2 = lists.tile([P, S // 16], U16, name="idx2")
         nc.sync.dma_start(idx[:], offs)
-        w1_w_raw = held([P, H], I32, "w1_w_raw")
-        nc.sync.dma_start(
-            out=w1_w_raw[:].rearrange("p (a c) -> p a c", a=2),
-            in_=w1_words.rearrange("a p c -> p a c").bitcast(I32),
-        )
+        w1_w_raw = [held([P, H // 2], I32, "w1_w_raw%d" % b) for b in range(2)]
+
+        def load_w1(b):
+            nc.sync.dma_start(
+                out=w1_w_raw[b][:].rearrange("p (a c) -> p a c", a=2),
+                in_=w1_words[:, :, H * b : H * (b + 1)].rearrange("a p c -> p a c").bitcast(I32),
+            )
+
+        load_w1(0)
         tab_w = [held([P, T], I32, "tab_w%d" % a) for a in range(2)]
         load_scales(tab_s, tab_scales)
         nc.sync.dma_start(out=tab_w[0][:], in_=tab_words[0].rearrange("p t i -> p (t i)").bitcast(I32))
@@ -85,13 +89,13 @@ def tile_list_stowage_bay_score_kernel(tc, tab_words, tab_scales, offs, w1_words
 
         lim_t = {}
 
-        def load_lim(b, u):
-            tile = held([P, 2, T2], F32, "lim%d%d" % (b, u))
+        def load_lim(s):
+            b, i = divmod(s, 4)
+            lim_t[s] = held([P, T2], F32, "lim%d" % s)
             nc.sync.dma_start(
-                out=tile[:],
-                in_=lim[PASS * b : PASS * (b + 1), :].rearrange("(p i) m -> p i m", i=4)[:, 2 * u : 2 * u + 2, :],
+                out=lim_t[s][:],
+                in_=lim[PASS * b : PASS * (b + 1), :].rearrange("(p i) m -> p i m", i=4)[:, i, :],
             )
-            lim_t[(b, u)] = tile
 
         load_w2(0, 0, 0, 512)
         load_w2(0, 1, 0, 256)
@@ -99,25 +103,36 @@ def tile_list_stowage_bay_score_kernel(tc, tab_words, tab_scales, offs, w1_words
         nc.sync.dma_start(idx2[:], offs2)
         wgt = held([P, S], F32, "wgt")
         nc.sync.dma_start(out=wgt[:], in_=wgs)
+        load_w1(1)
         load_w2(1, 0, 0, 512)
         load_w2(1, 1, 0, 512)
-        load_lim(0, 0)
-        load_lim(0, 1)
+        for s in range(4):
+            load_lim(s)
         w3_w = held([P, 2 * N], I32, "w3_w")
         nc.sync.dma_start(
             out=w3_w[:].rearrange("p (b c) -> p b c", b=2),
             in_=w3_words.rearrange("b p c i -> p b (c i)").bitcast(I32),
         )
         load_scales(w3_s, w3_scales)
-        load_lim(1, 0)
-        load_lim(1, 1)
+        for s in range(4, 8):
+            load_lim(s)
 
-        w1_w = held([P, 4 * H], U8, "w1_w")
-        w1_s = held([P, 2 * H], U8, "w1_s")
-        nc.vector.tensor_copy(
-            out=w1_w[:].bitcast(U16).rearrange("p (g t m) -> p g m t", g=4, t=4),
-            in_=w1_w_raw[:].bitcast(U16).rearrange("p (g m t) -> p g m t", g=4, t=4),
-        )
+        w1_w = [held([P, 2 * H], U8, "w1_w%d" % b) for b in range(2)]
+        w1_s = [held([P, H], U8, "w1_s%d" % b) for b in range(2)]
+
+        def order_w1_words(b):
+            nc.vector.tensor_copy(
+                out=w1_w[b][:].bitcast(U16).rearrange("p (a t m) -> p a m t", a=2, t=4),
+                in_=w1_w_raw[b][:].bitcast(U16).rearrange("p (a m t) -> p a m t", a=2, t=4),
+            )
+
+        def order_w1_scales(b):
+            nc.vector.tensor_copy(
+                out=w1_s[b][:].rearrange("p (a t m) -> p a m t", a=2, t=4),
+                in_=w1_s_raw[:].rearrange("p (a b m t) -> p b a m t", a=2, b=2, t=4)[:, b],
+            )
+
+        order_w1_words(0)
 
         v_w = [held([P, S], U32, "v_w%d" % a) for a in range(2)]
         v_s = [held([P, S], U8, "v_s%d" % a) for a in range(2)]
@@ -126,19 +141,18 @@ def tile_list_stowage_bay_score_kernel(tc, tab_words, tab_scales, offs, w1_words
         for a in range(2):
             nc.vector.tensor_copy(v_w[a][:], tab_w[a][:].bitcast(U32).indirect(idx[:]))
 
-        nc.vector.tensor_copy(
-            out=w1_s[:].rearrange("p (g t m) -> p g m t", g=4, t=4),
-            in_=w1_s_raw[:].rearrange("p (g m t) -> p g m t", g=4, t=4),
-        )
+        order_w1_scales(0)
+        order_w1_scales(1)
 
-        w2_g = {}
+        rounded = held([P, 8 * PASS], BF16, "rounded")
+        w2_g = {(0, a): rounded[:, 4 * PASS * a : 4 * PASS * (a + 1)] for a in range(2)}
         w2_w = {}
         w2_s = {}
 
         def cast_w2(b, a, c0, lo, hi, on_vector):
             if (b, a) not in w2_g:
                 w2_g[(b, a)] = held([P, 4 * PASS], BF16, "w2_g%d%d" % (b, a))
-            dst = w2_g[(b, a)][:].rearrange("p (t m j) -> p m j t", t=4, j=4)[:, lo // 4 : hi // 4]
+            dst = w2_g[(b, a)][:, :].rearrange("p (t m j) -> p m j t", t=4, j=4)[:, lo // 4 : hi // 4]
             src = w2_raw[(b, a, c0)][:, :, lo - c0 : hi - c0].rearrange("p j (m t) -> p m j t", t=4)
             if on_vector:
                 nc.vector.tensor_copy(out=dst, in_=src)
@@ -155,13 +169,14 @@ def tile_list_stowage_bay_score_kernel(tc, tab_words, tab_scales, offs, w1_words
                 in_=w2_g[(b, a)][:, 4 * P * t0 : 4 * P * t1],
             )
 
-        cast_w2(0, 0, 0, 0, 256, False)
-        cast_w2(0, 0, 0, 256, 512, True)
-        cast_w2(0, 1, 0, 0, 256, True)
-        quantize_w2(0, 0, 0, 4)
+        cast_w2(0, 0, 0, 0, 512, True)
+        cast_w2(0, 1, 0, 0, 256, False)
+        quantize_w2(0, 0, 0, 2)
         cast_w2(0, 1, 256, 256, 512, True)
+        quantize_w2(0, 0, 2, 4)
         quantize_w2(0, 1, 0, 2)
         quantize_w2(0, 1, 2, 4)
+        order_w1_words(1)
 
         neg_h = {}
 
@@ -174,18 +189,18 @@ def tile_list_stowage_bay_score_kernel(tc, tab_words, tab_scales, offs, w1_words
                 b, i = divmod(s, 4)
                 d1 = psum.tile([P, S], F32, name="d1", tag="d1")
                 for a in range(2):
-                    col = (2 * a + b) * PASS + i * P
+                    col = a * PASS + i * P
                     nc.tensor.matmul_mx(
                         out=d1[:],
-                        lhsT=w1_w[:, 2 * col : 2 * (col + P)].bitcast(FP4X4),
-                        lhsT_scale=w1_s[:, col : col + P],
+                        lhsT=w1_w[b][:, 2 * col : 2 * (col + P)].bitcast(FP4X4),
+                        lhsT_scale=w1_s[b][:, col : col + P],
                         rhs=v_w[a][:].bitcast(FP8X4),
                         rhs_scale=v_s[a][:],
                         start=(a == 0),
                         stop=(a == 1),
                     )
                 if s < 2:
-                    neg_d1[s] = held([P, S], F32, "neg_d1_%d" % s, tag="w2_raw0%d_0" % s)
+                    neg_d1[s] = held([P, S], F32, "neg_d1_%d" % s, tag="w2_raw01_%d" % (256 * s))
                 else:
                     neg_d1[s] = ring.tile([P, S], F32, name="neg_d1")
                 nc.scalar.activation(neg_d1[s][:], d1[:], ACT.Copy, scale=-1.0)
@@ -221,56 +236,29 @@ def tile_list_stowage_bay_score_kernel(tc, tab_words, tab_scales, offs, w1_words
 
         z_t = [held([P, 512], F32, "z_t%d" % c) for c in range(NCH)]
 
-        def turned_sum(bank, terms):
-            n = len(terms)
-            for k, (slot, src) in enumerate(terms):
-                nc.tensor.matmul(
-                    out=bank[:, slot * P : (slot + 1) * P], lhsT=src, rhs=ident[:],
-                    is_transpose=True, start=(k == 0), stop=(k == n - 1),
-                )
-
-        def subtract_pair(b, u):
+        def subtract(s):
+            u, e = divmod(s % 4, 2)
+            banks = [psum.tile([P, 512], F32, name="t1", tag="t1") for half in range(2)]
+            for term, src in enumerate((lim_t[s], pages[s % 4])):
+                for half in range(2):
+                    for mb in range(4):
+                        m0 = (4 * half + mb) * P
+                        nc.tensor.matmul(
+                            out=banks[half][:, mb * P : (mb + 1) * P], lhsT=src[:, m0 : m0 + P], rhs=ident[:],
+                            is_transpose=True, start=(term == 0 and mb == 0), stop=(term == 1 and mb == 3),
+                        )
             for c in range(NCH):
-                bank = psum.tile([P, 512], F32, name="t1", tag="t1")
-                terms = []
-                for e in range(2):
-                    for mb in range(2):
-                        m0 = c * CH + mb * P
-                        terms.append((2 * mb + e, lim_t[(b, u)][:, e, m0 : m0 + P]))
-                for e in range(2):
-                    for mb in range(2):
-                        m0 = c * CH + mb * P
-                        terms.append((2 * mb + e, pages[2 * u + e][:, m0 : m0 + P]))
-                turned_sum(bank, terms)
                 nc.scalar.copy(
-                    out=z_t[c][:].bitcast(BF16).rearrange("m (mb u q e) -> m mb u q e", mb=2, u=2, e=2)[:, :, u],
-                    in_=bank[:].rearrange("m (mb e q) -> m mb q e", mb=2, e=2),
+                    out=z_t[c][:].bitcast(BF16).rearrange("m (mb u q e) -> m mb u q e", mb=2, u=2, e=2)[:, :, u, :, e],
+                    in_=banks[c // 2][:, (c % 2) * CH : (c % 2 + 1) * CH].rearrange("m (mb q) -> m mb q", mb=2),
                 )
-
-        def subtract_single(b, u):
-            for half in range(2):
-                bank = psum.tile([P, 512], F32, name="t1", tag="t1")
-                terms = []
-                for mb in range(4):
-                    m0 = half * 2 * CH + mb * P
-                    terms.append((mb, lim_t[(b, u)][:, 0, m0 : m0 + P]))
-                for mb in range(4):
-                    m0 = half * 2 * CH + mb * P
-                    terms.append((mb, pages[2 * u][:, m0 : m0 + P]))
-                turned_sum(bank, terms)
-                for cc in range(2):
-                    c = 2 * half + cc
-                    nc.scalar.copy(
-                        out=z_t[c][:].bitcast(BF16).rearrange("m (mb u q e) -> m mb u q e", mb=2, u=2, e=2)[:, :, u, :, 0],
-                        in_=bank[:, cc * CH : (cc + 1) * CH].rearrange("m (mb q) -> m mb q", mb=2),
-                    )
 
         z = {}
         z_w = {}
         z_s = {}
 
-        def turn_back(b):
-            for c in range(NCH):
+        def turn_back(b, chunks):
+            for c in chunks:
                 bank = psum.tile([P, 512], F32, name="t2", tag="t2")
                 for u in range(2):
                     for mb in range(2):
@@ -282,6 +270,16 @@ def tile_list_stowage_bay_score_kernel(tc, tab_words, tab_scales, offs, w1_words
                     in_=bank[:].rearrange("p (u m) -> p m u", u=2),
                 )
 
+        def subtract_rows(s):
+            nc.vector.tensor_tensor(rounded[:, (s % 4) * T2 : (s % 4 + 1) * T2], lim_t[s][:], pages[s % 4][:], ALU.add)
+
+        def interleave(c):
+            z[(1, c)] = held([P, 4 * CH], BF16, "z1%d" % c)
+            nc.scalar.copy(
+                out=z[(1, c)][:].rearrange("p (g m i) -> p g i m", m=4, i=4),
+                in_=rounded[:].rearrange("p (i g m) -> p g i m", i=4, m=4)[:, c * CH // 4 : (c + 1) * CH // 4],
+            )
+
         def quantize_z(b, c):
             z_w[(b, c)] = held([P, CH], U32, "z_w%d%d" % (b, c))
             z_s[(b, c)] = held([P, CH], U8, "z_s%d%d" % (b, c))
@@ -289,10 +287,10 @@ def tile_list_stowage_bay_score_kernel(tc, tab_words, tab_scales, offs, w1_words
 
         y = {}
 
-        def score(b, c):
+        def score(b, c, first):
             for hf in range(2):
-                if b == 0:
-                    y[(c, hf)] = psum.tile([P, 512], F32, name="y", tag=(("d1", "d2"), ("d1", "d2"), ("t1", "t1"), ("t2", "t2"))[c][hf])
+                if first:
+                    y[(c, hf)] = psum.tile([P, 512], F32, name="y", tag=("t1", "t2", "d1", "d2")[c])
                 for nt in range(2):
                     col = b * N + (2 * hf + nt) * P
                     nc.tensor.matmul_mx(
@@ -301,8 +299,8 @@ def tile_list_stowage_bay_score_kernel(tc, tab_words, tab_scales, offs, w1_words
                         lhsT_scale=w3_s[:, col : col + P],
                         rhs=z_w[(b, c)][:].bitcast(FP8X4),
                         rhs_scale=z_s[(b, c)][:],
-                        start=(b == 0 and nt == 0),
-                        stop=(b == 1 and nt == 1),
+                        start=(first and nt == 0),
+                        stop=(not first and nt == 1),
                     )
 
         products(0)
@@ -312,6 +310,7 @@ def tile_list_stowage_bay_score_kernel(tc, tab_words, tab_scales, offs, w1_words
                     cast_w2(1, a, 0, 0, 256, False)
                     cast_w2(1, a, 0, 256, 512, False)
                     quantize_w2(1, a, 0, 4)
+                subtract(0)
             if k == 3:
                 for c in range(NCH):
                     quantize_z(0, c)
@@ -319,24 +318,30 @@ def tile_list_stowage_bay_score_kernel(tc, tab_words, tab_scales, offs, w1_words
             larger(2 * k + 1)
             if k < 3:
                 products(k + 1)
-            if k > 0:
-                subtract_pair((k - 1) // 2, (k - 1) % 2)
+            if k in (1, 2):
+                subtract(2 * k - 1)
             if k == 2:
-                turn_back(0)
+                turn_back(0, range(NCH))
             scatter(2 * k)
+            if k == 1:
+                subtract(2)
             if k == 3:
-                subtract_single(1, 1)
-                turn_back(1)
+                subtract_rows(6)
+                for c in range(NCH):
+                    interleave(c)
             scatter(2 * k + 1)
+            if k == 2:
+                subtract_rows(4)
+                subtract_rows(5)
         for c in range(NCH):
-            score(0, c)
+            score(0, c, True)
         for c in range(NCH):
             cols = slice(c * CH, (c + 1) * CH)
             nc.vector.tensor_tensor(
-                z[(1, c)][:].rearrange("p (m i) -> p m i", i=4)[:, :, 3], lim_t[(1, 1)][:, 1, cols], pages[3][:, cols], ALU.add
+                z[(1, c)][:].rearrange("p (m i) -> p m i", i=4)[:, :, 3], lim_t[7][:, cols], pages[7 % 4][:, cols], ALU.add
             )
             quantize_z(1, c)
-            score(1, c)
+            score(1, c, False)
             for hf in range(2):
                 res = held([P, 2 * CH], F32, "res%d%d" % (c, hf))
                 nc.scalar.activation(res[:], y[(c, hf)][:], ACT.Square)

@@ -35,17 +35,17 @@ def tile_list_stowage_bay_score_kernel(tc, tab_words, tab_scales, offs, w1_words
             return keep.tile(shape, dtype, name=name, tag=tag or name, align_bytes=64)
 
         def load_scales(tile, src):
-            for q in range(4):
+            for r in range(4):
                 nc.sync.dma_start(
-                    out=tile[32 * q : 32 * q + 4, :].bitcast(I32).rearrange("r (a c) -> r a c", a=2),
-                    in_=src[:, 4 * q : 4 * q + 4, :].rearrange("a r c -> r a c").bitcast(I32),
+                    out=tile[r:P:32, :].bitcast(I32).rearrange("q (a c) -> q a c", a=2),
+                    in_=src[:, r:16:4, :].rearrange("a q c -> q a c").bitcast(I32),
                 )
 
         tab_s = held([P, 2 * T], U8, "tab_s")
         w1_s_raw = held([P, 2 * H], U8, "w1_s_raw")
         w3_s = held([P, 2 * N], U8, "w3_s")
         nc.vector.memset(tab_s[:].bitcast(I32), 0)
-        nc.gpsimd.memset(w1_s_raw[:].bitcast(I32), 0)
+        nc.vector.memset(w1_s_raw[:].bitcast(I32), 0)
         nc.vector.memset(w3_s[:].bitcast(I32), 0)
 
         warm = held([P, 8], F32, "warm")
@@ -55,7 +55,7 @@ def tile_list_stowage_bay_score_kernel(tc, tab_words, tab_scales, offs, w1_words
 
         ident = held([P, P], F32, "ident")
         make_identity(nc, ident[:])
-        pages = [held([P, T2], F32, "page%d" % i) for i in range(4)]
+        pages = [held([P, T2], F32, "page%d" % i) for i in range(6)]
         for page in pages:
             nc.gpsimd.memset(page[:], 0.0)
 
@@ -72,8 +72,8 @@ def tile_list_stowage_bay_score_kernel(tc, tab_words, tab_scales, offs, w1_words
 
         load_w1(0)
         tab_w = [held([P, T], I32, "tab_w%d" % a) for a in range(2)]
-        load_scales(tab_s, tab_scales)
         nc.sync.dma_start(out=tab_w[0][:], in_=tab_words[0].rearrange("p t i -> p (t i)").bitcast(I32))
+        load_scales(tab_s, tab_scales)
         nc.sync.dma_start(out=tab_w[1][:], in_=tab_words[1].rearrange("p t i -> p (t i)").bitcast(I32))
         load_scales(w1_s_raw, w1_scales)
 
@@ -108,11 +108,6 @@ def tile_list_stowage_bay_score_kernel(tc, tab_words, tab_scales, offs, w1_words
         load_w2(1, 1, 0, 512)
         for s in range(4):
             load_lim(s)
-        w3_w = held([P, 2 * N], I32, "w3_w")
-        nc.sync.dma_start(
-            out=w3_w[:].rearrange("p (b c) -> p b c", b=2),
-            in_=w3_words.rearrange("b p c i -> p b (c i)").bitcast(I32),
-        )
         load_scales(w3_s, w3_scales)
         for s in range(4, 8):
             load_lim(s)
@@ -144,15 +139,14 @@ def tile_list_stowage_bay_score_kernel(tc, tab_words, tab_scales, offs, w1_words
         order_w1_scales(0)
         order_w1_scales(1)
 
-        rounded = held([P, 8 * PASS], BF16, "rounded")
-        w2_g = {(0, a): rounded[:, 4 * PASS * a : 4 * PASS * (a + 1)] for a in range(2)}
+        w2_g = {}
         w2_w = {}
         w2_s = {}
 
         def cast_w2(b, a, c0, lo, hi, on_vector):
             if (b, a) not in w2_g:
                 w2_g[(b, a)] = held([P, 4 * PASS], BF16, "w2_g%d%d" % (b, a))
-            dst = w2_g[(b, a)][:, :].rearrange("p (t m j) -> p m j t", t=4, j=4)[:, lo // 4 : hi // 4]
+            dst = w2_g[(b, a)][:].rearrange("p (t m j) -> p m j t", t=4, j=4)[:, lo // 4 : hi // 4]
             src = w2_raw[(b, a, c0)][:, :, lo - c0 : hi - c0].rearrange("p j (m t) -> p m j t", t=4)
             if on_vector:
                 nc.vector.tensor_copy(out=dst, in_=src)
@@ -232,25 +226,30 @@ def tile_list_stowage_bay_score_kernel(tc, tab_words, tab_scales, offs, w1_words
             )
 
         def scatter(s):
-            nc.vector.tensor_tensor(pages[s % 4][:].indirect(idx2[:]), neg_h[s][:], wgt[:], ALU.mult)
+            nc.vector.tensor_tensor(pages[s % 6][:].indirect(idx2[:]), neg_h[s][:], wgt[:], ALU.mult)
 
         z_t = [held([P, 512], F32, "z_t%d" % c) for c in range(NCH)]
 
-        def subtract(s):
+        def turned_sum(bank, terms):
+            n = len(terms)
+            for k, (slot, src) in enumerate(terms):
+                nc.tensor.matmul(
+                    out=bank[:, slot * P : (slot + 1) * P], lhsT=src, rhs=ident[:],
+                    is_transpose=True, start=(k == 0), stop=(k == n - 1),
+                )
+
+        def subtract(s, chunks):
             u, e = divmod(s % 4, 2)
-            banks = [psum.tile([P, 512], F32, name="t1", tag="t1") for half in range(2)]
-            for term, src in enumerate((lim_t[s], pages[s % 4])):
-                for half in range(2):
-                    for mb in range(4):
-                        m0 = (4 * half + mb) * P
-                        nc.tensor.matmul(
-                            out=banks[half][:, mb * P : (mb + 1) * P], lhsT=src[:, m0 : m0 + P], rhs=ident[:],
-                            is_transpose=True, start=(term == 0 and mb == 0), stop=(term == 1 and mb == 3),
-                        )
-            for c in range(NCH):
+            bank = psum.tile([P, 512], F32, name="t1", tag="t1")
+            blocks = range(2 * len(chunks))
+            m0 = chunks[0] * CH
+            terms = [(mb, lim_t[s][:, m0 + mb * P : m0 + (mb + 1) * P]) for mb in blocks]
+            terms.extend([(mb, pages[s % 6][:, m0 + mb * P : m0 + (mb + 1) * P]) for mb in blocks])
+            turned_sum(bank, terms)
+            for cc, c in enumerate(chunks):
                 nc.scalar.copy(
                     out=z_t[c][:].bitcast(BF16).rearrange("m (mb u q e) -> m mb u q e", mb=2, u=2, e=2)[:, :, u, :, e],
-                    in_=banks[c // 2][:, (c % 2) * CH : (c % 2 + 1) * CH].rearrange("m (mb q) -> m mb q", mb=2),
+                    in_=bank[:, cc * CH : (cc + 1) * CH].rearrange("m (mb q) -> m mb q", mb=2),
                 )
 
         z = {}
@@ -270,16 +269,6 @@ def tile_list_stowage_bay_score_kernel(tc, tab_words, tab_scales, offs, w1_words
                     in_=bank[:].rearrange("p (u m) -> p m u", u=2),
                 )
 
-        def subtract_rows(s):
-            nc.vector.tensor_tensor(rounded[:, (s % 4) * T2 : (s % 4 + 1) * T2], lim_t[s][:], pages[s % 4][:], ALU.add)
-
-        def interleave(c):
-            z[(1, c)] = held([P, 4 * CH], BF16, "z1%d" % c)
-            nc.scalar.copy(
-                out=z[(1, c)][:].rearrange("p (g m i) -> p g i m", m=4, i=4),
-                in_=rounded[:].rearrange("p (i g m) -> p g i m", i=4, m=4)[:, c * CH // 4 : (c + 1) * CH // 4],
-            )
-
         def quantize_z(b, c):
             z_w[(b, c)] = held([P, CH], U32, "z_w%d%d" % (b, c))
             z_s[(b, c)] = held([P, CH], U8, "z_s%d%d" % (b, c))
@@ -290,7 +279,7 @@ def tile_list_stowage_bay_score_kernel(tc, tab_words, tab_scales, offs, w1_words
         def score(b, c, first):
             for hf in range(2):
                 if first:
-                    y[(c, hf)] = psum.tile([P, 512], F32, name="y", tag=("t1", "t2", "d1", "d2")[c])
+                    y[(c, hf)] = psum.tile([P, 512], F32, name="y", tag=(("d1", "d1"), ("d2", "d2"), ("t1", "t1"), ("t2", "t2"))[c][hf])
                 for nt in range(2):
                     col = b * N + (2 * hf + nt) * P
                     nc.tensor.matmul_mx(
@@ -310,7 +299,8 @@ def tile_list_stowage_bay_score_kernel(tc, tab_words, tab_scales, offs, w1_words
                     cast_w2(1, a, 0, 0, 256, False)
                     cast_w2(1, a, 0, 256, 512, False)
                     quantize_w2(1, a, 0, 4)
-                subtract(0)
+                subtract(0, (0, 1))
+                subtract(0, (2, 3))
             if k == 3:
                 for c in range(NCH):
                     quantize_z(0, c)
@@ -318,27 +308,29 @@ def tile_list_stowage_bay_score_kernel(tc, tab_words, tab_scales, offs, w1_words
             larger(2 * k + 1)
             if k < 3:
                 products(k + 1)
-            if k in (1, 2):
-                subtract(2 * k - 1)
+            if k > 0:
+                subtract(2 * k - 1, (0, 1))
+                subtract(2 * k - 1, (2, 3))
             if k == 2:
                 turn_back(0, range(NCH))
             scatter(2 * k)
-            if k == 1:
-                subtract(2)
+            if k > 0:
+                subtract(2 * k, (0, 1))
+                subtract(2 * k, (2, 3))
             if k == 3:
-                subtract_rows(6)
-                for c in range(NCH):
-                    interleave(c)
+                turn_back(1, range(NCH))
             scatter(2 * k + 1)
-            if k == 2:
-                subtract_rows(4)
-                subtract_rows(5)
+        w3_w = held([P, 2 * N], I32, "w3_w", tag="lim5")
+        nc.sync.dma_start(
+            out=w3_w[:].rearrange("p (b c) -> p b c", b=2),
+            in_=w3_words.rearrange("b p c i -> p b (c i)").bitcast(I32),
+        )
         for c in range(NCH):
             score(0, c, True)
         for c in range(NCH):
             cols = slice(c * CH, (c + 1) * CH)
             nc.vector.tensor_tensor(
-                z[(1, c)][:].rearrange("p (m i) -> p m i", i=4)[:, :, 3], lim_t[7][:, cols], pages[7 % 4][:, cols], ALU.add
+                z[(1, c)][:].rearrange("p (m i) -> p m i", i=4)[:, :, 3], lim_t[7][:, cols], pages[7 % 6][:, cols], ALU.add
             )
             quantize_z(1, c)
             score(1, c, False)

@@ -48,16 +48,16 @@ def tile_list_stowage_bay_score_kernel(tc, tab_words, tab_scales, offs, w1_words
         nc.vector.memset(w1_s_raw[:].bitcast(I32), 0)
         nc.vector.memset(w3_s[:].bitcast(I32), 0)
 
-        warm = held([P, 8], F32, "warm")
-        warm2 = held([P, 8], F32, "warm2")
-        nc.vector.memset(warm[:], 0.0)
-        nc.scalar.activation(warm2[:], warm[:], ACT.Square)
-
         ident = held([P, P], F32, "ident")
         make_identity(nc, ident[:])
-        pages = [held([P, T2], F32, "page%d" % i) for i in range(6)]
-        for page in pages:
-            nc.gpsimd.memset(page[:], 0.0)
+        pages = {}
+
+        def clear_page(i, engine, tag=None):
+            pages[i] = held([P, T2], F32, "page%d" % i, tag=tag)
+            engine.memset(pages[i][:], 0.0)
+
+        for i in range(2):
+            clear_page(i, nc.vector)
 
         idx = lists.tile([P, S // 16], U16, name="idx")
         idx2 = lists.tile([P, S // 16], U16, name="idx2")
@@ -151,7 +151,7 @@ def tile_list_stowage_bay_score_kernel(tc, tab_words, tab_scales, offs, w1_words
             if on_vector:
                 nc.vector.tensor_copy(out=dst, in_=src)
             else:
-                nc.scalar.copy(out=dst, in_=src)
+                nc.scalar.activation(dst, src, ACT.Copy)
 
         def quantize_w2(b, a, t0, t1):
             if (b, a) not in w2_w:
@@ -313,6 +313,12 @@ def tile_list_stowage_bay_score_kernel(tc, tab_words, tab_scales, offs, w1_words
                 subtract(2 * k - 1, (2, 3))
             if k == 2:
                 turn_back(0, range(NCH))
+            if k == 0:
+                clear_page(2, nc.gpsimd, "w2_raw01_0")
+                clear_page(3, nc.gpsimd, "w2_raw01_256")
+            if k == 2:
+                clear_page(4, nc.gpsimd, "w2_g11")
+                clear_page(5, nc.gpsimd, "w2_g10")
             scatter(2 * k)
             if k > 0:
                 subtract(2 * k, (0, 1))

@@ -28,11 +28,13 @@ def tile_list_stowage_bay_score_kernel(tc, tab_words, tab_scales, offs, w1_words
     with ExitStack() as ctx:
         lists = ctx.enter_context(tc.tile_pool(name="lists", bufs=1))
         keep = ctx.enter_context(tc.tile_pool(name="keep", bufs=1))
-        ring = ctx.enter_context(tc.tile_pool(name="ring", bufs=2))
-        psum = ctx.enter_context(tc.psum_pool(name="psum", bufs=2))
+        psum = ctx.enter_context(tc.psum_pool(name="psum", bufs=1))
 
         def held(shape, dtype, name, tag=None):
             return keep.tile(shape, dtype, name=name, tag=tag or name, align_bytes=64)
+
+        def bank(tag):
+            return psum.tile([P, 512], F32, name="bank", tag=tag)
 
         def load_scales(tile, src):
             for r in range(4):
@@ -44,37 +46,31 @@ def tile_list_stowage_bay_score_kernel(tc, tab_words, tab_scales, offs, w1_words
         tab_s = held([P, 2 * T], U8, "tab_s")
         w1_s_raw = held([P, 2 * H], U8, "w1_s_raw")
         w3_s = held([P, 2 * N], U8, "w3_s")
-        nc.vector.memset(tab_s[:].bitcast(I32), 0)
+        nc.gpsimd.memset(tab_s[:].bitcast(I32), 0)
         nc.vector.memset(w1_s_raw[:].bitcast(I32), 0)
-        nc.vector.memset(w3_s[:].bitcast(I32), 0)
-
-        ident = held([P, P], F32, "ident")
-        make_identity(nc, ident[:])
+        nc.gpsimd.memset(w3_s[:].bitcast(I32), 0)
         pages = {}
 
         def clear_page(i, engine, tag=None):
             pages[i] = held([P, T2], F32, "page%d" % i, tag=tag)
-            engine.memset(pages[i][:], 0.0)
+            engine.memset(pages[i][:].bitcast(I32), 0)
 
         for i in range(2):
-            clear_page(i, nc.vector)
+            clear_page(i, nc.gpsimd)
+        ident = held([P, P], F32, "ident")
+        make_identity(nc, ident[:])
 
         idx = lists.tile([P, S // 16], U16, name="idx")
         idx2 = lists.tile([P, S // 16], U16, name="idx2")
         nc.sync.dma_start(idx[:], offs)
-        w1_w_raw = [held([P, H // 2], I32, "w1_w_raw%d" % b) for b in range(2)]
-
-        def load_w1(b):
-            nc.sync.dma_start(
-                out=w1_w_raw[b][:].rearrange("p (a c) -> p a c", a=2),
-                in_=w1_words[:, :, H * b : H * (b + 1)].rearrange("a p c -> p a c").bitcast(I32),
-            )
-
-        load_w1(0)
+        w1_w_raw = held([P, H], I32, "w1_w_raw")
+        nc.sync.dma_start(
+            out=w1_w_raw[:].rearrange("p (a c) -> p a c", a=2), in_=w1_words.rearrange("a p c -> p a c").bitcast(I32)
+        )
         tab_w = [held([P, T], I32, "tab_w%d" % a) for a in range(2)]
-        nc.sync.dma_start(out=tab_w[0][:], in_=tab_words[0].rearrange("p t i -> p (t i)").bitcast(I32))
         load_scales(tab_s, tab_scales)
-        nc.sync.dma_start(out=tab_w[1][:], in_=tab_words[1].rearrange("p t i -> p (t i)").bitcast(I32))
+        for a in range(2):
+            nc.sync.dma_start(out=tab_w[a][:], in_=tab_words[a].rearrange("p t i -> p (t i)").bitcast(I32))
         load_scales(w1_s_raw, w1_scales)
 
         w2_raw = {}
@@ -89,12 +85,12 @@ def tile_list_stowage_bay_score_kernel(tc, tab_words, tab_scales, offs, w1_words
 
         lim_t = {}
 
-        def load_lim(s):
-            b, i = divmod(s, 4)
-            lim_t[s] = held([P, T2], F32, "lim%d" % s)
+        def load_lim(k):
+            b, u = divmod(k, 2)
+            lim_t[k] = held([P, 2, T2], F32, "lim%d" % k)
             nc.sync.dma_start(
-                out=lim_t[s][:],
-                in_=lim[PASS * b : PASS * (b + 1), :].rearrange("(p i) m -> p i m", i=4)[:, i, :],
+                out=lim_t[k][:],
+                in_=lim[PASS * b : PASS * (b + 1), :].rearrange("(p i) m -> p i m", i=4)[:, 2 * u : 2 * u + 2, :],
             )
 
         load_w2(0, 0, 0, 512)
@@ -103,31 +99,25 @@ def tile_list_stowage_bay_score_kernel(tc, tab_words, tab_scales, offs, w1_words
         nc.sync.dma_start(idx2[:], offs2)
         wgt = held([P, S], F32, "wgt")
         nc.sync.dma_start(out=wgt[:], in_=wgs)
-        load_w1(1)
         load_w2(1, 0, 0, 512)
         load_w2(1, 1, 0, 512)
-        for s in range(4):
-            load_lim(s)
+        load_lim(0)
+        load_lim(1)
         load_scales(w3_s, w3_scales)
-        for s in range(4, 8):
-            load_lim(s)
+        load_lim(2)
+        load_lim(3)
+        w3_w = held([P, 2 * N], I32, "w3_w")
+        nc.sync.dma_start(
+            out=w3_w[:].rearrange("p (b c) -> p b c", b=2),
+            in_=w3_words.rearrange("b p c i -> p b (c i)").bitcast(I32),
+        )
 
-        w1_w = [held([P, 2 * H], U8, "w1_w%d" % b) for b in range(2)]
+        w1_w = held([P, 4 * H], U8, "w1_w")
         w1_s = [held([P, H], U8, "w1_s%d" % b) for b in range(2)]
-
-        def order_w1_words(b):
-            nc.vector.tensor_copy(
-                out=w1_w[b][:].bitcast(U16).rearrange("p (a t m) -> p a m t", a=2, t=4),
-                in_=w1_w_raw[b][:].bitcast(U16).rearrange("p (a m t) -> p a m t", a=2, t=4),
-            )
-
-        def order_w1_scales(b):
-            nc.vector.tensor_copy(
-                out=w1_s[b][:].rearrange("p (a t m) -> p a m t", a=2, t=4),
-                in_=w1_s_raw[:].rearrange("p (a b m t) -> p b a m t", a=2, b=2, t=4)[:, b],
-            )
-
-        order_w1_words(0)
+        nc.vector.tensor_copy(
+            out=w1_w[:].bitcast(U16).rearrange("p (g t m) -> p g m t", g=4, t=4),
+            in_=w1_w_raw[:].bitcast(U16).rearrange("p (g m t) -> p g m t", g=4, t=4),
+        )
 
         v_w = [held([P, S], U32, "v_w%d" % a) for a in range(2)]
         v_s = [held([P, S], U8, "v_s%d" % a) for a in range(2)]
@@ -136,214 +126,261 @@ def tile_list_stowage_bay_score_kernel(tc, tab_words, tab_scales, offs, w1_words
         for a in range(2):
             nc.vector.tensor_copy(v_w[a][:], tab_w[a][:].bitcast(U32).indirect(idx[:]))
 
+        def order_w1_scales(b):
+            nc.vector.tensor_copy(
+                out=w1_s[b][:].rearrange("p (a t m) -> p a m t", a=2, t=4),
+                in_=w1_s_raw[:].rearrange("p (a b m t) -> p b a m t", a=2, b=2, t=4)[:, b],
+            )
+
         order_w1_scales(0)
-        order_w1_scales(1)
 
-        w2_g = {}
-        w2_w = {}
-        w2_s = {}
+        neg_d1 = {}
 
-        def cast_w2(b, a, c0, lo, hi, on_vector):
-            if (b, a) not in w2_g:
-                w2_g[(b, a)] = held([P, 4 * PASS], BF16, "w2_g%d%d" % (b, a))
-            dst = w2_g[(b, a)][:].rearrange("p (t m j) -> p m j t", t=4, j=4)[:, lo // 4 : hi // 4]
-            src = w2_raw[(b, a, c0)][:, :, lo - c0 : hi - c0].rearrange("p j (m t) -> p m j t", t=4)
-            if on_vector:
+        def first_product(s):
+            b, i = divmod(s, 4)
+            d1 = bank("AB"[s % 2])
+            for a in range(2):
+                col = a * H + b * PASS + i * P
+                nc.tensor.matmul_mx(
+                    out=d1[:],
+                    lhsT=w1_w[:, 2 * col : 2 * (col + P)].bitcast(FP4X4),
+                    lhsT_scale=w1_s[b][:, a * PASS + i * P : a * PASS + (i + 1) * P],
+                    rhs=v_w[a][:].bitcast(FP8X4),
+                    rhs_scale=v_s[a][:],
+                    start=(a == 0),
+                    stop=(a == 1),
+                )
+            neg_d1[s] = held([P, S], F32, "neg_d1_%d" % s)
+            nc.scalar.activation(neg_d1[s][:], d1[:], ACT.Copy, scale=-1.0)
+
+        q1_w = held([P, 2 * PASS], U32, "q1_w")
+        q1_s = held([P, 2 * PASS], U8, "q1_s")
+        g0 = {(a, u): held([P, 2 * PASS], BF16, "w2_g0%d%d" % (a, u)) for a in range(2) for u in range(2)}
+        g1 = held([P, 8 * PASS], BF16, "w2_g1")
+
+        def cast_first(a, c0, c1, u):
+            dst = g0[(a, u)][:].rearrange("p (t m j) -> p m j t", t=2, j=4)[:, c0 // 4 : c1 // 4]
+            src = w2_raw[(0, a, c0)][:].rearrange("p j (m t) -> p m j t", t=4)[:, :, :, 2 * u : 2 * u + 2]
+            if (a, u) == (1, 0):
                 nc.vector.tensor_copy(out=dst, in_=src)
             else:
                 nc.scalar.activation(dst, src, ACT.Copy)
 
-        def quantize_w2(b, a, t0, t1):
-            if (b, a) not in w2_w:
-                w2_w[(b, a)] = held([P, PASS], U32, "w2_w%d%d" % (b, a))
-                w2_s[(b, a)] = held([P, PASS], U8, "w2_s%d%d" % (b, a))
-            nc.vector.quantize_mx(
-                out=w2_w[(b, a)][:, P * t0 : P * t1].bitcast(FP8X4),
-                scales=w2_s[(b, a)][:, P * t0 : P * t1],
-                in_=w2_g[(b, a)][:, 4 * P * t0 : 4 * P * t1],
-            )
+        q0 = {}
 
-        cast_w2(0, 0, 0, 0, 512, True)
-        cast_w2(0, 1, 0, 0, 256, False)
-        quantize_w2(0, 0, 0, 2)
-        cast_w2(0, 1, 256, 256, 512, True)
-        quantize_w2(0, 0, 2, 4)
-        quantize_w2(0, 1, 0, 2)
-        quantize_w2(0, 1, 2, 4)
-        order_w1_words(1)
+        def quantize_first(a, u, tag=None):
+            words = held([P, 2 * P], U32, "q0_w%d%d" % (a, u), tag=tag)
+            scales = held([P, 2 * P], U8, "q0_s%d%d" % (a, u))
+            q0[(a, u)] = (words, scales)
+            nc.vector.quantize_mx(out=words[:].bitcast(FP8X4), scales=scales[:], in_=g0[(a, u)][:])
 
-        neg_h = {}
+        cast_first(0, 0, 512, 0)
+        first_product(0)
+        first_product(1)
+        quantize_first(0, 0)
+        for c0 in (0, 256):
+            cast_first(1, c0, c0 + 256, 0)
+        quantize_first(1, 0)
+        order_w1_scales(1)
+        cast_first(0, 0, 512, 1)
+        for c0 in (0, 256):
+            cast_first(1, c0, c0 + 256, 1)
 
         d2 = {}
-        neg_d1 = {}
 
-        def products(k):
+        def second_products(k):
             pair = (2 * k, 2 * k + 1)
             for s in pair:
-                b, i = divmod(s, 4)
-                d1 = psum.tile([P, S], F32, name="d1", tag="d1")
-                for a in range(2):
-                    col = a * PASS + i * P
-                    nc.tensor.matmul_mx(
-                        out=d1[:],
-                        lhsT=w1_w[b][:, 2 * col : 2 * (col + P)].bitcast(FP4X4),
-                        lhsT_scale=w1_s[b][:, col : col + P],
-                        rhs=v_w[a][:].bitcast(FP8X4),
-                        rhs_scale=v_s[a][:],
-                        start=(a == 0),
-                        stop=(a == 1),
-                    )
-                if s < 2:
-                    neg_d1[s] = held([P, S], F32, "neg_d1_%d" % s, tag="w2_raw01_%d" % (256 * s))
-                else:
-                    neg_d1[s] = ring.tile([P, S], F32, name="neg_d1")
-                nc.scalar.activation(neg_d1[s][:], d1[:], ACT.Copy, scale=-1.0)
-                d2[s] = psum.tile([P, S], F32, name="d2", tag="d2")
+                d2[s] = bank("EF"[s % 2])
             for a in range(2):
                 for s in pair:
                     b, i = divmod(s, 4)
+                    if b == 0:
+                        words, scales = q0[(a, i // 2)]
+                        col = (i % 2) * P
+                    else:
+                        words, scales = q1_w, q1_s
+                        col = a * PASS + i * P
                     nc.tensor.matmul_mx(
                         out=d2[s][:],
-                        lhsT=w2_w[(b, a)][:, i * P : (i + 1) * P].bitcast(FP8X4),
-                        lhsT_scale=w2_s[(b, a)][:, i * P : (i + 1) * P],
+                        lhsT=words[:, col : col + P].bitcast(FP8X4),
+                        lhsT_scale=scales[:, col : col + P],
                         rhs=v_w[a][:].bitcast(FP8X4),
                         rhs_scale=v_s[a][:],
                         start=(a == 0),
                         stop=(a == 1),
                     )
 
-        def larger(s):
-            if s == 2:
-                neg_h[s] = held([P, S], F32, "neg_h2", tag="w2_g11")
-            elif s == 3:
-                neg_h[s] = held([P, S], F32, "neg_h3", tag="w2_g10")
-            elif s == 7:
-                neg_h[s] = held([P, S], F32, "neg_h7", tag="z03")
-            else:
-                neg_h[s] = ring.tile([P, S], F32, name="neg_h")
-            nc.vector.scalar_tensor_tensor(
-                out=neg_h[s][:], in0=d2[s][:], scalar=-1.0, in1=neg_d1[s][:], op0=ALU.mult, op1=ALU.min
-            )
+        neg_h = {}
+
+        def larger(k, tag=None):
+            both = held([P, 2, S], F32, "neg_h%d" % k, tag=tag)
+            for e in range(2):
+                s = 2 * k + e
+                neg_h[s] = both[:, e, :]
+                nc.vector.scalar_tensor_tensor(
+                    out=neg_h[s], in0=d2[s][:], scalar=-1.0, in1=neg_d1[s][:], op0=ALU.mult, op1=ALU.min
+                )
 
         def scatter(s):
-            nc.vector.tensor_tensor(pages[s % 6][:].indirect(idx2[:]), neg_h[s][:], wgt[:], ALU.mult)
+            nc.vector.tensor_tensor(pages[s % 6][:].indirect(idx2[:]), neg_h[s], wgt[:], ALU.mult)
 
         z_t = [held([P, 512], F32, "z_t%d" % c) for c in range(NCH)]
 
-        def turned_sum(bank, terms):
-            n = len(terms)
-            for k, (slot, src) in enumerate(terms):
-                nc.tensor.matmul(
-                    out=bank[:, slot * P : (slot + 1) * P], lhsT=src, rhs=ident[:],
-                    is_transpose=True, start=(k == 0), stop=(k == n - 1),
-                )
+        def turn(acc, slot, src, start, stop):
+            nc.tensor.matmul(
+                out=acc[:, slot * P : (slot + 1) * P], lhsT=src, rhs=ident[:], is_transpose=True, start=start, stop=stop
+            )
 
-        def subtract(s, chunks):
-            u, e = divmod(s % 4, 2)
-            bank = psum.tile([P, 512], F32, name="t1", tag="t1")
-            blocks = range(2 * len(chunks))
-            m0 = chunks[0] * CH
-            terms = [(mb, lim_t[s][:, m0 + mb * P : m0 + (mb + 1) * P]) for mb in blocks]
-            terms.extend([(mb, pages[s % 6][:, m0 + mb * P : m0 + (mb + 1) * P]) for mb in blocks])
-            turned_sum(bank, terms)
-            for cc, c in enumerate(chunks):
-                nc.scalar.copy(
-                    out=z_t[c][:].bitcast(BF16).rearrange("m (mb u q e) -> m mb u q e", mb=2, u=2, e=2)[:, :, u, :, e],
-                    in_=bank[:, cc * CH : (cc + 1) * CH].rearrange("m (mb q) -> m mb q", mb=2),
-                )
-
-        z = {}
-        z_w = {}
-        z_s = {}
-
-        def turn_back(b, chunks):
-            for c in chunks:
-                bank = psum.tile([P, 512], F32, name="t2", tag="t2")
-                for u in range(2):
+        def subtract_pair(k, tags):
+            u = k % 2
+            acc = [bank(t) for t in tags]
+            for c in range(NCH):
+                for mb in range(2):
+                    for e in range(2):
+                        m0 = c * CH + mb * P
+                        turn(acc[c], 2 * mb + e, lim_t[k][:, e, m0 : m0 + P], mb == 0 and e == 0, False)
+            for e in range(2):
+                for c in range(NCH):
                     for mb in range(2):
-                        w0 = (2 * mb + u) * P
-                        nc.tensor.transpose(bank[:, u * CH + mb * P : u * CH + (mb + 1) * P], z_t[c][:, w0 : w0 + P], ident[:])
-                z[(b, c)] = held([P, 4 * CH], BF16, "z%d%d" % (b, c))
+                        m0 = c * CH + mb * P
+                        turn(acc[c], 2 * mb + e, pages[(2 * k + e) % 6][:, m0 : m0 + P], False, mb == 1 and e == 1)
+            for c in range(NCH):
                 nc.scalar.copy(
-                    out=z[(b, c)][:].bitcast(F32).rearrange("p (m u) -> p m u", u=2),
-                    in_=bank[:].rearrange("p (u m) -> p m u", u=2),
+                    out=z_t[c][:].bitcast(BF16).rearrange("m (mb u q e) -> m mb u q e", mb=2, u=2, e=2)[:, :, u],
+                    in_=acc[c][:].rearrange("m (mb e q) -> m mb q e", mb=2, e=2),
                 )
 
-        def quantize_z(b, c):
-            z_w[(b, c)] = held([P, CH], U32, "z_w%d%d" % (b, c))
-            z_s[(b, c)] = held([P, CH], U8, "z_s%d%d" % (b, c))
-            nc.vector.quantize_mx(out=z_w[(b, c)][:].bitcast(FP8X4), scales=z_s[(b, c)][:], in_=z[(b, c)][:])
+        def turn_back(acc, c, u):
+            for mb in range(2):
+                w0 = (2 * mb + u) * P
+                nc.tensor.transpose(acc[:, u * CH + mb * P : u * CH + (mb + 1) * P], z_t[c][:, w0 : w0 + P], ident[:])
+
+        def empty_turned(acc, dst):
+            nc.scalar.copy(
+                out=dst.bitcast(F32).rearrange("p (m u) -> p m u", u=2), in_=acc[:].rearrange("p (u m) -> p m u", u=2)
+            )
 
         y = {}
 
-        def score(b, c, first):
+        def score(b, c, codes, scales, tags=None):
+            first = b == 0
             for hf in range(2):
                 if first:
-                    y[(c, hf)] = psum.tile([P, 512], F32, name="y", tag=(("d1", "d1"), ("d2", "d2"), ("t1", "t1"), ("t2", "t2"))[c][hf])
+                    y[(c, hf)] = bank(tags[hf])
                 for nt in range(2):
                     col = b * N + (2 * hf + nt) * P
                     nc.tensor.matmul_mx(
                         out=y[(c, hf)][:, nt * CH : (nt + 1) * CH],
                         lhsT=w3_w[:, col : col + P].bitcast(FP8X4),
                         lhsT_scale=w3_s[:, col : col + P],
-                        rhs=z_w[(b, c)][:].bitcast(FP8X4),
-                        rhs_scale=z_s[(b, c)][:],
+                        rhs=codes.bitcast(FP8X4),
+                        rhs_scale=scales,
                         start=(first and nt == 0),
                         stop=(not first and nt == 1),
                     )
 
-        products(0)
-        for k in range(4):
-            if k == 1:
-                for a in range(2):
-                    cast_w2(1, a, 0, 0, 256, False)
-                    cast_w2(1, a, 0, 256, 512, False)
-                    quantize_w2(1, a, 0, 4)
-                subtract(0, (0, 1))
-                subtract(0, (2, 3))
-            if k == 3:
-                for c in range(NCH):
-                    quantize_z(0, c)
-            larger(2 * k)
-            larger(2 * k + 1)
-            if k < 3:
-                products(k + 1)
-            if k > 0:
-                subtract(2 * k - 1, (0, 1))
-                subtract(2 * k - 1, (2, 3))
-            if k == 2:
-                turn_back(0, range(NCH))
-            if k == 0:
-                clear_page(2, nc.gpsimd, "w2_raw01_0")
-                clear_page(3, nc.gpsimd, "w2_raw01_256")
-            if k == 2:
-                clear_page(4, nc.gpsimd, "w2_g11")
-                clear_page(5, nc.gpsimd, "w2_g10")
-            scatter(2 * k)
-            if k > 0:
-                subtract(2 * k, (0, 1))
-                subtract(2 * k, (2, 3))
-            if k == 3:
-                turn_back(1, range(NCH))
-            scatter(2 * k + 1)
-        w3_w = held([P, 2 * N], I32, "w3_w", tag="lim5")
-        nc.sync.dma_start(
-            out=w3_w[:].rearrange("p (b c) -> p b c", b=2),
-            in_=w3_words.rearrange("b p c i -> p b (c i)").bitcast(I32),
-        )
+        second_products(0)
+        quantize_first(0, 1)
+        larger(0)
+        quantize_first(1, 1, tag="neg_d1_1")
+        first_product(2)
+        first_product(3)
+        second_products(1)
+        clear_page(2, nc.gpsimd, "neg_d1_0")
+        clear_page(4, nc.gpsimd, "w2_g011")
+        scatter(0)
+        scatter(1)
+        for a in range(2):
+            for c0 in (0, 256):
+                nc.scalar.activation(
+                    g1[:].rearrange("p (a t m j) -> p a m j t", a=2, t=4, j=4)[:, a, c0 // 4 : c0 // 4 + 64],
+                    w2_raw[(1, a, 0)][:, :, c0 : c0 + 256].rearrange("p j (m t) -> p m j t", t=4),
+                    ACT.Copy,
+                )
+        for s in range(4, 8):
+            first_product(s)
+        larger(1)
+        clear_page(5, nc.gpsimd, "neg_d1_2")
+        clear_page(3, nc.gpsimd, "w2_raw11_0")
+        nc.vector.quantize_mx(out=q1_w[:].bitcast(FP8X4), scales=q1_s[:], in_=g1[:])
+        second_products(2)
+        subtract_pair(0, "CDAB")
+        scatter(2)
+        scatter(3)
+        larger(2)
+        second_products(3)
+        subtract_pair(1, "CDAB")
+        z0 = [held([P, 8 * CH], BF16, "z0%d" % h) for h in range(2)]
         for c in range(NCH):
-            score(0, c, True)
+            acc = bank("GHCD"[c])
+            for u in range(2):
+                turn_back(acc, c, u)
+            empty_turned(acc, z0[c // 2][:, 4 * CH * (c % 2) : 4 * CH * (c % 2 + 1)])
+        scatter(4)
+        scatter(5)
+        subtract_pair(2, "GHCD")
+        z0_w = [held([P, 2 * CH], U32, "z0_w%d" % h) for h in range(2)]
+        z0_s = [held([P, 2 * CH], U8, "z0_s%d" % h) for h in range(2)]
+        for h in range(2):
+            nc.vector.quantize_mx(out=z0_w[h][:].bitcast(FP8X4), scales=z0_s[h][:], in_=z0[h][:])
+        larger(3, tag="z01")
+
+        def first_score(c, tags):
+            cols = slice(CH * (c % 2), CH * (c % 2 + 1))
+            score(0, c, z0_w[c // 2][:, cols], z0_s[c // 2][:, cols], tags)
+
+        scatter(6)
+        acc6 = [bank(t) for t in "GH"]
+        for h in range(2):
+            for mb in range(4):
+                m0 = 512 * h + mb * P
+                turn(acc6[h], mb, lim_t[3][:, 0, m0 : m0 + P], mb == 0, False)
+        first_score(0, "EF")
+        first_score(1, "AB")
+        back = {}
+        for c in range(2):
+            back[c] = bank("CD"[c])
+            turn_back(back[c], c, 0)
+        for h in range(2):
+            for mb in range(4):
+                m0 = 512 * h + mb * P
+                turn(acc6[h], mb, pages[0][:, m0 : m0 + P], False, mb == 3)
+        z1 = [held([P, 4 * CH], BF16, "z1%d" % c) for c in range(NCH)]
+
+        def round_six(c):
+            nc.scalar.copy(
+                out=z_t[c][:].bitcast(BF16).rearrange("m (mb u q e) -> m mb u q e", mb=2, u=2, e=2)[:, :, 1, :, 0],
+                in_=acc6[c // 2][:, (c % 2) * CH : (c % 2 + 1) * CH].rearrange("m (mb q) -> m mb q", mb=2),
+            )
+
+        round_six(0)
+        round_six(1)
+        for c in range(NCH):
+            if c >= 2:
+                back[c] = bank("GH"[c - 2])
+                turn_back(back[c], c, 0)
+            turn_back(back[c], c, 1)
+            empty_turned(back[c], z1[c][:])
+            if c == 0:
+                round_six(2)
+                round_six(3)
+        scatter(7)
         for c in range(NCH):
             cols = slice(c * CH, (c + 1) * CH)
             nc.vector.tensor_tensor(
-                z[(1, c)][:].rearrange("p (m i) -> p m i", i=4)[:, :, 3], lim_t[7][:, cols], pages[7 % 6][:, cols], ALU.add
+                z1[c][:].rearrange("p (m i) -> p m i", i=4)[:, :, 3], lim_t[3][:, 1, cols], pages[1][:, cols], ALU.add
             )
-            quantize_z(1, c)
-            score(1, c, False)
+            z1_w = held([P, CH], U32, "z1_w%d" % c)
+            z1_s = held([P, CH], U8, "z1_s%d" % c)
+            nc.vector.quantize_mx(out=z1_w[:].bitcast(FP8X4), scales=z1_s[:], in_=z1[c][:])
+            score(1, c, z1_w[:], z1_s[:])
+            if c < 2:
+                first_score(c + 2, ("CD", "GH")[c])
+            res = held([P, 2, 2 * CH], F32, "res%d" % c, tag="z_t3" if c == 0 else None)
             for hf in range(2):
-                res = held([P, 2 * CH], F32, "res%d%d" % (c, hf))
-                nc.scalar.activation(res[:], y[(c, hf)][:], ACT.Square)
+                nc.scalar.activation(res[:, hf, :], y[(c, hf)][:], ACT.Square)
                 nc.sync.dma_start(
                     out=out[2 * P * hf : 2 * P * (hf + 1), cols].rearrange("(n p) m -> p n m", p=P),
-                    in_=res[:].rearrange("p (n m) -> p n m", n=2),
+                    in_=res[:, hf, :].rearrange("p (n m) -> p n m", n=2),
                 )

@@ -223,7 +223,7 @@ def tile_list_stowage_bay_score_kernel(tc, tab_words, tab_scales, offs, w1_words
                 )
 
         def scatter(s):
-            nc.vector.tensor_tensor(pages[s % 6][:].indirect(idx2[:]), neg_h[s], wgt[:], ALU.mult)
+            nc.vector.tensor_tensor(pages[s % 4][:].indirect(idx2[:]), neg_h[s], wgt[:], ALU.mult)
 
         z_t = [held([P, 512], F32, "z_t%d" % c) for c in range(NCH)]
 
@@ -244,7 +244,7 @@ def tile_list_stowage_bay_score_kernel(tc, tab_words, tab_scales, offs, w1_words
                 for c in range(NCH):
                     for mb in range(2):
                         m0 = c * CH + mb * P
-                        turn(acc[c], 2 * mb + e, pages[(2 * k + e) % 6][:, m0 : m0 + P], False, mb == 1 and e == 1)
+                        turn(acc[c], 2 * mb + e, pages[(2 * k + e) % 4][:, m0 : m0 + P], False, mb == 1 and e == 1)
             for c in range(NCH):
                 nc.scalar.copy(
                     out=z_t[c][:].bitcast(BF16).rearrange("m (mb u q e) -> m mb u q e", mb=2, u=2, e=2)[:, :, u],
@@ -287,8 +287,7 @@ def tile_list_stowage_bay_score_kernel(tc, tab_words, tab_scales, offs, w1_words
         first_product(2)
         first_product(3)
         second_products(1)
-        clear_page(2, nc.gpsimd, "neg_d1_0")
-        clear_page(4, nc.gpsimd, "w2_g011")
+        clear_page(2, nc.gpsimd, "w2_g011")
         scatter(0)
         scatter(1)
         for a in range(2):
@@ -301,7 +300,6 @@ def tile_list_stowage_bay_score_kernel(tc, tab_words, tab_scales, offs, w1_words
         for s in range(4, 8):
             first_product(s)
         larger(1)
-        clear_page(5, nc.gpsimd, "neg_d1_2")
         clear_page(3, nc.gpsimd, "w2_raw11_0")
         nc.vector.quantize_mx(out=q1_w[:].bitcast(FP8X4), scales=q1_s[:], in_=g1[:])
         second_products(2)
@@ -336,16 +334,15 @@ def tile_list_stowage_bay_score_kernel(tc, tab_words, tab_scales, offs, w1_words
             for mb in range(4):
                 m0 = 512 * h + mb * P
                 turn(acc6[h], mb, lim_t[3][:, 0, m0 : m0 + P], mb == 0, False)
-        first_score(0, "EF")
-        first_score(1, "AB")
+        first_score(1, "EF")
         back = {}
-        for c in range(2):
-            back[c] = bank("CD"[c])
+        for c in range(NCH):
+            back[c] = bank("ABCD"[c])
             turn_back(back[c], c, 0)
         for h in range(2):
             for mb in range(4):
                 m0 = 512 * h + mb * P
-                turn(acc6[h], mb, pages[0][:, m0 : m0 + P], False, mb == 3)
+                turn(acc6[h], mb, pages[2][:, m0 : m0 + P], False, mb == 3)
         z1 = [held([P, 4 * CH], BF16, "z1%d" % c) for c in range(NCH)]
 
         def round_six(c):
@@ -357,26 +354,24 @@ def tile_list_stowage_bay_score_kernel(tc, tab_words, tab_scales, offs, w1_words
         round_six(0)
         round_six(1)
         for c in range(NCH):
-            if c >= 2:
-                back[c] = bank("GH"[c - 2])
-                turn_back(back[c], c, 0)
             turn_back(back[c], c, 1)
             empty_turned(back[c], z1[c][:])
             if c == 0:
                 round_six(2)
                 round_six(3)
         scatter(7)
+        first_score(0, "GH")
         for c in range(NCH):
             cols = slice(c * CH, (c + 1) * CH)
             nc.vector.tensor_tensor(
-                z1[c][:].rearrange("p (m i) -> p m i", i=4)[:, :, 3], lim_t[3][:, 1, cols], pages[1][:, cols], ALU.add
+                z1[c][:].rearrange("p (m i) -> p m i", i=4)[:, :, 3], lim_t[3][:, 1, cols], pages[3][:, cols], ALU.add
             )
             z1_w = held([P, CH], U32, "z1_w%d" % c)
             z1_s = held([P, CH], U8, "z1_s%d" % c)
             nc.vector.quantize_mx(out=z1_w[:].bitcast(FP8X4), scales=z1_s[:], in_=z1[c][:])
             score(1, c, z1_w[:], z1_s[:])
             if c < 2:
-                first_score(c + 2, ("CD", "GH")[c])
+                first_score(c + 2, ("AB", "CD")[c])
             res = held([P, 2, 2 * CH], F32, "res%d" % c, tag="z_t3" if c == 0 else None)
             for hf in range(2):
                 nc.scalar.activation(res[:, hf, :], y[(c, hf)][:], ACT.Square)

@@ -188,10 +188,10 @@ def tile_list_stowage_bay_score_kernel(tc, tab_words, tab_scales, offs, w1_words
 
         d2 = {}
 
-        def second_products(k):
+        def second_products(k, tags):
             pair = (2 * k, 2 * k + 1)
             for s in pair:
-                d2[s] = bank("EF"[s % 2])
+                d2[s] = bank(tags[s % 2])
             for a in range(2):
                 for s in pair:
                     b, i = divmod(s, 4)
@@ -280,13 +280,14 @@ def tile_list_stowage_bay_score_kernel(tc, tab_words, tab_scales, offs, w1_words
                         stop=(not first and nt == 1),
                     )
 
-        second_products(0)
+        second_products(0, "EF")
         quantize_first(0, 1)
         larger(0)
         quantize_first(1, 1, tag="neg_d1_1")
         first_product(2)
         first_product(3)
-        second_products(1)
+        second_products(1, "EF")
+        clear_page(3, nc.gpsimd, "neg_d1_0")
         clear_page(2, nc.gpsimd, "w2_g011")
         scatter(0)
         scatter(1)
@@ -299,25 +300,24 @@ def tile_list_stowage_bay_score_kernel(tc, tab_words, tab_scales, offs, w1_words
                 )
         for s in range(4, 8):
             first_product(s)
-        larger(1)
-        clear_page(3, nc.gpsimd, "w2_raw11_0")
         nc.vector.quantize_mx(out=q1_w[:].bitcast(FP8X4), scales=q1_s[:], in_=g1[:])
-        second_products(2)
+        larger(1, tag="w2_g1")
+        second_products(2, "EF")
         subtract_pair(0, "CDAB")
         scatter(2)
         scatter(3)
         larger(2)
-        second_products(3)
         subtract_pair(1, "CDAB")
+        second_products(3, "CD")
         z0 = [held([P, 8 * CH], BF16, "z0%d" % h) for h in range(2)]
         for c in range(NCH):
-            acc = bank("GHCD"[c])
+            acc = bank("GHEF"[c])
             for u in range(2):
                 turn_back(acc, c, u)
             empty_turned(acc, z0[c // 2][:, 4 * CH * (c % 2) : 4 * CH * (c % 2 + 1)])
         scatter(4)
         scatter(5)
-        subtract_pair(2, "GHCD")
+        subtract_pair(2, "GHEF")
         z0_w = [held([P, 2 * CH], U32, "z0_w%d" % h) for h in range(2)]
         z0_s = [held([P, 2 * CH], U8, "z0_s%d" % h) for h in range(2)]
         for h in range(2):

@@ -138,7 +138,7 @@ def tile_list_stowage_bay_score_kernel(tc, tab_words, tab_scales, offs, w1_words
 
         def first_product(s):
             b, i = divmod(s, 4)
-            d1 = bank("AB"[s % 2])
+            d1 = bank("GHGHGHAB"[s])
             for a in range(2):
                 col = a * H + b * PASS + i * P
                 nc.tensor.matmul_mx(
@@ -283,12 +283,12 @@ def tile_list_stowage_bay_score_kernel(tc, tab_words, tab_scales, offs, w1_words
         second_products(0, "EF")
         quantize_first(0, 1)
         larger(0)
-        quantize_first(1, 1, tag="neg_d1_1")
+        quantize_first(1, 1, tag="neg_d1_0")
         first_product(2)
         first_product(3)
         second_products(1, "EF")
-        clear_page(3, nc.gpsimd, "neg_d1_0")
         clear_page(2, nc.gpsimd, "w2_g011")
+        clear_page(3, nc.gpsimd, "q0_w01")
         scatter(0)
         scatter(1)
         for a in range(2):
@@ -329,26 +329,25 @@ def tile_list_stowage_bay_score_kernel(tc, tab_words, tab_scales, offs, w1_words
             score(0, c, z0_w[c // 2][:, cols], z0_s[c // 2][:, cols], tags)
 
         scatter(6)
-        acc6 = [bank(t) for t in "GH"]
-        for h in range(2):
-            for mb in range(4):
-                m0 = 512 * h + mb * P
-                turn(acc6[h], mb, lim_t[3][:, 0, m0 : m0 + P], mb == 0, False)
-        first_score(1, "EF")
+        acc6 = [bank(t) for t in "GHEF"]
+        for c in range(NCH):
+            for mb in range(2):
+                m0 = c * CH + mb * P
+                turn(acc6[c], mb, lim_t[3][:, 0, m0 : m0 + P], mb == 0, False)
         back = {}
         for c in range(NCH):
             back[c] = bank("ABCD"[c])
             turn_back(back[c], c, 0)
-        for h in range(2):
-            for mb in range(4):
-                m0 = 512 * h + mb * P
-                turn(acc6[h], mb, pages[2][:, m0 : m0 + P], False, mb == 3)
+        for c in range(NCH):
+            for mb in range(2):
+                m0 = c * CH + mb * P
+                turn(acc6[c], mb, pages[2][:, m0 : m0 + P], False, mb == 1)
         z1 = [held([P, 4 * CH], BF16, "z1%d" % c) for c in range(NCH)]
 
         def round_six(c):
             nc.scalar.copy(
                 out=z_t[c][:].bitcast(BF16).rearrange("m (mb u q e) -> m mb u q e", mb=2, u=2, e=2)[:, :, 1, :, 0],
-                in_=acc6[c // 2][:, (c % 2) * CH : (c % 2 + 1) * CH].rearrange("m (mb q) -> m mb q", mb=2),
+                in_=acc6[c][:, 0:CH].rearrange("m (mb q) -> m mb q", mb=2),
             )
 
         round_six(0)
@@ -361,6 +360,7 @@ def tile_list_stowage_bay_score_kernel(tc, tab_words, tab_scales, offs, w1_words
                 round_six(3)
         scatter(7)
         first_score(0, "GH")
+        first_score(1, "EF")
         for c in range(NCH):
             cols = slice(c * CH, (c + 1) * CH)
             nc.vector.tensor_tensor(

@@ -55,7 +55,7 @@ def tile_list_stowage_bay_score_kernel(tc, tab_words, tab_scales, offs, w1_words
             pages[i] = held([P, T2], F32, "page%d" % i, tag=tag)
             engine.memset(pages[i][:].bitcast(I32), 0)
 
-        for i in range(2):
+        for i in range(4):
             clear_page(i, nc.gpsimd)
         ident = held([P, P], F32, "ident")
         make_identity(nc, ident[:])
@@ -150,8 +150,10 @@ def tile_list_stowage_bay_score_kernel(tc, tab_words, tab_scales, offs, w1_words
                     start=(a == 0),
                     stop=(a == 1),
                 )
-            neg_d1[s] = held([P, S], F32, "neg_d1_%d" % s)
-            nc.scalar.activation(neg_d1[s][:], d1[:], ACT.Copy, scale=-1.0)
+            if s < 4:
+                own = held([P, S], F32, "neg_d1_%d" % s)
+                neg_d1[s] = own[:]
+            nc.scalar.activation(neg_d1[s], d1[:], ACT.Copy, scale=-1.0)
 
         q1_w = held([P, 2 * PASS], U32, "q1_w")
         q1_s = held([P, 2 * PASS], U8, "q1_s")
@@ -219,7 +221,7 @@ def tile_list_stowage_bay_score_kernel(tc, tab_words, tab_scales, offs, w1_words
                 s = 2 * k + e
                 neg_h[s] = both[:, e, :]
                 nc.vector.scalar_tensor_tensor(
-                    out=neg_h[s], in0=d2[s][:], scalar=-1.0, in1=neg_d1[s][:], op0=ALU.mult, op1=ALU.min
+                    out=neg_h[s], in0=d2[s][:], scalar=-1.0, in1=neg_d1[s], op0=ALU.mult, op1=ALU.min
                 )
 
         def scatter(s):
@@ -287,8 +289,6 @@ def tile_list_stowage_bay_score_kernel(tc, tab_words, tab_scales, offs, w1_words
         first_product(2)
         first_product(3)
         second_products(1, "EF")
-        clear_page(2, nc.gpsimd, "w2_g011")
-        clear_page(3, nc.gpsimd, "q0_w01")
         scatter(0)
         scatter(1)
         for a in range(2):
@@ -298,7 +298,9 @@ def tile_list_stowage_bay_score_kernel(tc, tab_words, tab_scales, offs, w1_words
                     w2_raw[(1, a, 0)][:, :, c0 : c0 + 256].rearrange("p j (m t) -> p m j t", t=4),
                     ACT.Copy,
                 )
+        late_d1 = held([P, 4, S], F32, "late_d1", tag="w2_raw11_0")
         for s in range(4, 8):
+            neg_d1[s] = late_d1[:, s - 4, :]
             first_product(s)
         nc.vector.quantize_mx(out=q1_w[:].bitcast(FP8X4), scales=q1_s[:], in_=g1[:])
         larger(1, tag="w2_g1")
@@ -363,13 +365,28 @@ def tile_list_stowage_bay_score_kernel(tc, tab_words, tab_scales, offs, w1_words
         first_score(1, "EF")
         for c in range(NCH):
             cols = slice(c * CH, (c + 1) * CH)
-            nc.vector.tensor_tensor(
-                z1[c][:].rearrange("p (m i) -> p m i", i=4)[:, :, 3], lim_t[3][:, 1, cols], pages[3][:, cols], ALU.add
-            )
-            z1_w = held([P, CH], U32, "z1_w%d" % c)
-            z1_s = held([P, CH], U8, "z1_s%d" % c)
-            nc.vector.quantize_mx(out=z1_w[:].bitcast(FP8X4), scales=z1_s[:], in_=z1[c][:])
-            score(1, c, z1_w[:], z1_s[:])
+            for h in range(2):
+                m0 = c * CH + h * P
+                nc.vector.tensor_tensor(
+                    z1[c][:].rearrange("p (m i) -> p m i", i=4)[:, h * P : (h + 1) * P, 3],
+                    lim_t[3][:, 1, m0 : m0 + P], pages[3][:, m0 : m0 + P], ALU.add,
+                )
+            for h in range(2):
+                z1_w = held([P, P], U32, "z1_w%d%d" % (c, h))
+                z1_s = held([P, P], U8, "z1_s%d%d" % (c, h))
+                nc.vector.quantize_mx(out=z1_w[:].bitcast(FP8X4), scales=z1_s[:], in_=z1[c][:, 4 * P * h : 4 * P * (h + 1)])
+                for hf in range(2):
+                    for nt in range(2):
+                        col = N + (2 * hf + nt) * P
+                        nc.tensor.matmul_mx(
+                            out=y[(c, hf)][:, nt * CH + h * P : nt * CH + (h + 1) * P],
+                            lhsT=w3_w[:, col : col + P].bitcast(FP8X4),
+                            lhsT_scale=w3_s[:, col : col + P],
+                            rhs=z1_w[:].bitcast(FP8X4),
+                            rhs_scale=z1_s[:],
+                            start=False,
+                            stop=(h == 1 and nt == 1),
+                        )
             if c < 2:
                 first_score(c + 2, ("AB", "CD")[c])
             res = held([P, 2, 2 * CH], F32, "res%d" % c, tag="z_t3" if c == 0 else None)

@@ -55,8 +55,8 @@ def tile_list_stowage_bay_score_kernel(tc, tab_words, tab_scales, offs, w1_words
             pages[i] = held([P, T2], F32, "page%d" % i, tag=tag)
             engine.memset(pages[i][:].bitcast(I32), 0)
 
-        for i in range(4):
-            clear_page(i, nc.gpsimd)
+        for i in range(2):
+            clear_page(i, nc.vector)
         ident = held([P, P], F32, "ident")
         make_identity(nc, ident[:])
 
@@ -289,6 +289,8 @@ def tile_list_stowage_bay_score_kernel(tc, tab_words, tab_scales, offs, w1_words
         first_product(2)
         first_product(3)
         second_products(1, "EF")
+        clear_page(2, nc.gpsimd, "w2_g011")
+        clear_page(3, nc.gpsimd, "q0_w01")
         scatter(0)
         scatter(1)
         for a in range(2):

@@ -63,14 +63,19 @@ def tile_list_stowage_bay_score_kernel(tc, tab_words, tab_scales, offs, w1_words
         idx = lists.tile([P, S // 16], U16, name="idx")
         idx2 = lists.tile([P, S // 16], U16, name="idx2")
         nc.sync.dma_start(idx[:], offs)
-        w1_w_raw = held([P, H], I32, "w1_w_raw")
-        nc.sync.dma_start(
-            out=w1_w_raw[:].rearrange("p (a c) -> p a c", a=2), in_=w1_words.rearrange("a p c -> p a c").bitcast(I32)
-        )
+        w1_w_raw = [held([P, H // 2], I32, "w1_w_raw%d" % b) for b in range(2)]
+
+        def load_w1(b):
+            nc.sync.dma_start(
+                out=w1_w_raw[b][:].rearrange("p (a c) -> p a c", a=2),
+                in_=w1_words[:, :, H * b : H * (b + 1)].rearrange("a p c -> p a c").bitcast(I32),
+            )
+
         tab_w = [held([P, T], I32, "tab_w%d" % a) for a in range(2)]
+        nc.sync.dma_start(out=tab_w[0][:], in_=tab_words[0].rearrange("p t i -> p (t i)").bitcast(I32))
         load_scales(tab_s, tab_scales)
-        for a in range(2):
-            nc.sync.dma_start(out=tab_w[a][:], in_=tab_words[a].rearrange("p t i -> p (t i)").bitcast(I32))
+        load_w1(0)
+        nc.sync.dma_start(out=tab_w[1][:], in_=tab_words[1].rearrange("p t i -> p (t i)").bitcast(I32))
         load_scales(w1_s_raw, w1_scales)
 
         w2_raw = {}
@@ -96,6 +101,7 @@ def tile_list_stowage_bay_score_kernel(tc, tab_words, tab_scales, offs, w1_words
         load_w2(0, 0, 0, 512)
         load_w2(0, 1, 0, 256)
         load_w2(0, 1, 256, 512)
+        load_w1(1)
         nc.sync.dma_start(idx2[:], offs2)
         wgt = held([P, S], F32, "wgt")
         nc.sync.dma_start(out=wgt[:], in_=wgs)
@@ -112,19 +118,24 @@ def tile_list_stowage_bay_score_kernel(tc, tab_words, tab_scales, offs, w1_words
             in_=w3_words.rearrange("b p c i -> p b (c i)").bitcast(I32),
         )
 
-        w1_w = held([P, 4 * H], U8, "w1_w")
+        w1_w = {}
         w1_s = [held([P, H], U8, "w1_s%d" % b) for b in range(2)]
-        nc.vector.tensor_copy(
-            out=w1_w[:].bitcast(U16).rearrange("p (g t m) -> p g m t", g=4, t=4),
-            in_=w1_w_raw[:].bitcast(U16).rearrange("p (g m t) -> p g m t", g=4, t=4),
-        )
+
+        def order_w1_words(b, tag=None):
+            w1_w[b] = held([P, 2 * H], U8, "w1_w%d" % b, tag=tag)
+            nc.vector.tensor_copy(
+                out=w1_w[b][:].bitcast(U16).rearrange("p (a t m) -> p a m t", a=2, t=4),
+                in_=w1_w_raw[b][:].bitcast(U16).rearrange("p (a m t) -> p a m t", a=2, t=4),
+            )
+
 
         v_w = [held([P, S], U32, "v_w%d" % a) for a in range(2)]
         v_s = [held([P, S], U8, "v_s%d" % a) for a in range(2)]
+        nc.vector.tensor_copy(v_w[0][:], tab_w[0][:].bitcast(U32).indirect(idx[:]))
         for a in range(2):
             nc.vector.tensor_copy(v_s[a][:], tab_s[:, a * T : (a + 1) * T].indirect(idx[:]))
-        for a in range(2):
-            nc.vector.tensor_copy(v_w[a][:], tab_w[a][:].bitcast(U32).indirect(idx[:]))
+        order_w1_words(0)
+        nc.vector.tensor_copy(v_w[1][:], tab_w[1][:].bitcast(U32).indirect(idx[:]))
 
         def order_w1_scales(b):
             nc.vector.tensor_copy(
@@ -140,11 +151,11 @@ def tile_list_stowage_bay_score_kernel(tc, tab_words, tab_scales, offs, w1_words
             b, i = divmod(s, 4)
             d1 = bank("GHGHGHAB"[s])
             for a in range(2):
-                col = a * H + b * PASS + i * P
+                col = a * PASS + i * P
                 nc.tensor.matmul_mx(
                     out=d1[:],
-                    lhsT=w1_w[:, 2 * col : 2 * (col + P)].bitcast(FP4X4),
-                    lhsT_scale=w1_s[b][:, a * PASS + i * P : a * PASS + (i + 1) * P],
+                    lhsT=w1_w[b][:, 2 * col : 2 * (col + P)].bitcast(FP4X4),
+                    lhsT_scale=w1_s[b][:, col : col + P],
                     rhs=v_w[a][:].bitcast(FP8X4),
                     rhs_scale=v_s[a][:],
                     start=(a == 0),
@@ -163,7 +174,7 @@ def tile_list_stowage_bay_score_kernel(tc, tab_words, tab_scales, offs, w1_words
         def cast_first(a, c0, c1, u):
             dst = g0[(a, u)][:].rearrange("p (t m j) -> p m j t", t=2, j=4)[:, c0 // 4 : c1 // 4]
             src = w2_raw[(0, a, c0)][:].rearrange("p j (m t) -> p m j t", t=4)[:, :, :, 2 * u : 2 * u + 2]
-            if (a, u) == (1, 0):
+            if a == 1 and (u == 0 or c0 == 0):
                 nc.vector.tensor_copy(out=dst, in_=src)
             else:
                 nc.scalar.activation(dst, src, ACT.Copy)
@@ -177,6 +188,7 @@ def tile_list_stowage_bay_score_kernel(tc, tab_words, tab_scales, offs, w1_words
             nc.vector.quantize_mx(out=words[:].bitcast(FP8X4), scales=scales[:], in_=g0[(a, u)][:])
 
         cast_first(0, 0, 512, 0)
+        cast_first(0, 0, 512, 1)
         first_product(0)
         first_product(1)
         quantize_first(0, 0)
@@ -184,7 +196,6 @@ def tile_list_stowage_bay_score_kernel(tc, tab_words, tab_scales, offs, w1_words
             cast_first(1, c0, c0 + 256, 0)
         quantize_first(1, 0)
         order_w1_scales(1)
-        cast_first(0, 0, 512, 1)
         for c0 in (0, 256):
             cast_first(1, c0, c0 + 256, 1)
 
@@ -284,6 +295,7 @@ def tile_list_stowage_bay_score_kernel(tc, tab_words, tab_scales, offs, w1_words
 
         second_products(0, "EF")
         quantize_first(0, 1)
+        order_w1_words(1, tag="w2_g010")
         larger(0)
         quantize_first(1, 1, tag="neg_d1_0")
         first_product(2)

@@ -161,9 +161,6 @@ def tile_list_stowage_bay_score_kernel(tc, tab_words, tab_scales, offs, w1_words
                     start=(a == 0),
                     stop=(a == 1),
                 )
-            if s < 4:
-                own = held([P, S], F32, "neg_d1_%d" % s)
-                neg_d1[s] = own[:]
             nc.scalar.activation(neg_d1[s], d1[:], ACT.Copy, scale=-1.0)
 
         q1_w = held([P, 2 * PASS], U32, "q1_w")
@@ -189,6 +186,9 @@ def tile_list_stowage_bay_score_kernel(tc, tab_words, tab_scales, offs, w1_words
 
         cast_first(0, 0, 512, 0)
         cast_first(0, 0, 512, 1)
+        early_d1 = held([P, 4, S], F32, "early_d1", tag="w2_raw00_0")
+        for s in range(4):
+            neg_d1[s] = early_d1[:, s, :]
         first_product(0)
         first_product(1)
         quantize_first(0, 0)
@@ -297,7 +297,7 @@ def tile_list_stowage_bay_score_kernel(tc, tab_words, tab_scales, offs, w1_words
         quantize_first(0, 1)
         order_w1_words(1, tag="w2_g010")
         larger(0)
-        quantize_first(1, 1, tag="neg_d1_0")
+        quantize_first(1, 1)
         first_product(2)
         first_product(3)
         second_products(1, "EF")

@@ -28,6 +28,7 @@ def tile_list_stowage_bay_score_kernel(tc, tab_words, tab_scales, offs, w1_words
     with ExitStack() as ctx:
         lists = ctx.enter_context(tc.tile_pool(name="lists", bufs=1))
         keep = ctx.enter_context(tc.tile_pool(name="keep", bufs=1))
+        shared = ctx.enter_context(tc.tile_pool(name="shared", bufs=1))
         psum = ctx.enter_context(tc.psum_pool(name="psum", bufs=1))
 
         def held(shape, dtype, name, tag=None):
@@ -105,9 +106,9 @@ def tile_list_stowage_bay_score_kernel(tc, tab_words, tab_scales, offs, w1_words
         nc.sync.dma_start(idx2[:], offs2)
         wgt = held([P, S], F32, "wgt")
         nc.sync.dma_start(out=wgt[:], in_=wgs)
+        load_lim(0)
         load_w2(1, 0, 0, 512)
         load_w2(1, 1, 0, 512)
-        load_lim(0)
         load_lim(1)
         load_scales(w3_s, w3_scales)
         load_lim(2)
@@ -149,7 +150,7 @@ def tile_list_stowage_bay_score_kernel(tc, tab_words, tab_scales, offs, w1_words
 
         def first_product(s):
             b, i = divmod(s, 4)
-            d1 = bank("GHGHGHAB"[s])
+            d1 = bank("GH"[s % 2])
             for a in range(2):
                 col = a * PASS + i * P
                 nc.tensor.matmul_mx(
@@ -163,10 +164,12 @@ def tile_list_stowage_bay_score_kernel(tc, tab_words, tab_scales, offs, w1_words
                 )
             nc.scalar.activation(neg_d1[s], d1[:], ACT.Copy, scale=-1.0)
 
-        q1_w = held([P, 2 * PASS], U32, "q1_w")
-        q1_s = held([P, 2 * PASS], U8, "q1_s")
+        q1_w = [held([P, PASS], U32, "q1_w%d" % u) for u in range(2)]
+        q1_s = [held([P, PASS], U8, "q1_s%d" % u) for u in range(2)]
         g0 = {(a, u): held([P, 2 * PASS], BF16, "w2_g0%d%d" % (a, u)) for a in range(2) for u in range(2)}
-        g1 = held([P, 8 * PASS], BF16, "w2_g1")
+        g1_span = shared.tile([P, 8 * PASS + 64], BF16, name="g1_span", offset=4096 - 64, align_bytes=64)
+        g1_late = held([P, 4 * PASS], BF16, "w2_g1")
+        g1 = [g1_span[:, 0 : 4 * PASS], g1_late[:]]
 
         def cast_first(a, c0, c1, u):
             dst = g0[(a, u)][:].rearrange("p (t m j) -> p m j t", t=2, j=4)[:, c0 // 4 : c1 // 4]
@@ -212,8 +215,8 @@ def tile_list_stowage_bay_score_kernel(tc, tab_words, tab_scales, offs, w1_words
                         words, scales = q0[(a, i // 2)]
                         col = (i % 2) * P
                     else:
-                        words, scales = q1_w, q1_s
-                        col = a * PASS + i * P
+                        words, scales = q1_w[i // 2], q1_s[i // 2]
+                        col = (2 * a + i % 2) * P
                     nc.tensor.matmul_mx(
                         out=d2[s][:],
                         lhsT=words[:, col : col + P].bitcast(FP8X4),
@@ -227,7 +230,10 @@ def tile_list_stowage_bay_score_kernel(tc, tab_words, tab_scales, offs, w1_words
         neg_h = {}
 
         def larger(k, tag=None):
-            both = held([P, 2, S], F32, "neg_h%d" % k, tag=tag)
+            if k == 1:
+                both = shared.tile([P, 2, S], F32, name="neg_h1", offset=0, align_bytes=64)
+            else:
+                both = held([P, 2, S], F32, "neg_h%d" % k, tag=tag)
             for e in range(2):
                 s = 2 * k + e
                 neg_h[s] = both[:, e, :]
@@ -238,7 +244,9 @@ def tile_list_stowage_bay_score_kernel(tc, tab_words, tab_scales, offs, w1_words
         def scatter(s):
             nc.vector.tensor_tensor(pages[s % 4][:].indirect(idx2[:]), neg_h[s], wgt[:], ALU.mult)
 
-        z_t = [held([P, 512], F32, "z_t%d" % c) for c in range(NCH)]
+        z_t = [
+            shared.tile([P, 512], F32, name="z_t%d" % c, offset=4096 + 2048 * c, align_bytes=64) for c in range(NCH)
+        ]
 
         def turn(acc, slot, src, start, stop):
             nc.tensor.matmul(
@@ -305,24 +313,35 @@ def tile_list_stowage_bay_score_kernel(tc, tab_words, tab_scales, offs, w1_words
         clear_page(3, nc.gpsimd, "q0_w01")
         scatter(0)
         scatter(1)
-        for a in range(2):
-            for c0 in (0, 256):
+
+        def cast_second(u):
+            for a in range(2):
                 nc.scalar.activation(
-                    g1[:].rearrange("p (a t m j) -> p a m j t", a=2, t=4, j=4)[:, a, c0 // 4 : c0 // 4 + 64],
-                    w2_raw[(1, a, 0)][:, :, c0 : c0 + 256].rearrange("p j (m t) -> p m j t", t=4),
+                    g1[u].rearrange("p (a t m j) -> p a m j t", a=2, t=2, j=4)[:, a],
+                    w2_raw[(1, a, 0)][:].rearrange("p j (m t) -> p m j t", t=4)[:, :, :, 2 * u : 2 * u + 2],
                     ACT.Copy,
                 )
-        late_d1 = held([P, 4, S], F32, "late_d1", tag="w2_raw11_0")
+
+        def quantize_second(u):
+            nc.vector.quantize_mx(out=q1_w[u][:].bitcast(FP8X4), scales=q1_s[u][:], in_=g1[u])
+
+        cast_second(0)
+        late_d1 = [
+            held([P, 2, S], F32, "late_d1"),
+            shared.tile([P, 2, S], F32, name="last_d1", offset=4096 + 2048 * 4, align_bytes=64),
+        ]
         for s in range(4, 8):
-            neg_d1[s] = late_d1[:, s - 4, :]
+            neg_d1[s] = late_d1[s // 6][:, s % 2, :]
             first_product(s)
-        nc.vector.quantize_mx(out=q1_w[:].bitcast(FP8X4), scales=q1_s[:], in_=g1[:])
-        larger(1, tag="w2_g1")
+        quantize_second(0)
+        larger(1)
         second_products(2, "EF")
         subtract_pair(0, "CDAB")
+        cast_second(1)
         scatter(2)
         scatter(3)
-        larger(2)
+        quantize_second(1)
+        larger(2, tag="w2_g1")
         subtract_pair(1, "CDAB")
         second_products(3, "CD")
         z0 = [held([P, 8 * CH], BF16, "z0%d" % h) for h in range(2)]
@@ -403,7 +422,10 @@ def tile_list_stowage_bay_score_kernel(tc, tab_words, tab_scales, offs, w1_words
                         )
             if c < 2:
                 first_score(c + 2, ("AB", "CD")[c])
-            res = held([P, 2, 2 * CH], F32, "res%d" % c, tag="z_t3" if c == 0 else None)
+            if c == 0:
+                res = shared.tile([P, 2, 2 * CH], F32, name="res0", offset=4096 + 2048 * 3, align_bytes=64)
+            else:
+                res = held([P, 2, 2 * CH], F32, "res%d" % c)
             for hf in range(2):
                 nc.scalar.activation(res[:, hf, :], y[(c, hf)][:], ACT.Square)
                 nc.sync.dma_start(

@@ -21,9 +21,12 @@ P = 128
 PASS = 512
 CH = 256
 NCH = T2 // CH
+UNIT = 2048
 
 
-def tile_list_stowage_bay_score_kernel(tc, tab_words, tab_scales, offs, w1_words, w1_scales, w2, offs2, wgs, lim, w3_words, w3_scales, out):
+def tile_list_stowage_bay_score_kernel(
+    tc, tab_words, tab_scales, offs, w1_words, w1_scales, w2, offs2, wgs, lim, w3_words, w3_scales, out
+):
     nc = tc.nc
     with ExitStack() as ctx:
         lists = ctx.enter_context(tc.tile_pool(name="lists", bufs=1))
@@ -34,8 +37,27 @@ def tile_list_stowage_bay_score_kernel(tc, tab_words, tab_scales, offs, w1_words
         def held(shape, dtype, name, tag=None):
             return keep.tile(shape, dtype, name=name, tag=tag or name, align_bytes=64)
 
-        def bank(tag):
-            return psum.tile([P, 512], F32, name="bank", tag=tag)
+        def placed(shape, dtype, name, offset):
+            return shared.tile(shape, dtype, name=name, offset=offset, align_bytes=64)
+
+        def bank(letter):
+            return psum.tile([P, 512], F32, name="bank", tag=letter)
+
+        tab_s = held([P, 2 * T], U8, "tab_s")
+        w1_s_raw = held([P, 2 * H], U8, "w1_s_raw")
+        w3_s = held([P, 2 * N], U8, "w3_s")
+        for scale_tile in (tab_s, w1_s_raw, w3_s):
+            nc.vector.memset(scale_tile[:].bitcast(I32), 0)
+
+        pages = {}
+
+        def clear_page(i, engine, tag=None):
+            pages[i] = held([P, T2], F32, "page%d" % i, tag=tag)
+            engine.memset(pages[i][:].bitcast(I32), 0)
+
+        clear_page(0, nc.vector)
+        ident = held([P, P], F32, "ident")
+        make_identity(nc, ident[:])
 
         def load_scales(tile, src):
             for r in range(4):
@@ -44,26 +66,11 @@ def tile_list_stowage_bay_score_kernel(tc, tab_words, tab_scales, offs, w1_words
                     in_=src[:, r:16:4, :].rearrange("a q c -> q a c").bitcast(I32),
                 )
 
-        tab_s = held([P, 2 * T], U8, "tab_s")
-        w1_s_raw = held([P, 2 * H], U8, "w1_s_raw")
-        w3_s = held([P, 2 * N], U8, "w3_s")
-        nc.gpsimd.memset(tab_s[:].bitcast(I32), 0)
-        nc.vector.memset(w1_s_raw[:].bitcast(I32), 0)
-        nc.gpsimd.memset(w3_s[:].bitcast(I32), 0)
-        pages = {}
+        tab_w = [held([P, T], I32, "tab_w%d" % a) for a in range(2)]
 
-        def clear_page(i, engine, tag=None):
-            pages[i] = held([P, T2], F32, "page%d" % i, tag=tag)
-            engine.memset(pages[i][:].bitcast(I32), 0)
+        def load_table(a):
+            nc.sync.dma_start(out=tab_w[a][:], in_=tab_words[a].rearrange("p t i -> p (t i)").bitcast(I32))
 
-        for i in range(2):
-            clear_page(i, nc.vector)
-        ident = held([P, P], F32, "ident")
-        make_identity(nc, ident[:])
-
-        idx = lists.tile([P, S // 16], U16, name="idx")
-        idx2 = lists.tile([P, S // 16], U16, name="idx2")
-        nc.sync.dma_start(idx[:], offs)
         w1_w_raw = [held([P, H // 2], I32, "w1_w_raw%d" % b) for b in range(2)]
 
         def load_w1(b):
@@ -72,22 +79,14 @@ def tile_list_stowage_bay_score_kernel(tc, tab_words, tab_scales, offs, w1_words
                 in_=w1_words[:, :, H * b : H * (b + 1)].rearrange("a p c -> p a c").bitcast(I32),
             )
 
-        tab_w = [held([P, T], I32, "tab_w%d" % a) for a in range(2)]
-        nc.sync.dma_start(out=tab_w[0][:], in_=tab_words[0].rearrange("p t i -> p (t i)").bitcast(I32))
-        load_scales(tab_s, tab_scales)
-        load_w1(0)
-        nc.sync.dma_start(out=tab_w[1][:], in_=tab_words[1].rearrange("p t i -> p (t i)").bitcast(I32))
-        load_scales(w1_s_raw, w1_scales)
+        def w2_block(b, a):
+            return w2[PASS * a : PASS * (a + 1), PASS * b : PASS * (b + 1)].rearrange("(p j) c -> p j c", j=4)
 
         w2_raw = {}
 
-        def load_w2(b, a, c0, c1):
-            raw = held([P, 4, c1 - c0], F32, "w2_raw%d%d_%d" % (b, a, c0))
-            nc.sync.dma_start(
-                out=raw[:],
-                in_=w2[PASS * a : PASS * (a + 1), PASS * b + c0 : PASS * b + c1].rearrange("(p j) c -> p j c", j=4),
-            )
-            w2_raw[(b, a, c0)] = raw
+        def load_w2(b, a):
+            w2_raw[(b, a)] = held([P, 4, PASS], F32, "w2_raw%d%d" % (b, a))
+            nc.sync.dma_start(out=w2_raw[(b, a)][:], in_=w2_block(b, a))
 
         lim_t = {}
 
@@ -99,16 +98,25 @@ def tile_list_stowage_bay_score_kernel(tc, tab_words, tab_scales, offs, w1_words
                 in_=lim[PASS * b : PASS * (b + 1), :].rearrange("(p i) m -> p i m", i=4)[:, 2 * u : 2 * u + 2, :],
             )
 
-        load_w2(0, 0, 0, 512)
-        load_w2(0, 1, 0, 256)
-        load_w2(0, 1, 256, 512)
+        idx = lists.tile([P, S // 16], U16, name="idx")
+        idx2 = lists.tile([P, S // 16], U16, name="idx2")
+        load_table(0)
+        nc.sync.dma_start(idx[:], offs)
+        load_scales(tab_s, tab_scales)
+        load_w1(0)
+        load_table(1)
+        load_scales(w1_s_raw, w1_scales)
+        load_w2(0, 0)
+        w2_rows = [held([P, 2, PASS], F32, "w2_rows%d" % v) for v in range(2)]
+        for v in range(2):
+            nc.sync.dma_start(out=w2_rows[v][:], in_=w2_block(0, 1)[:, 2 * v : 2 * v + 2, :])
         load_w1(1)
         nc.sync.dma_start(idx2[:], offs2)
         wgt = held([P, S], F32, "wgt")
         nc.sync.dma_start(out=wgt[:], in_=wgs)
+        load_w2(1, 0)
+        load_w2(1, 1)
         load_lim(0)
-        load_w2(1, 0, 0, 512)
-        load_w2(1, 1, 0, 512)
         load_lim(1)
         load_scales(w3_s, w3_scales)
         load_lim(2)
@@ -125,10 +133,15 @@ def tile_list_stowage_bay_score_kernel(tc, tab_words, tab_scales, offs, w1_words
         def order_w1_words(b, tag=None):
             w1_w[b] = held([P, 2 * H], U8, "w1_w%d" % b, tag=tag)
             nc.vector.tensor_copy(
-                out=w1_w[b][:].bitcast(U16).rearrange("p (a t m) -> p a m t", a=2, t=4),
-                in_=w1_w_raw[b][:].bitcast(U16).rearrange("p (a m t) -> p a m t", a=2, t=4),
+                out=w1_w[b][:].bitcast(U16).rearrange("p (a i m) -> p a i m", a=2, i=4),
+                in_=w1_w_raw[b][:].bitcast(U16).rearrange("p (a m i) -> p a i m", a=2, i=4),
             )
 
+        def order_w1_scales(b):
+            nc.vector.tensor_copy(
+                out=w1_s[b][:].rearrange("p (a i m) -> p a i m", a=2, i=4),
+                in_=w1_s_raw[:].rearrange("p (a b m i) -> p b a i m", a=2, b=2, i=4)[:, b],
+            )
 
         v_w = [held([P, S], U32, "v_w%d" % a) for a in range(2)]
         v_s = [held([P, S], U8, "v_s%d" % a) for a in range(2)]
@@ -137,14 +150,8 @@ def tile_list_stowage_bay_score_kernel(tc, tab_words, tab_scales, offs, w1_words
             nc.vector.tensor_copy(v_s[a][:], tab_s[:, a * T : (a + 1) * T].indirect(idx[:]))
         order_w1_words(0)
         nc.vector.tensor_copy(v_w[1][:], tab_w[1][:].bitcast(U32).indirect(idx[:]))
-
-        def order_w1_scales(b):
-            nc.vector.tensor_copy(
-                out=w1_s[b][:].rearrange("p (a t m) -> p a m t", a=2, t=4),
-                in_=w1_s_raw[:].rearrange("p (a b m t) -> p b a m t", a=2, b=2, t=4)[:, b],
-            )
-
         order_w1_scales(0)
+        order_w1_scales(1)
 
         neg_d1 = {}
 
@@ -164,63 +171,57 @@ def tile_list_stowage_bay_score_kernel(tc, tab_words, tab_scales, offs, w1_words
                 )
             nc.scalar.activation(neg_d1[s], d1[:], ACT.Copy, scale=-1.0)
 
-        q1_w = [held([P, PASS], U32, "q1_w%d" % u) for u in range(2)]
-        q1_s = [held([P, PASS], U8, "q1_s%d" % u) for u in range(2)]
-        g0 = {(a, u): held([P, 2 * PASS], BF16, "w2_g0%d%d" % (a, u)) for a in range(2) for u in range(2)}
-        g1_span = shared.tile([P, 8 * PASS + 64], BF16, name="g1_span", offset=4096 - 64, align_bytes=64)
-        g1_late = held([P, 4 * PASS], BF16, "w2_g1")
-        g1 = [g1_span[:, 0 : 4 * PASS], g1_late[:]]
+        def round_w2(dst, b, a, u):
+            nc.scalar.activation(
+                dst.rearrange("p (e m j) -> p m j e", e=2, j=4),
+                w2_raw[(b, a)][:].rearrange("p j (m i) -> p m j i", i=4)[:, :, :, 2 * u : 2 * u + 2],
+                ACT.Copy,
+            )
 
-        def cast_first(a, c0, c1, u):
-            dst = g0[(a, u)][:].rearrange("p (t m j) -> p m j t", t=2, j=4)[:, c0 // 4 : c1 // 4]
-            src = w2_raw[(0, a, c0)][:].rearrange("p j (m t) -> p m j t", t=4)[:, :, :, 2 * u : 2 * u + 2]
-            if a == 1 and (u == 0 or c0 == 0):
-                nc.vector.tensor_copy(out=dst, in_=src)
-            else:
+        w2_first = {(a, u): held([P, 2 * PASS], BF16, "w2_first%d%d" % (a, u)) for a in range(2) for u in range(2)}
+        w2_codes = {}
+
+        def round_w2_rows(v, u):
+            dst = w2_first[(1, u)][:].rearrange("p (e m j) -> p m e j", e=2, j=4)[:, :, :, 2 * v : 2 * v + 2]
+            src = w2_rows[v][:].rearrange("p j (m i) -> p m i j", i=4)[:, :, 2 * u : 2 * u + 2, :]
+            if u == 1 and v == 1:
                 nc.scalar.activation(dst, src, ACT.Copy)
+            else:
+                nc.vector.tensor_copy(out=dst, in_=src)
 
-        q0 = {}
+        def quantize_first(a, u):
+            words = held([P, 2 * P], U32, "first_w%d%d" % (a, u))
+            scales = held([P, 2 * P], U8, "first_s%d%d" % (a, u))
+            nc.vector.quantize_mx(out=words[:].bitcast(FP8X4), scales=scales[:], in_=w2_first[(a, u)][:])
+            w2_codes[(u, a)] = (words[:], scales[:])
 
-        def quantize_first(a, u, tag=None):
-            words = held([P, 2 * P], U32, "q0_w%d%d" % (a, u), tag=tag)
-            scales = held([P, 2 * P], U8, "q0_s%d%d" % (a, u))
-            q0[(a, u)] = (words, scales)
-            nc.vector.quantize_mx(out=words[:].bitcast(FP8X4), scales=scales[:], in_=g0[(a, u)][:])
-
-        cast_first(0, 0, 512, 0)
-        cast_first(0, 0, 512, 1)
-        early_d1 = held([P, 4, S], F32, "early_d1", tag="w2_raw00_0")
+        round_w2(w2_first[(0, 0)][:], 0, 0, 0)
+        round_w2(w2_first[(0, 1)][:], 0, 0, 1)
+        early_d1 = held([P, 4, S], F32, "early_d1", tag="w2_raw00")
         for s in range(4):
             neg_d1[s] = early_d1[:, s, :]
         first_product(0)
         first_product(1)
         quantize_first(0, 0)
-        for c0 in (0, 256):
-            cast_first(1, c0, c0 + 256, 0)
+        round_w2_rows(0, 0)
+        round_w2_rows(0, 1)
+        quantize_first(0, 1)
+        round_w2_rows(1, 0)
         quantize_first(1, 0)
-        order_w1_scales(1)
-        for c0 in (0, 256):
-            cast_first(1, c0, c0 + 256, 1)
+        round_w2_rows(1, 1)
 
         d2 = {}
 
-        def second_products(k, tags):
-            pair = (2 * k, 2 * k + 1)
-            for s in pair:
-                d2[s] = bank(tags[s % 2])
+        def second_products(k, letters):
+            for e in range(2):
+                d2[2 * k + e] = bank(letters[e])
             for a in range(2):
-                for s in pair:
-                    b, i = divmod(s, 4)
-                    if b == 0:
-                        words, scales = q0[(a, i // 2)]
-                        col = (i % 2) * P
-                    else:
-                        words, scales = q1_w[i // 2], q1_s[i // 2]
-                        col = (2 * a + i % 2) * P
+                words, scales = w2_codes[(k, a)]
+                for e in range(2):
                     nc.tensor.matmul_mx(
-                        out=d2[s][:],
-                        lhsT=words[:, col : col + P].bitcast(FP8X4),
-                        lhsT_scale=scales[:, col : col + P],
+                        out=d2[2 * k + e][:],
+                        lhsT=words[:, e * P : (e + 1) * P].bitcast(FP8X4),
+                        lhsT_scale=scales[:, e * P : (e + 1) * P],
                         rhs=v_w[a][:].bitcast(FP8X4),
                         rhs_scale=v_s[a][:],
                         start=(a == 0),
@@ -229,11 +230,7 @@ def tile_list_stowage_bay_score_kernel(tc, tab_words, tab_scales, offs, w1_words
 
         neg_h = {}
 
-        def larger(k, tag=None):
-            if k == 1:
-                both = shared.tile([P, 2, S], F32, name="neg_h1", offset=0, align_bytes=64)
-            else:
-                both = held([P, 2, S], F32, "neg_h%d" % k, tag=tag)
+        def larger(k, both):
             for e in range(2):
                 s = 2 * k + e
                 neg_h[s] = both[:, e, :]
@@ -244,32 +241,45 @@ def tile_list_stowage_bay_score_kernel(tc, tab_words, tab_scales, offs, w1_words
         def scatter(s):
             nc.vector.tensor_tensor(pages[s % 4][:].indirect(idx2[:]), neg_h[s], wgt[:], ALU.mult)
 
-        z_t = [
-            shared.tile([P, 512], F32, name="z_t%d" % c, offset=4096 + 2048 * c, align_bytes=64) for c in range(NCH)
-        ]
+        z_t = [placed([P, 512], F32, "z_t%d" % c, (2 + c) * UNIT) for c in range(NCH)]
+
+        def z_t_pairs(c):
+            return z_t[c][:].bitcast(BF16).rearrange("m (mb u q e) -> m mb u q e", mb=2, u=2, e=2)
 
         def turn(acc, slot, src, start, stop):
             nc.tensor.matmul(
                 out=acc[:, slot * P : (slot + 1) * P], lhsT=src, rhs=ident[:], is_transpose=True, start=start, stop=stop
             )
 
-        def subtract_pair(k, tags):
-            u = k % 2
-            acc = [bank(t) for t in tags]
-            for c in range(NCH):
-                for mb in range(2):
-                    for e in range(2):
-                        m0 = c * CH + mb * P
-                        turn(acc[c], 2 * mb + e, lim_t[k][:, e, m0 : m0 + P], mb == 0 and e == 0, False)
-            for e in range(2):
+        def subtract_pair(k, letters, pages_first):
+            acc = [bank(letter) for letter in letters]
+
+            def turn_limits(opens):
                 for c in range(NCH):
-                    for mb in range(2):
+                    for slot in range(4):
+                        mb, e = divmod(slot, 2)
                         m0 = c * CH + mb * P
-                        turn(acc[c], 2 * mb + e, pages[(2 * k + e) % 4][:, m0 : m0 + P], False, mb == 1 and e == 1)
+                        src = lim_t[k][:, e, m0 : m0 + P]
+                        turn(acc[c], slot, src, opens and slot == 0, not opens and slot == 3)
+
+            def turn_pages(opens):
+                for e in range(2):
+                    for c in range(NCH):
+                        for mb in range(2):
+                            slot = 2 * mb + e
+                            m0 = c * CH + mb * P
+                            src = pages[(2 * k + e) % 4][:, m0 : m0 + P]
+                            turn(acc[c], slot, src, opens and slot == 0, not opens and slot == 3)
+
+            if pages_first:
+                turn_pages(True)
+                turn_limits(False)
+            else:
+                turn_limits(True)
+                turn_pages(False)
             for c in range(NCH):
                 nc.scalar.copy(
-                    out=z_t[c][:].bitcast(BF16).rearrange("m (mb u q e) -> m mb u q e", mb=2, u=2, e=2)[:, :, u],
-                    in_=acc[c][:].rearrange("m (mb e q) -> m mb q e", mb=2, e=2),
+                    out=z_t_pairs(c)[:, :, k % 2], in_=acc[c][:].rearrange("m (mb e q) -> m mb q e", mb=2, e=2)
                 )
 
         def turn_back(acc, c, u):
@@ -277,158 +287,154 @@ def tile_list_stowage_bay_score_kernel(tc, tab_words, tab_scales, offs, w1_words
                 w0 = (2 * mb + u) * P
                 nc.tensor.transpose(acc[:, u * CH + mb * P : u * CH + (mb + 1) * P], z_t[c][:, w0 : w0 + P], ident[:])
 
-        def empty_turned(acc, dst):
+        def empty_turned(acc, m0, m1, dst):
             nc.scalar.copy(
-                out=dst.bitcast(F32).rearrange("p (m u) -> p m u", u=2), in_=acc[:].rearrange("p (u m) -> p m u", u=2)
+                out=dst.bitcast(F32).rearrange("p (m u) -> p m u", u=2),
+                in_=acc[:].rearrange("p (u m) -> p m u", u=2)[:, m0:m1],
             )
 
-        y = {}
-
-        def score(b, c, codes, scales, tags=None):
-            first = b == 0
-            for hf in range(2):
-                if first:
-                    y[(c, hf)] = bank(tags[hf])
-                for nt in range(2):
-                    col = b * N + (2 * hf + nt) * P
-                    nc.tensor.matmul_mx(
-                        out=y[(c, hf)][:, nt * CH : (nt + 1) * CH],
-                        lhsT=w3_w[:, col : col + P].bitcast(FP8X4),
-                        lhsT_scale=w3_s[:, col : col + P],
-                        rhs=codes.bitcast(FP8X4),
-                        rhs_scale=scales,
-                        start=(first and nt == 0),
-                        stop=(not first and nt == 1),
-                    )
-
         second_products(0, "EF")
-        quantize_first(0, 1)
-        order_w1_words(1, tag="w2_g010")
-        larger(0)
+        order_w1_words(1, tag="w2_first10")
+        larger(0, held([P, 2, S], F32, "neg_h0"))
         quantize_first(1, 1)
         first_product(2)
         first_product(3)
         second_products(1, "EF")
-        clear_page(2, nc.gpsimd, "w2_g011")
-        clear_page(3, nc.gpsimd, "q0_w01")
+        clear_page(1, nc.gpsimd, "w2_first11")
+        clear_page(2, nc.gpsimd, "first_w01")
+        clear_page(3, nc.gpsimd, "first_w11")
         scatter(0)
         scatter(1)
 
-        def cast_second(u):
+        pair2_span = placed([P, (5 * UNIT + 128) // 2], BF16, "pair2_span", UNIT - 64)
+        pair3_rounded = held([P, 4 * PASS], BF16, "pair3_rounded")
+        w2_second = [pair2_span[:, 0 : 4 * PASS], pair3_rounded[:]]
+        for u in range(2):
             for a in range(2):
-                nc.scalar.activation(
-                    g1[u].rearrange("p (a t m j) -> p a m j t", a=2, t=2, j=4)[:, a],
-                    w2_raw[(1, a, 0)][:].rearrange("p j (m t) -> p m j t", t=4)[:, :, :, 2 * u : 2 * u + 2],
-                    ACT.Copy,
-                )
+                round_w2(w2_second[u][:, 2 * PASS * a : 2 * PASS * (a + 1)], 1, a, u)
 
         def quantize_second(u):
-            nc.vector.quantize_mx(out=q1_w[u][:].bitcast(FP8X4), scales=q1_s[u][:], in_=g1[u])
+            words = held([P, PASS], U32, "second_w%d" % u)
+            scales = held([P, PASS], U8, "second_s%d" % u)
+            nc.vector.quantize_mx(out=words[:].bitcast(FP8X4), scales=scales[:], in_=w2_second[u])
+            for a in range(2):
+                cols = slice(2 * P * a, 2 * P * (a + 1))
+                w2_codes[(2 + u, a)] = (words[:, cols], scales[:, cols])
 
-        cast_second(0)
-        late_d1 = [
-            held([P, 2, S], F32, "late_d1"),
-            shared.tile([P, 2, S], F32, name="last_d1", offset=4096 + 2048 * 4, align_bytes=64),
-        ]
+        late_d1 = [held([P, 2, S], F32, "pair2_d1"), placed([P, 2, S], F32, "pair3_d1", 6 * UNIT)]
         for s in range(4, 8):
-            neg_d1[s] = late_d1[s // 6][:, s % 2, :]
+            neg_d1[s] = late_d1[s // 2 - 2][:, s % 2, :]
             first_product(s)
         quantize_second(0)
-        larger(1)
+        larger(1, placed([P, 2, S], F32, "neg_h1", 0))
         second_products(2, "EF")
-        subtract_pair(0, "CDAB")
-        cast_second(1)
+        subtract_pair(0, "CDAB", True)
         scatter(2)
         scatter(3)
+
         quantize_second(1)
-        larger(2, tag="w2_g1")
-        subtract_pair(1, "CDAB")
+        larger(2, held([P, 2, S], F32, "neg_h2", tag="pair3_rounded"))
+        subtract_pair(1, "CDAB", False)
         second_products(3, "CD")
         z0 = [held([P, 8 * CH], BF16, "z0%d" % h) for h in range(2)]
         for c in range(NCH):
-            acc = bank("GHEF"[c])
+            acc = bank("EF"[c % 2])
             for u in range(2):
                 turn_back(acc, c, u)
-            empty_turned(acc, z0[c // 2][:, 4 * CH * (c % 2) : 4 * CH * (c % 2 + 1)])
+            empty_turned(acc, 0, CH, z0[c // 2][:, 4 * CH * (c % 2) : 4 * CH * (c % 2 + 1)])
         scatter(4)
         scatter(5)
-        subtract_pair(2, "GHEF")
+        subtract_pair(2, "GHAB", False)
         z0_w = [held([P, 2 * CH], U32, "z0_w%d" % h) for h in range(2)]
         z0_s = [held([P, 2 * CH], U8, "z0_s%d" % h) for h in range(2)]
         for h in range(2):
             nc.vector.quantize_mx(out=z0_w[h][:].bitcast(FP8X4), scales=z0_s[h][:], in_=z0[h][:])
-        larger(3, tag="z01")
+        larger(3, held([P, 2, S], F32, "neg_h3", tag="z01"))
 
-        def first_score(c, tags):
+        y = {}
+
+        def score(b, c, n, lo, hi, codes, scales, start, stop):
+            col = b * N + n * P
+            nc.tensor.matmul_mx(
+                out=y[(c, n // 2)][:, (n % 2) * CH + lo : (n % 2) * CH + hi],
+                lhsT=w3_w[:, col : col + P].bitcast(FP8X4),
+                lhsT_scale=w3_s[:, col : col + P],
+                rhs=codes.bitcast(FP8X4),
+                rhs_scale=scales,
+                start=start,
+                stop=stop,
+            )
+
+        def first_score(c, letters):
             cols = slice(CH * (c % 2), CH * (c % 2 + 1))
-            score(0, c, z0_w[c // 2][:, cols], z0_s[c // 2][:, cols], tags)
+            for n in range(4):
+                if n % 2 == 0:
+                    y[(c, n // 2)] = bank(letters[n // 2])
+                score(0, c, n, 0, CH, z0_w[c // 2][:, cols], z0_s[c // 2][:, cols], n % 2 == 0, False)
 
         scatter(6)
-        acc6 = [bank(t) for t in "GHEF"]
+
+        six = [bank(letter) for letter in "EFCD"]
+        blocks = T2 // P
+        for blk in range(blocks):
+            turn(six[blk // 2], blk % 2, lim_t[3][:, 0, blk * P : (blk + 1) * P], blk % 2 == 0, False)
+        back = [bank(letter) for letter in "GHAB"]
         for c in range(NCH):
-            for mb in range(2):
-                m0 = c * CH + mb * P
-                turn(acc6[c], mb, lim_t[3][:, 0, m0 : m0 + P], mb == 0, False)
-        back = {}
-        for c in range(NCH):
-            back[c] = bank("ABCD"[c])
             turn_back(back[c], c, 0)
-        for c in range(NCH):
-            for mb in range(2):
-                m0 = c * CH + mb * P
-                turn(acc6[c], mb, pages[2][:, m0 : m0 + P], False, mb == 1)
-        z1 = [held([P, 4 * CH], BF16, "z1%d" % c) for c in range(NCH)]
+        for blk in range(blocks):
+            turn(six[blk // 2], blk % 2, pages[2][:, blk * P : (blk + 1) * P], False, blk % 2 == 1)
 
         def round_six(c):
             nc.scalar.copy(
-                out=z_t[c][:].bitcast(BF16).rearrange("m (mb u q e) -> m mb u q e", mb=2, u=2, e=2)[:, :, 1, :, 0],
-                in_=acc6[c][:, 0:CH].rearrange("m (mb q) -> m mb q", mb=2),
+                out=z_t_pairs(c)[:, :, 1, :, 0],
+                in_=six[c][:, 0:CH].rearrange("m (mb q) -> m mb q", mb=2),
             )
 
+        z1 = {(c, h): held([P, 4 * P], BF16, "z1_%d%d" % (c, h)) for c in range(NCH) for h in range(2)}
         round_six(0)
         round_six(1)
         for c in range(NCH):
             turn_back(back[c], c, 1)
-            empty_turned(back[c], z1[c][:])
+            for h in range(2):
+                empty_turned(back[c], h * P, (h + 1) * P, z1[(c, h)][:])
             if c == 0:
                 round_six(2)
                 round_six(3)
         scatter(7)
-        first_score(0, "GH")
-        first_score(1, "EF")
+        first_score(0, "EF")
+        first_score(1, "CD")
+
         for c in range(NCH):
-            cols = slice(c * CH, (c + 1) * CH)
             for h in range(2):
                 m0 = c * CH + h * P
                 nc.vector.tensor_tensor(
-                    z1[c][:].rearrange("p (m i) -> p m i", i=4)[:, h * P : (h + 1) * P, 3],
-                    lim_t[3][:, 1, m0 : m0 + P], pages[3][:, m0 : m0 + P], ALU.add,
+                    z1[(c, h)][:].rearrange("p (m i) -> p m i", i=4)[:, :, 3],
+                    lim_t[3][:, 1, m0 : m0 + P],
+                    pages[3][:, m0 : m0 + P],
+                    ALU.add,
                 )
+            z1_w = held([P, CH], U32, "z1_w%d" % c)
+            z1_s = held([P, CH], U8, "z1_s%d" % c)
             for h in range(2):
-                z1_w = held([P, P], U32, "z1_w%d%d" % (c, h))
-                z1_s = held([P, P], U8, "z1_s%d%d" % (c, h))
-                nc.vector.quantize_mx(out=z1_w[:].bitcast(FP8X4), scales=z1_s[:], in_=z1[c][:, 4 * P * h : 4 * P * (h + 1)])
-                for hf in range(2):
-                    for nt in range(2):
-                        col = N + (2 * hf + nt) * P
-                        nc.tensor.matmul_mx(
-                            out=y[(c, hf)][:, nt * CH + h * P : nt * CH + (h + 1) * P],
-                            lhsT=w3_w[:, col : col + P].bitcast(FP8X4),
-                            lhsT_scale=w3_s[:, col : col + P],
-                            rhs=z1_w[:].bitcast(FP8X4),
-                            rhs_scale=z1_s[:],
-                            start=False,
-                            stop=(h == 1 and nt == 1),
-                        )
+                lo, hi = h * P, (h + 1) * P
+                nc.vector.quantize_mx(out=z1_w[:, lo:hi].bitcast(FP8X4), scales=z1_s[:, lo:hi], in_=z1[(c, h)][:])
+                for n in range(2):
+                    score(1, c, n, lo, hi, z1_w[:, lo:hi], z1_s[:, lo:hi], False, h == 1 and n == 1)
+            for n in range(2, 4):
+                score(1, c, n, 0, CH, z1_w[:], z1_s[:], False, n == 3)
             if c < 2:
-                first_score(c + 2, ("AB", "CD")[c])
+                first_score(c + 2, ("GH", "AB")[c])
             if c == 0:
-                res = shared.tile([P, 2, 2 * CH], F32, name="res0", offset=4096 + 2048 * 3, align_bytes=64)
+                res = placed([P, 2, 2 * CH], F32, "res0", 5 * UNIT)
             else:
                 res = held([P, 2, 2 * CH], F32, "res%d" % c)
             for hf in range(2):
-                nc.scalar.activation(res[:, hf, :], y[(c, hf)][:], ACT.Square)
-                nc.sync.dma_start(
-                    out=out[2 * P * hf : 2 * P * (hf + 1), cols].rearrange("(n p) m -> p n m", p=P),
-                    in_=res[:, hf, :].rearrange("p (n m) -> p n m", n=2),
-                )
+                step = 1 if (c, hf) in ((0, 0), (NCH - 1, 1)) else 2
+                for n0 in range(0, 2, step):
+                    part = slice(n0 * CH, (n0 + step) * CH)
+                    rows = slice(P * (2 * hf + n0), P * (2 * hf + n0 + step))
+                    nc.scalar.activation(res[:, hf, part], y[(c, hf)][:, part], ACT.Square)
+                    nc.sync.dma_start(
+                        out=out[rows, c * CH : (c + 1) * CH].rearrange("(n p) m -> p n m", p=P),
+                        in_=res[:, hf, part].rearrange("p (n m) -> p n m", n=step),
+                    )

@@ -336,20 +336,25 @@ def tile_list_stowage_bay_score_kernel(
         larger(2, held([P, 2, S], F32, "neg_h2", tag="pair3_rounded"))
         subtract_pair(1, "CDAB", False)
         second_products(3, "CD")
-        z0 = [held([P, 8 * CH], BF16, "z0%d" % h) for h in range(2)]
+        z0 = [held([P, 4 * CH], BF16, "z0%d" % c) for c in range(NCH)]
         for c in range(NCH):
             acc = bank("EF"[c % 2])
             for u in range(2):
                 turn_back(acc, c, u)
-            empty_turned(acc, 0, CH, z0[c // 2][:, 4 * CH * (c % 2) : 4 * CH * (c % 2 + 1)])
+            empty_turned(acc, 0, CH, z0[c][:])
         scatter(4)
         scatter(5)
         subtract_pair(2, "GHAB", False)
-        z0_w = [held([P, 2 * CH], U32, "z0_w%d" % h) for h in range(2)]
-        z0_s = [held([P, 2 * CH], U8, "z0_s%d" % h) for h in range(2)]
-        for h in range(2):
-            nc.vector.quantize_mx(out=z0_w[h][:].bitcast(FP8X4), scales=z0_s[h][:], in_=z0[h][:])
-        larger(3, held([P, 2, S], F32, "neg_h3", tag="z01"))
+        z0_codes = {}
+
+        def quantize_z0(c, tag=None):
+            words = held([P, CH], U32, "z0_w%d" % c, tag=tag)
+            scales = held([P, CH], U8, "z0_s%d" % c)
+            nc.vector.quantize_mx(out=words[:].bitcast(FP8X4), scales=scales[:], in_=z0[c][:])
+            z0_codes[c] = (words, scales)
+
+        quantize_z0(0)
+        larger(3, held([P, 2, S], F32, "neg_h3", tag="z00"))
 
         y = {}
 
@@ -366,11 +371,11 @@ def tile_list_stowage_bay_score_kernel(
             )
 
         def first_score(c, letters):
-            cols = slice(CH * (c % 2), CH * (c % 2 + 1))
+            words, scales = z0_codes[c]
             for n in range(4):
                 if n % 2 == 0:
                     y[(c, n // 2)] = bank(letters[n // 2])
-                score(0, c, n, 0, CH, z0_w[c // 2][:, cols], z0_s[c // 2][:, cols], n % 2 == 0, False)
+                score(0, c, n, 0, CH, words[:], scales[:], n % 2 == 0, False)
 
         scatter(6)
 
@@ -402,7 +407,6 @@ def tile_list_stowage_bay_score_kernel(
                 round_six(3)
         scatter(7)
         first_score(0, "EF")
-        first_score(1, "CD")
 
         for c in range(NCH):
             for h in range(2):
@@ -422,8 +426,9 @@ def tile_list_stowage_bay_score_kernel(
                     score(1, c, n, lo, hi, z1_w[:, lo:hi], z1_s[:, lo:hi], False, h == 1 and n == 1)
             for n in range(2, 4):
                 score(1, c, n, 0, CH, z1_w[:], z1_s[:], False, n == 3)
-            if c < 2:
-                first_score(c + 2, ("GH", "AB")[c])
+            if c + 1 < NCH:
+                quantize_z0(c + 1, tag="z1_%d0" % c)
+                first_score(c + 1, ("CD", "GH", "AB")[c])
             if c == 0:
                 res = placed([P, 2, 2 * CH], F32, "res0", 5 * UNIT)
             else:

@@ -49,13 +49,9 @@ def tile_list_stowage_bay_score_kernel(
         for scale_tile in (tab_s, w1_s_raw, w3_s):
             nc.vector.memset(scale_tile[:].bitcast(I32), 0)
 
-        pages = {}
-
-        def clear_page(i, engine, tag=None):
-            pages[i] = held([P, T2], F32, "page%d" % i, tag=tag)
-            engine.memset(pages[i][:].bitcast(I32), 0)
-
-        clear_page(0, nc.vector)
+        pages = [held([P, T2], F32, "page%d" % i) for i in range(4)]
+        for page in pages:
+            nc.vector.memset(page[:].bitcast(I32), 0)
         ident = held([P, P], F32, "ident")
         make_identity(nc, ident[:])
 
@@ -300,9 +296,6 @@ def tile_list_stowage_bay_score_kernel(
         first_product(2)
         first_product(3)
         second_products(1, "EF")
-        clear_page(1, nc.gpsimd, "w2_first11")
-        clear_page(2, nc.gpsimd, "first_w01")
-        clear_page(3, nc.gpsimd, "first_w11")
         scatter(0)
         scatter(1)
 
@@ -347,14 +340,16 @@ def tile_list_stowage_bay_score_kernel(
         subtract_pair(2, "GHAB", False)
         z0_codes = {}
 
-        def quantize_z0(c, tag=None):
-            words = held([P, CH], U32, "z0_w%d" % c, tag=tag)
+        def quantize_z0(c, tag=None, offset=None):
+            if offset is None:
+                words = held([P, CH], U32, "z0_w%d" % c, tag=tag)
+            else:
+                words = placed([P, CH], U32, "z0_w%d" % c, offset)
             scales = held([P, CH], U8, "z0_s%d" % c)
             nc.vector.quantize_mx(out=words[:].bitcast(FP8X4), scales=scales[:], in_=z0[c][:])
             z0_codes[c] = (words, scales)
 
-        quantize_z0(0)
-        larger(3, held([P, 2, S], F32, "neg_h3", tag="z00"))
+        larger(3, held([P, 2, S], F32, "neg_h3"))
 
         y = {}
 
@@ -378,6 +373,7 @@ def tile_list_stowage_bay_score_kernel(
                 score(0, c, n, 0, CH, words[:], scales[:], n % 2 == 0, False)
 
         scatter(6)
+        quantize_z0(0, offset=7 * UNIT)
 
         six = [bank(letter) for letter in "EFCD"]
         blocks = T2 // P
@@ -395,13 +391,14 @@ def tile_list_stowage_bay_score_kernel(
                 in_=six[c][:, 0:CH].rearrange("m (mb q) -> m mb q", mb=2),
             )
 
-        z1 = {(c, h): held([P, 4 * P], BF16, "z1_%d%d" % (c, h)) for c in range(NCH) for h in range(2)}
+        z1 = {(c, h): held([P, 4 * P], BF16, "z1_%d%d" % (c, h)) for c in range(NCH - 1) for h in range(2)}
         round_six(0)
         round_six(1)
         for c in range(NCH):
             turn_back(back[c], c, 1)
-            for h in range(2):
-                empty_turned(back[c], h * P, (h + 1) * P, z1[(c, h)][:])
+            if c + 1 < NCH:
+                for h in range(2):
+                    empty_turned(back[c], h * P, (h + 1) * P, z1[(c, h)][:])
             if c == 0:
                 round_six(2)
                 round_six(3)
@@ -429,6 +426,9 @@ def tile_list_stowage_bay_score_kernel(
             if c + 1 < NCH:
                 quantize_z0(c + 1, tag="z1_%d0" % c)
                 first_score(c + 1, ("CD", "GH", "AB")[c])
+            if c < 2:
+                z1[(NCH - 1, c)] = held([P, 4 * P], BF16, "z1_last%d" % c, tag="z1_%d1" % c)
+                empty_turned(back[NCH - 1], c * P, (c + 1) * P, z1[(NCH - 1, c)][:])
             if c == 0:
                 res = placed([P, 2, 2 * CH], F32, "res0", 5 * UNIT)
             else:

@@ -21,6 +21,7 @@ P = 128
 PASS = 512
 CH = 256
 NCH = T2 // CH
+PAGES = 3
 UNIT = 2048
 
 
@@ -49,7 +50,7 @@ def tile_list_stowage_bay_score_kernel(
         for scale_tile in (tab_s, w1_s_raw, w3_s):
             nc.vector.memset(scale_tile[:].bitcast(I32), 0)
 
-        pages = [held([P, T2], F32, "page%d" % i) for i in range(4)]
+        pages = [held([P, T2], F32, "page%d" % i) for i in range(PAGES)]
         for page in pages:
             nc.vector.memset(page[:].bitcast(I32), 0)
         ident = held([P, P], F32, "ident")
@@ -81,7 +82,10 @@ def tile_list_stowage_bay_score_kernel(
         w2_raw = {}
 
         def load_w2(b, a):
-            w2_raw[(b, a)] = held([P, 4, PASS], F32, "w2_raw%d%d" % (b, a))
+            if (b, a) == (0, 0):
+                w2_raw[(b, a)] = placed([P, 4, PASS], F32, "w2_raw00", 8 * UNIT)
+            else:
+                w2_raw[(b, a)] = held([P, 4, PASS], F32, "w2_raw%d%d" % (b, a))
             nc.sync.dma_start(out=w2_raw[(b, a)][:], in_=w2_block(b, a))
 
         lim_t = {}
@@ -98,11 +102,22 @@ def tile_list_stowage_bay_score_kernel(
         idx2 = lists.tile([P, S // 16], U16, name="idx2")
         load_table(0)
         nc.sync.dma_start(idx[:], offs)
-        load_scales(tab_s, tab_scales)
+        nc.sync.dma_start(
+            out=tab_s[0:P:8, :].bitcast(I32).rearrange("q (a c) -> q a c", a=2),
+            in_=tab_scales.rearrange("a q c -> q a c").bitcast(I32),
+        )
         load_w1(0)
         load_table(1)
         load_scales(w1_s_raw, w1_scales)
         load_w2(0, 0)
+        picked_s = held([P, 2 * S], U8, "picked_s")
+        for a in range(2):
+            nc.vector.tensor_copy(picked_s[:, a * S : (a + 1) * S], tab_s[:, a * T : (a + 1) * T].indirect(idx[:]))
+        moved_s = held([P, 2 * S], U8, "moved_s")
+        nc.vector.tensor_copy(out=moved_s[:].bitcast(I32), in_=picked_s[:].bitcast(I32))
+        for r in range(1, 4):
+            nc.sync.dma_start(out=moved_s[r:P:32, :].bitcast(I32), in_=picked_s[8 * r : P : 32, :].bitcast(I32))
+        v_s = [moved_s[:, a * S : (a + 1) * S] for a in range(2)]
         w2_rows = [held([P, 2, PASS], F32, "w2_rows%d" % v) for v in range(2)]
         for v in range(2):
             nc.sync.dma_start(out=w2_rows[v][:], in_=w2_block(0, 1)[:, 2 * v : 2 * v + 2, :])
@@ -139,11 +154,8 @@ def tile_list_stowage_bay_score_kernel(
                 in_=w1_s_raw[:].rearrange("p (a b m i) -> p b a i m", a=2, b=2, i=4)[:, b],
             )
 
-        v_w = [held([P, S], U32, "v_w%d" % a) for a in range(2)]
-        v_s = [held([P, S], U8, "v_s%d" % a) for a in range(2)]
+        v_w = [held([P, S], U32, "v_w0", tag="tab_s"), held([P, S], U32, "v_w1")]
         nc.vector.tensor_copy(v_w[0][:], tab_w[0][:].bitcast(U32).indirect(idx[:]))
-        for a in range(2):
-            nc.vector.tensor_copy(v_s[a][:], tab_s[:, a * T : (a + 1) * T].indirect(idx[:]))
         order_w1_words(0)
         nc.vector.tensor_copy(v_w[1][:], tab_w[1][:].bitcast(U32).indirect(idx[:]))
         order_w1_scales(0)
@@ -153,7 +165,7 @@ def tile_list_stowage_bay_score_kernel(
 
         def first_product(s):
             b, i = divmod(s, 4)
-            d1 = bank("GH"[s % 2])
+            d1 = bank(("GH" if s < 2 else "EF")[s % 2])
             for a in range(2):
                 col = a * PASS + i * P
                 nc.tensor.matmul_mx(
@@ -161,7 +173,7 @@ def tile_list_stowage_bay_score_kernel(
                     lhsT=w1_w[b][:, 2 * col : 2 * (col + P)].bitcast(FP4X4),
                     lhsT_scale=w1_s[b][:, col : col + P],
                     rhs=v_w[a][:].bitcast(FP8X4),
-                    rhs_scale=v_s[a][:],
+                    rhs_scale=v_s[a],
                     start=(a == 0),
                     stop=(a == 1),
                 )
@@ -174,28 +186,44 @@ def tile_list_stowage_bay_score_kernel(
                 ACT.Copy,
             )
 
-        w2_first = {(a, u): held([P, 2 * PASS], BF16, "w2_first%d%d" % (a, u)) for a in range(2) for u in range(2)}
+        w2_first = {au: held([P, 2 * PASS], BF16, "w2_first%d%d" % au) for au in ((0, 0), (0, 1), (1, 1))}
+        w2_last = [held([P, PASS], BF16, "w2_last%d" % e) for e in range(2)]
         w2_codes = {}
 
         def round_w2_rows(v, u):
-            dst = w2_first[(1, u)][:].rearrange("p (e m j) -> p m e j", e=2, j=4)[:, :, :, 2 * v : 2 * v + 2]
             src = w2_rows[v][:].rearrange("p j (m i) -> p m i j", i=4)[:, :, 2 * u : 2 * u + 2, :]
-            if u == 1 and v == 1:
+            if u == 0:
+                for e in range(2):
+                    dst = w2_last[e][:].rearrange("p (m j) -> p m j", j=4)[:, :, 2 * v : 2 * v + 2]
+                    nc.vector.tensor_copy(out=dst, in_=src[:, :, e, :])
+                return
+            dst = w2_first[(1, u)][:].rearrange("p (e m j) -> p m e j", e=2, j=4)[:, :, :, 2 * v : 2 * v + 2]
+            if v == 1:
                 nc.scalar.activation(dst, src, ACT.Copy)
             else:
                 nc.vector.tensor_copy(out=dst, in_=src)
 
         def quantize_first(a, u):
-            words = held([P, 2 * P], U32, "first_w%d%d" % (a, u))
+            if (a, u) == (1, 1):
+                words = placed([P, 2 * P], U32, "first_w11", 8 * UNIT)
+            else:
+                words = held([P, 2 * P], U32, "first_w%d%d" % (a, u))
             scales = held([P, 2 * P], U8, "first_s%d%d" % (a, u))
             nc.vector.quantize_mx(out=words[:].bitcast(FP8X4), scales=scales[:], in_=w2_first[(a, u)][:])
-            w2_codes[(u, a)] = (words[:], scales[:])
+            w2_codes[(u, a)] = [(words[:, e * P : (e + 1) * P], scales[:, e * P : (e + 1) * P]) for e in range(2)]
+
+        def quantize_last():
+            w2_codes[(0, 1)] = []
+            for e in range(2):
+                words = held([P, P], U32, "last_w%d" % e)
+                scales = held([P, P], U8, "last_s%d" % e)
+                nc.vector.quantize_mx(out=words[:].bitcast(FP8X4), scales=scales[:], in_=w2_last[e][:])
+                w2_codes[(0, 1)].append((words[:], scales[:]))
 
         round_w2(w2_first[(0, 0)][:], 0, 0, 0)
         round_w2(w2_first[(0, 1)][:], 0, 0, 1)
-        early_d1 = held([P, 4, S], F32, "early_d1", tag="w2_raw00")
         for s in range(4):
-            neg_d1[s] = early_d1[:, s, :]
+            neg_d1[s] = placed([P, S], F32, "early_d1%d" % s, (8 + s) * UNIT)[:]
         first_product(0)
         first_product(1)
         quantize_first(0, 0)
@@ -203,7 +231,7 @@ def tile_list_stowage_bay_score_kernel(
         round_w2_rows(0, 1)
         quantize_first(0, 1)
         round_w2_rows(1, 0)
-        quantize_first(1, 0)
+        quantize_last()
         round_w2_rows(1, 1)
 
         d2 = {}
@@ -211,17 +239,18 @@ def tile_list_stowage_bay_score_kernel(
         def second_products(k, letters):
             for e in range(2):
                 d2[2 * k + e] = bank(letters[e])
-            for a in range(2):
-                words, scales = w2_codes[(k, a)]
+            passes = (1, 0) if k == 1 else (0, 1)
+            for a in passes:
                 for e in range(2):
+                    words, scales = w2_codes[(k, a)][e]
                     nc.tensor.matmul_mx(
                         out=d2[2 * k + e][:],
-                        lhsT=words[:, e * P : (e + 1) * P].bitcast(FP8X4),
-                        lhsT_scale=scales[:, e * P : (e + 1) * P],
+                        lhsT=words.bitcast(FP8X4),
+                        lhsT_scale=scales,
                         rhs=v_w[a][:].bitcast(FP8X4),
-                        rhs_scale=v_s[a][:],
-                        start=(a == 0),
-                        stop=(a == 1),
+                        rhs_scale=v_s[a],
+                        start=(a == passes[0]),
+                        stop=(a == passes[1]),
                     )
 
         neg_h = {}
@@ -235,7 +264,7 @@ def tile_list_stowage_bay_score_kernel(
                 )
 
         def scatter(s):
-            nc.vector.tensor_tensor(pages[s % 4][:].indirect(idx2[:]), neg_h[s], wgt[:], ALU.mult)
+            nc.vector.tensor_tensor(pages[s % PAGES][:].indirect(idx2[:]), neg_h[s], wgt[:], ALU.mult)
 
         z_t = [placed([P, 512], F32, "z_t%d" % c, (2 + c) * UNIT) for c in range(NCH)]
 
@@ -264,7 +293,7 @@ def tile_list_stowage_bay_score_kernel(
                         for mb in range(2):
                             slot = 2 * mb + e
                             m0 = c * CH + mb * P
-                            src = pages[(2 * k + e) % 4][:, m0 : m0 + P]
+                            src = pages[(2 * k + e) % PAGES][:, m0 : m0 + P]
                             turn(acc[c], slot, src, opens and slot == 0, not opens and slot == 3)
 
             if pages_first:
@@ -290,12 +319,12 @@ def tile_list_stowage_bay_score_kernel(
             )
 
         second_products(0, "EF")
-        order_w1_words(1, tag="w2_first10")
+        order_w1_words(1, tag="w2_last0")
         larger(0, held([P, 2, S], F32, "neg_h0"))
         quantize_first(1, 1)
         first_product(2)
         first_product(3)
-        second_products(1, "EF")
+        second_products(1, "GH")
         scatter(0)
         scatter(1)
 
@@ -311,8 +340,8 @@ def tile_list_stowage_bay_score_kernel(
             scales = held([P, PASS], U8, "second_s%d" % u)
             nc.vector.quantize_mx(out=words[:].bitcast(FP8X4), scales=scales[:], in_=w2_second[u])
             for a in range(2):
-                cols = slice(2 * P * a, 2 * P * (a + 1))
-                w2_codes[(2 + u, a)] = (words[:, cols], scales[:, cols])
+                cols = [slice(P * (2 * a + e), P * (2 * a + e + 1)) for e in range(2)]
+                w2_codes[(2 + u, a)] = [(words[:, col], scales[:, col]) for col in cols]
 
         late_d1 = [held([P, 2, S], F32, "pair2_d1"), placed([P, 2, S], F32, "pair3_d1", 6 * UNIT)]
         for s in range(4, 8):
@@ -383,7 +412,7 @@ def tile_list_stowage_bay_score_kernel(
         for c in range(NCH):
             turn_back(back[c], c, 0)
         for blk in range(blocks):
-            turn(six[blk // 2], blk % 2, pages[2][:, blk * P : (blk + 1) * P], False, blk % 2 == 1)
+            turn(six[blk // 2], blk % 2, pages[6 % PAGES][:, blk * P : (blk + 1) * P], False, blk % 2 == 1)
 
         def round_six(c):
             nc.scalar.copy(
@@ -411,7 +440,7 @@ def tile_list_stowage_bay_score_kernel(
                 nc.vector.tensor_tensor(
                     z1[(c, h)][:].rearrange("p (m i) -> p m i", i=4)[:, :, 3],
                     lim_t[3][:, 1, m0 : m0 + P],
-                    pages[3][:, m0 : m0 + P],
+                    pages[7 % PAGES][:, m0 : m0 + P],
                     ALU.add,
                 )
             z1_w = held([P, CH], U32, "z1_w%d" % c)

@@ -45,9 +45,11 @@ def tile_list_stowage_bay_score_kernel(
             return psum.tile([P, 512], F32, name="bank", tag=letter)
 
         tab_s = held([P, 2 * T], U8, "tab_s")
-        w1_s_raw = held([P, 2 * H], U8, "w1_s_raw")
+        w1_s_raw = [held([P, H], U8, "w1_s_raw%d" % b) for b in range(2)]
         w3_s = held([P, 2 * N], U8, "w3_s")
-        for scale_tile in (tab_s, w1_s_raw, w3_s):
+        moved_s = held([P, 2 * S], U8, "moved_s")
+        w1_s = [held([P, H], U8, "w1_s%d" % b) for b in range(2)]
+        for scale_tile in (tab_s, w1_s_raw[0], w1_s_raw[1], moved_s, w1_s[1], w3_s):
             nc.vector.memset(scale_tile[:].bitcast(I32), 0)
 
         pages = [held([P, T2], F32, "page%d" % i) for i in range(PAGES)]
@@ -62,6 +64,22 @@ def tile_list_stowage_bay_score_kernel(
                     out=tile[r:P:32, :].bitcast(I32).rearrange("q (a c) -> q a c", a=2),
                     in_=src[:, r:16:4, :].rearrange("a q c -> q a c").bitcast(I32),
                 )
+
+        def load_spread(tile, src):
+            nc.sync.dma_start(
+                out=tile[4:P:8, :].bitcast(I32).rearrange("q (a c) -> q a c", a=2),
+                in_=src.rearrange("a q c -> q a c").bitcast(I32),
+            )
+
+        def move_rows(dst, src):
+            for r in range(4):
+                nc.sync.dma_start(out=dst[r:P:32, :].bitcast(I32), in_=src[8 * r + 4 : P : 32, :].bitcast(I32))
+
+        def order_w1_scales(dst, b):
+            nc.vector.tensor_copy(
+                out=dst.rearrange("p (a i m) -> p a i m", a=2, i=4),
+                in_=w1_s_raw[b][:].rearrange("p (a m i) -> p a i m", a=2, i=4),
+            )
 
         tab_w = [held([P, T], I32, "tab_w%d" % a) for a in range(2)]
 
@@ -83,7 +101,7 @@ def tile_list_stowage_bay_score_kernel(
 
         def load_w2(b, a):
             if (b, a) == (0, 0):
-                w2_raw[(b, a)] = placed([P, 4, PASS], F32, "w2_raw00", 8 * UNIT)
+                w2_raw[(b, a)] = placed([P, 4, PASS], F32, "w2_raw00", 10 * UNIT)
             else:
                 w2_raw[(b, a)] = held([P, 4, PASS], F32, "w2_raw%d%d" % (b, a))
             nc.sync.dma_start(out=w2_raw[(b, a)][:], in_=w2_block(b, a))
@@ -102,26 +120,40 @@ def tile_list_stowage_bay_score_kernel(
         idx2 = lists.tile([P, S // 16], U16, name="idx2")
         load_table(0)
         nc.sync.dma_start(idx[:], offs)
-        nc.sync.dma_start(
-            out=tab_s[0:P:8, :].bitcast(I32).rearrange("q (a c) -> q a c", a=2),
-            in_=tab_scales.rearrange("a q c -> q a c").bitcast(I32),
-        )
+        load_spread(tab_s, tab_scales)
         load_w1(0)
         load_table(1)
-        load_scales(w1_s_raw, w1_scales)
+        load_scales(w1_s_raw[0], w1_scales[:, :, 0:PASS])
+        load_spread(w1_s_raw[1], w1_scales[:, :, PASS:H])
         load_w2(0, 0)
         picked_s = held([P, 2 * S], U8, "picked_s")
         for a in range(2):
             nc.vector.tensor_copy(picked_s[:, a * S : (a + 1) * S], tab_s[:, a * T : (a + 1) * T].indirect(idx[:]))
-        moved_s = held([P, 2 * S], U8, "moved_s")
-        nc.vector.tensor_copy(out=moved_s[:].bitcast(I32), in_=picked_s[:].bitcast(I32))
-        for r in range(1, 4):
-            nc.sync.dma_start(out=moved_s[r:P:32, :].bitcast(I32), in_=picked_s[8 * r : P : 32, :].bitcast(I32))
+        move_rows(moved_s, picked_s)
         v_s = [moved_s[:, a * S : (a + 1) * S] for a in range(2)]
         w2_rows = [held([P, 2, PASS], F32, "w2_rows%d" % v) for v in range(2)]
         for v in range(2):
             nc.sync.dma_start(out=w2_rows[v][:], in_=w2_block(0, 1)[:, 2 * v : 2 * v + 2, :])
         load_w1(1)
+
+        w1_w = {}
+
+        def order_w1_words(b, tag=None):
+            w1_w[b] = held([P, 2 * H], U8, "w1_w%d" % b, tag=tag)
+            nc.vector.tensor_copy(
+                out=w1_w[b][:].bitcast(U16).rearrange("p (a i m) -> p a i m", a=2, i=4),
+                in_=w1_w_raw[b][:].bitcast(U16).rearrange("p (a m i) -> p a i m", a=2, i=4),
+            )
+
+        v_w = [held([P, S], U32, "v_w0", tag="tab_s"), held([P, S], U32, "v_w1")]
+        nc.vector.tensor_copy(v_w[0][:], tab_w[0][:].bitcast(U32).indirect(idx[:]))
+        order_w1_words(0)
+        nc.vector.tensor_copy(v_w[1][:], tab_w[1][:].bitcast(U32).indirect(idx[:]))
+        order_w1_scales(w1_s[0][:], 0)
+        w1_s_spread = held([P, H], U8, "w1_s_spread")
+        order_w1_scales(w1_s_spread[:], 1)
+        move_rows(w1_s[1], w1_s_spread)
+
         nc.sync.dma_start(idx2[:], offs2)
         wgt = held([P, S], F32, "wgt")
         nc.sync.dma_start(out=wgt[:], in_=wgs)
@@ -137,29 +169,6 @@ def tile_list_stowage_bay_score_kernel(
             out=w3_w[:].rearrange("p (b c) -> p b c", b=2),
             in_=w3_words.rearrange("b p c i -> p b (c i)").bitcast(I32),
         )
-
-        w1_w = {}
-        w1_s = [held([P, H], U8, "w1_s%d" % b) for b in range(2)]
-
-        def order_w1_words(b, tag=None):
-            w1_w[b] = held([P, 2 * H], U8, "w1_w%d" % b, tag=tag)
-            nc.vector.tensor_copy(
-                out=w1_w[b][:].bitcast(U16).rearrange("p (a i m) -> p a i m", a=2, i=4),
-                in_=w1_w_raw[b][:].bitcast(U16).rearrange("p (a m i) -> p a i m", a=2, i=4),
-            )
-
-        def order_w1_scales(b):
-            nc.vector.tensor_copy(
-                out=w1_s[b][:].rearrange("p (a i m) -> p a i m", a=2, i=4),
-                in_=w1_s_raw[:].rearrange("p (a b m i) -> p b a i m", a=2, b=2, i=4)[:, b],
-            )
-
-        v_w = [held([P, S], U32, "v_w0", tag="tab_s"), held([P, S], U32, "v_w1")]
-        nc.vector.tensor_copy(v_w[0][:], tab_w[0][:].bitcast(U32).indirect(idx[:]))
-        order_w1_words(0)
-        nc.vector.tensor_copy(v_w[1][:], tab_w[1][:].bitcast(U32).indirect(idx[:]))
-        order_w1_scales(0)
-        order_w1_scales(1)
 
         neg_d1 = {}
 
@@ -205,7 +214,7 @@ def tile_list_stowage_bay_score_kernel(
 
         def quantize_first(a, u):
             if (a, u) == (1, 1):
-                words = placed([P, 2 * P], U32, "first_w11", 8 * UNIT)
+                words = placed([P, 2 * P], U32, "first_w11", 10 * UNIT)
             else:
                 words = held([P, 2 * P], U32, "first_w%d%d" % (a, u))
             scales = held([P, 2 * P], U8, "first_s%d%d" % (a, u))
@@ -223,7 +232,7 @@ def tile_list_stowage_bay_score_kernel(
         round_w2(w2_first[(0, 0)][:], 0, 0, 0)
         round_w2(w2_first[(0, 1)][:], 0, 0, 1)
         for s in range(4):
-            neg_d1[s] = placed([P, S], F32, "early_d1%d" % s, (8 + s) * UNIT)[:]
+            neg_d1[s] = placed([P, S], F32, "early_d1%d" % s, (10 + s) * UNIT)[:]
         first_product(0)
         first_product(1)
         quantize_first(0, 0)
@@ -328,7 +337,7 @@ def tile_list_stowage_bay_score_kernel(
         scatter(0)
         scatter(1)
 
-        pair2_span = placed([P, (5 * UNIT + 128) // 2], BF16, "pair2_span", UNIT - 64)
+        pair2_span = placed([P, (7 * UNIT + 128) // 2], BF16, "pair2_span", UNIT - 64)
         pair3_rounded = held([P, 4 * PASS], BF16, "pair3_rounded")
         w2_second = [pair2_span[:, 0 : 4 * PASS], pair3_rounded[:]]
         for u in range(2):
@@ -343,7 +352,7 @@ def tile_list_stowage_bay_score_kernel(
                 cols = [slice(P * (2 * a + e), P * (2 * a + e + 1)) for e in range(2)]
                 w2_codes[(2 + u, a)] = [(words[:, col], scales[:, col]) for col in cols]
 
-        late_d1 = [held([P, 2, S], F32, "pair2_d1"), placed([P, 2, S], F32, "pair3_d1", 6 * UNIT)]
+        late_d1 = [placed([P, 2, S], F32, "pair2_d1", 8 * UNIT), placed([P, 2, S], F32, "pair3_d1", 6 * UNIT)]
         for s in range(4, 8):
             neg_d1[s] = late_d1[s // 2 - 2][:, s % 2, :]
             first_product(s)
@@ -355,7 +364,7 @@ def tile_list_stowage_bay_score_kernel(
         scatter(3)
 
         quantize_second(1)
-        larger(2, held([P, 2, S], F32, "neg_h2", tag="pair3_rounded"))
+        larger(2, held([P, 2, S], F32, "neg_h2"))
         subtract_pair(1, "CDAB", False)
         second_products(3, "CD")
         z0 = [held([P, 4 * CH], BF16, "z0%d" % c) for c in range(NCH)]

@@ -45,11 +45,11 @@ def tile_list_stowage_bay_score_kernel(
             return psum.tile([P, 512], F32, name="bank", tag=letter)
 
         tab_s = held([P, 2 * T], U8, "tab_s")
-        w1_s_raw = [held([P, H], U8, "w1_s_raw%d" % b) for b in range(2)]
+        w1_s_raw = held([P, H], U8, "w1_s_raw")
         w3_s = held([P, 2 * N], U8, "w3_s")
         moved_s = held([P, 2 * S], U8, "moved_s")
         w1_s = [held([P, H], U8, "w1_s%d" % b) for b in range(2)]
-        for scale_tile in (tab_s, w1_s_raw[0], w1_s_raw[1], moved_s, w1_s[1], w3_s):
+        for scale_tile in (tab_s, w1_s_raw, moved_s, w1_s[1], w3_s):
             nc.vector.memset(scale_tile[:].bitcast(I32), 0)
 
         pages = [held([P, T2], F32, "page%d" % i) for i in range(PAGES)]
@@ -74,12 +74,6 @@ def tile_list_stowage_bay_score_kernel(
         def move_rows(dst, src):
             for r in range(4):
                 nc.sync.dma_start(out=dst[r:P:32, :].bitcast(I32), in_=src[8 * r + 4 : P : 32, :].bitcast(I32))
-
-        def order_w1_scales(dst, b):
-            nc.vector.tensor_copy(
-                out=dst.rearrange("p (a i m) -> p a i m", a=2, i=4),
-                in_=w1_s_raw[b][:].rearrange("p (a m i) -> p a i m", a=2, i=4),
-            )
 
         tab_w = [held([P, T], I32, "tab_w%d" % a) for a in range(2)]
 
@@ -123,8 +117,8 @@ def tile_list_stowage_bay_score_kernel(
         load_spread(tab_s, tab_scales)
         load_w1(0)
         load_table(1)
-        load_scales(w1_s_raw[0], w1_scales[:, :, 0:PASS])
-        load_spread(w1_s_raw[1], w1_scales[:, :, PASS:H])
+        load_scales(w1_s_raw, w1_scales[:, :, 0:PASS])
+        load_spread(w1_s_raw, w1_scales[:, :, PASS:H])
         load_w2(0, 0)
         picked_s = held([P, 2 * S], U8, "picked_s")
         for a in range(2):
@@ -138,21 +132,23 @@ def tile_list_stowage_bay_score_kernel(
 
         w1_w = {}
 
-        def order_w1_words(b, tag=None):
-            w1_w[b] = held([P, 2 * H], U8, "w1_w%d" % b, tag=tag)
-            nc.vector.tensor_copy(
+        def order_w1_words(b):
+            w1_w[b] = held([P, 2 * H], U8, "w1_w%d" % b)
+            nc.scalar.copy(
                 out=w1_w[b][:].bitcast(U16).rearrange("p (a i m) -> p a i m", a=2, i=4),
                 in_=w1_w_raw[b][:].bitcast(U16).rearrange("p (a m i) -> p a i m", a=2, i=4),
             )
 
-        v_w = [held([P, S], U32, "v_w0", tag="tab_s"), held([P, S], U32, "v_w1")]
+        v_w = [held([P, S], U32, "v_w0", tag="tab_s"), None]
         nc.vector.tensor_copy(v_w[0][:], tab_w[0][:].bitcast(U32).indirect(idx[:]))
         order_w1_words(0)
+        nc.vector.tensor_copy(
+            out=w1_s[0][:].rearrange("p (a i m) -> p a i m", a=2, i=4),
+            in_=w1_s_raw[:].rearrange("p (a m i) -> p a i m", a=2, i=4),
+        )
+        v_w[1] = held([P, S], U32, "v_w1", tag="w1_s_raw")
         nc.vector.tensor_copy(v_w[1][:], tab_w[1][:].bitcast(U32).indirect(idx[:]))
-        order_w1_scales(w1_s[0][:], 0)
-        w1_s_spread = held([P, H], U8, "w1_s_spread")
-        order_w1_scales(w1_s_spread[:], 1)
-        move_rows(w1_s[1], w1_s_spread)
+        move_rows(w1_s[1], w1_s[0])
 
         nc.sync.dma_start(idx2[:], offs2)
         wgt = held([P, S], F32, "wgt")
@@ -328,9 +324,9 @@ def tile_list_stowage_bay_score_kernel(
             )
 
         second_products(0, "EF")
-        order_w1_words(1, tag="w2_last0")
         larger(0, held([P, 2, S], F32, "neg_h0"))
         quantize_first(1, 1)
+        order_w1_words(1)
         first_product(2)
         first_product(3)
         second_products(1, "GH")

@@ -132,16 +132,17 @@ def tile_list_stowage_bay_score_kernel(
 
         w1_w = {}
 
-        def order_w1_words(b):
-            w1_w[b] = held([P, 2 * H], U8, "w1_w%d" % b)
-            nc.scalar.copy(
-                out=w1_w[b][:].bitcast(U16).rearrange("p (a i m) -> p a i m", a=2, i=4),
-                in_=w1_w_raw[b][:].bitcast(U16).rearrange("p (a m i) -> p a i m", a=2, i=4),
+        def order_w1_words(copy, b, a, tag=None):
+            w1_w[(b, a)] = held([P, H], U8, "w1_w%d%d" % (b, a), tag=tag)
+            copy(
+                out=w1_w[(b, a)][:].bitcast(U16).rearrange("p (i m) -> p i m", i=4),
+                in_=w1_w_raw[b][:].bitcast(U16).rearrange("p (a m i) -> p a i m", a=2, i=4)[:, a],
             )
 
         v_w = [held([P, S], U32, "v_w0", tag="tab_s"), None]
         nc.vector.tensor_copy(v_w[0][:], tab_w[0][:].bitcast(U32).indirect(idx[:]))
-        order_w1_words(0)
+        for a in range(2):
+            order_w1_words(nc.scalar.copy, 0, a)
         nc.vector.tensor_copy(
             out=w1_s[0][:].rearrange("p (a i m) -> p a i m", a=2, i=4),
             in_=w1_s_raw[:].rearrange("p (a m i) -> p a i m", a=2, i=4),
@@ -175,7 +176,7 @@ def tile_list_stowage_bay_score_kernel(
                 col = a * PASS + i * P
                 nc.tensor.matmul_mx(
                     out=d1[:],
-                    lhsT=w1_w[b][:, 2 * col : 2 * (col + P)].bitcast(FP4X4),
+                    lhsT=w1_w[(b, a)][:, 2 * i * P : 2 * (i + 1) * P].bitcast(FP4X4),
                     lhsT_scale=w1_s[b][:, col : col + P],
                     rhs=v_w[a][:].bitcast(FP8X4),
                     rhs_scale=v_s[a],
@@ -203,14 +204,11 @@ def tile_list_stowage_bay_score_kernel(
                     nc.vector.tensor_copy(out=dst, in_=src[:, :, e, :])
                 return
             dst = w2_first[(1, u)][:].rearrange("p (e m j) -> p m e j", e=2, j=4)[:, :, :, 2 * v : 2 * v + 2]
-            if v == 1:
-                nc.scalar.activation(dst, src, ACT.Copy)
-            else:
-                nc.vector.tensor_copy(out=dst, in_=src)
+            nc.scalar.activation(dst, src, ACT.Copy)
 
         def quantize_first(a, u):
             if (a, u) == (1, 1):
-                words = placed([P, 2 * P], U32, "first_w11", 10 * UNIT)
+                words = placed([P, 2 * P], U32, "first_w11", 11 * UNIT)
             else:
                 words = held([P, 2 * P], U32, "first_w%d%d" % (a, u))
             scales = held([P, 2 * P], U8, "first_s%d%d" % (a, u))
@@ -226,15 +224,18 @@ def tile_list_stowage_bay_score_kernel(
                 w2_codes[(0, 1)].append((words[:], scales[:]))
 
         round_w2(w2_first[(0, 0)][:], 0, 0, 0)
-        round_w2(w2_first[(0, 1)][:], 0, 0, 1)
+        nc.vector.tensor_copy(
+            out=w2_first[(0, 1)][:].rearrange("p (e m j) -> p m j e", e=2, j=4),
+            in_=w2_raw[(0, 0)][:].rearrange("p j (m i) -> p m j i", i=4)[:, :, :, 2:4],
+        )
         for s in range(4):
             neg_d1[s] = placed([P, S], F32, "early_d1%d" % s, (10 + s) * UNIT)[:]
         first_product(0)
         first_product(1)
-        quantize_first(0, 0)
-        round_w2_rows(0, 0)
-        round_w2_rows(0, 1)
         quantize_first(0, 1)
+        round_w2_rows(0, 0)
+        quantize_first(0, 0)
+        round_w2_rows(0, 1)
         round_w2_rows(1, 0)
         quantize_last()
         round_w2_rows(1, 1)
@@ -324,13 +325,13 @@ def tile_list_stowage_bay_score_kernel(
             )
 
         second_products(0, "EF")
+        order_w1_words(nc.vector.tensor_copy, 1, 0, tag="w2_last0")
         larger(0, held([P, 2, S], F32, "neg_h0"))
+        scatter(0)
         quantize_first(1, 1)
-        order_w1_words(1)
         first_product(2)
         first_product(3)
         second_products(1, "GH")
-        scatter(0)
         scatter(1)
 
         pair2_span = placed([P, (7 * UNIT + 128) // 2], BF16, "pair2_span", UNIT - 64)
@@ -339,6 +340,7 @@ def tile_list_stowage_bay_score_kernel(
         for u in range(2):
             for a in range(2):
                 round_w2(w2_second[u][:, 2 * PASS * a : 2 * PASS * (a + 1)], 1, a, u)
+        order_w1_words(nc.scalar.copy, 1, 1, tag="w2_raw11")
 
         def quantize_second(u):
             words = held([P, PASS], U32, "second_w%d" % u)

@@ -94,8 +94,8 @@ def tile_list_stowage_bay_score_kernel(
         w2_raw = {}
 
         def load_w2(b, a):
-            if (b, a) == (0, 0):
-                w2_raw[(b, a)] = placed([P, 4, PASS], F32, "w2_raw00", 10 * UNIT)
+            if a == 0:
+                w2_raw[(b, a)] = placed([P, 4, PASS], F32, "w2_raw%d0" % b, (10 + 4 * b) * UNIT)
             else:
                 w2_raw[(b, a)] = held([P, 4, PASS], F32, "w2_raw%d%d" % (b, a))
             nc.sync.dma_start(out=w2_raw[(b, a)][:], in_=w2_block(b, a))
@@ -171,7 +171,7 @@ def tile_list_stowage_bay_score_kernel(
 
         def first_product(s):
             b, i = divmod(s, 4)
-            d1 = bank(("GH" if s < 2 else "EF")[s % 2])
+            d1 = bank("GHEFEFGH"[s])
             for a in range(2):
                 col = a * PASS + i * P
                 nc.tensor.matmul_mx(
@@ -246,18 +246,18 @@ def tile_list_stowage_bay_score_kernel(
             for e in range(2):
                 d2[2 * k + e] = bank(letters[e])
             passes = (1, 0) if k == 1 else (0, 1)
-            for a in passes:
-                for e in range(2):
-                    words, scales = w2_codes[(k, a)][e]
-                    nc.tensor.matmul_mx(
-                        out=d2[2 * k + e][:],
-                        lhsT=words.bitcast(FP8X4),
-                        lhsT_scale=scales,
-                        rhs=v_w[a][:].bitcast(FP8X4),
-                        rhs_scale=v_s[a],
-                        start=(a == passes[0]),
-                        stop=(a == passes[1]),
-                    )
+            order = [(a, e) for a in passes for e in range(2)] if k == 0 else [(a, e) for e in range(2) for a in passes]
+            for a, e in order:
+                words, scales = w2_codes[(k, a)][e]
+                nc.tensor.matmul_mx(
+                    out=d2[2 * k + e][:],
+                    lhsT=words.bitcast(FP8X4),
+                    lhsT_scale=scales,
+                    rhs=v_w[a][:].bitcast(FP8X4),
+                    rhs_scale=v_s[a],
+                    start=(a == passes[0]),
+                    stop=(a == passes[1]),
+                )
 
         neg_h = {}
 
@@ -269,8 +269,17 @@ def tile_list_stowage_bay_score_kernel(
                     out=neg_h[s], in0=d2[s][:], scalar=-1.0, in1=neg_d1[s], op0=ALU.mult, op1=ALU.min
                 )
 
-        def scatter(s):
+        def scatter_fused(s):
             nc.vector.tensor_tensor(pages[s % PAGES][:].indirect(idx2[:]), neg_h[s], wgt[:], ALU.mult)
+
+        weighted = {}
+
+        def weigh(s, tag=None):
+            weighted[s] = held([P, S], F32, "weighted%d" % s, tag=tag)
+            nc.gpsimd.tensor_tensor(weighted[s][:], neg_h[s], wgt[:], ALU.mult)
+
+        def scatter(s):
+            nc.vector.tensor_copy(pages[s % PAGES][:].indirect(idx2[:]), weighted[s][:])
 
         z_t = [placed([P, 512], F32, "z_t%d" % c, (2 + c) * UNIT) for c in range(NCH)]
 
@@ -325,55 +334,75 @@ def tile_list_stowage_bay_score_kernel(
             )
 
         second_products(0, "EF")
-        order_w1_words(nc.vector.tensor_copy, 1, 0, tag="w2_last0")
+        for a in range(2):
+            order_w1_words(nc.vector.tensor_copy, 1, a, tag="w2_last%d" % a)
         larger(0, held([P, 2, S], F32, "neg_h0"))
-        scatter(0)
+        scatter_fused(0)
         quantize_first(1, 1)
         first_product(2)
         first_product(3)
         second_products(1, "GH")
-        scatter(1)
+        scatter_fused(1)
 
-        pair2_span = placed([P, (7 * UNIT + 128) // 2], BF16, "pair2_span", UNIT - 64)
+        pair2_span = placed([P, 4 * PASS], BF16, "pair2_span", UNIT - 64)
         pair3_rounded = held([P, 4 * PASS], BF16, "pair3_rounded")
         w2_second = [pair2_span[:, 0 : 4 * PASS], pair3_rounded[:]]
         for u in range(2):
             for a in range(2):
                 round_w2(w2_second[u][:, 2 * PASS * a : 2 * PASS * (a + 1)], 1, a, u)
-        order_w1_words(nc.scalar.copy, 1, 1, tag="w2_raw11")
 
         def quantize_second(u):
-            words = held([P, PASS], U32, "second_w%d" % u)
+            if u == 0:
+                words = held([P, PASS], U32, "second_w0")
+            else:
+                words = placed([P, PASS], U32, "second_w1", 15 * UNIT)
             scales = held([P, PASS], U8, "second_s%d" % u)
             nc.vector.quantize_mx(out=words[:].bitcast(FP8X4), scales=scales[:], in_=w2_second[u])
             for a in range(2):
                 cols = [slice(P * (2 * a + e), P * (2 * a + e + 1)) for e in range(2)]
                 w2_codes[(2 + u, a)] = [(words[:, col], scales[:, col]) for col in cols]
 
-        late_d1 = [placed([P, 2, S], F32, "pair2_d1", 8 * UNIT), placed([P, 2, S], F32, "pair3_d1", 6 * UNIT)]
         for s in range(4, 8):
-            neg_d1[s] = late_d1[s // 2 - 2][:, s % 2, :]
-            first_product(s)
+            neg_d1[s] = placed([P, S], F32, "late_d1%d" % s, (s + 10) * UNIT)[:]
+        first_product(4)
+        first_product(5)
         quantize_second(0)
         larger(1, placed([P, 2, S], F32, "neg_h1", 0))
         second_products(2, "EF")
+        larger(2, held([P, 2, S], F32, "neg_h2"))
+        for s in range(2, 5):
+            weigh(s)
+        first_product(6)
+        first_product(7)
         subtract_pair(0, "CDAB", True)
         scatter(2)
+        quantize_second(1)
+        weigh(5, tag="pair3_rounded")
         scatter(3)
 
-        quantize_second(1)
-        larger(2, held([P, 2, S], F32, "neg_h2"))
+        second_products(3, "GH")
+        gap = {}
+        for s in range(6, 8):
+            neg_d2 = held([P, S], F32, "neg_d2%d" % s)
+            nc.scalar.activation(neg_d2[:], d2[s][:], ACT.Copy, scale=-1.0)
+            gap[s] = held([P, S], F32, "gap%d" % s)
+            nc.gpsimd.tensor_tensor(gap[s][:], neg_d1[s], neg_d2[:], ALU.subtract)
+        for s in range(6, 8):
+            excess = held([P, S], F32, "excess%d" % s, tag="neg_d2%d" % s)
+            nc.scalar.activation(excess[:], gap[s][:], ACT.Relu)
+            neg_h[s] = held([P, S], F32, "neg_h%d" % s, tag="gap%d" % s)[:]
+            nc.gpsimd.tensor_tensor(neg_h[s], neg_d1[s], excess[:], ALU.subtract)
+            weigh(s)
         subtract_pair(1, "CDAB", False)
-        second_products(3, "CD")
         z0 = [held([P, 4 * CH], BF16, "z0%d" % c) for c in range(NCH)]
         for c in range(NCH):
-            acc = bank("EF"[c % 2])
+            acc = bank("AB"[c % 2])
             for u in range(2):
                 turn_back(acc, c, u)
             empty_turned(acc, 0, CH, z0[c][:])
         scatter(4)
         scatter(5)
-        subtract_pair(2, "GHAB", False)
+        subtract_pair(2, "EFGH", False)
         z0_codes = {}
 
         def quantize_z0(c, tag=None, offset=None):
@@ -385,7 +414,6 @@ def tile_list_stowage_bay_score_kernel(
             nc.vector.quantize_mx(out=words[:].bitcast(FP8X4), scales=scales[:], in_=z0[c][:])
             z0_codes[c] = (words, scales)
 
-        larger(3, held([P, 2, S], F32, "neg_h3"))
 
         y = {}
 
@@ -409,13 +437,13 @@ def tile_list_stowage_bay_score_kernel(
                 score(0, c, n, 0, CH, words[:], scales[:], n % 2 == 0, False)
 
         scatter(6)
-        quantize_z0(0, offset=7 * UNIT)
+        quantize_z0(0, tag="gap7")
 
-        six = [bank(letter) for letter in "EFCD"]
+        six = [bank(letter) for letter in "ABCD"]
         blocks = T2 // P
         for blk in range(blocks):
             turn(six[blk // 2], blk % 2, lim_t[3][:, 0, blk * P : (blk + 1) * P], blk % 2 == 0, False)
-        back = [bank(letter) for letter in "GHAB"]
+        back = [bank(letter) for letter in "EFGH"]
         for c in range(NCH):
             turn_back(back[c], c, 0)
         for blk in range(blocks):
@@ -439,7 +467,7 @@ def tile_list_stowage_bay_score_kernel(
                 round_six(2)
                 round_six(3)
         scatter(7)
-        first_score(0, "EF")
+        first_score(0, "AB")
 
         for c in range(NCH):
             for h in range(2):
@@ -461,7 +489,7 @@ def tile_list_stowage_bay_score_kernel(
                 score(1, c, n, 0, CH, z1_w[:], z1_s[:], False, n == 3)
             if c + 1 < NCH:
                 quantize_z0(c + 1, tag="z1_%d0" % c)
-                first_score(c + 1, ("CD", "GH", "AB")[c])
+                first_score(c + 1, ("CD", "EF", "GH")[c])
             if c < 2:
                 z1[(NCH - 1, c)] = held([P, 4 * P], BF16, "z1_last%d" % c, tag="z1_%d1" % c)
                 empty_turned(back[NCH - 1], c * P, (c + 1) * P, z1[(NCH - 1, c)][:])

@@ -157,9 +157,9 @@ def tile_list_stowage_bay_score_kernel(
         load_w2(1, 0)
         load_w2(1, 1)
         load_lim(0)
+        load_lim(2)
         load_lim(1)
         load_scales(w3_s, w3_scales)
-        load_lim(2)
         load_lim(3)
         w3_w = held([P, 2 * N], I32, "w3_w")
         nc.sync.dma_start(
@@ -261,21 +261,26 @@ def tile_list_stowage_bay_score_kernel(
 
         neg_h = {}
 
+        def larger_one(s, dst):
+            neg_h[s] = dst
+            nc.vector.scalar_tensor_tensor(
+                out=neg_h[s], in0=d2[s][:], scalar=-1.0, in1=neg_d1[s], op0=ALU.mult, op1=ALU.min
+            )
+
         def larger(k, both):
             for e in range(2):
-                s = 2 * k + e
-                neg_h[s] = both[:, e, :]
-                nc.vector.scalar_tensor_tensor(
-                    out=neg_h[s], in0=d2[s][:], scalar=-1.0, in1=neg_d1[s], op0=ALU.mult, op1=ALU.min
-                )
+                larger_one(2 * k + e, both[:, e, :])
 
         def scatter_fused(s):
             nc.vector.tensor_tensor(pages[s % PAGES][:].indirect(idx2[:]), neg_h[s], wgt[:], ALU.mult)
 
         weighted = {}
 
-        def weigh(s, tag=None):
-            weighted[s] = held([P, S], F32, "weighted%d" % s, tag=tag)
+        def weigh(s):
+            if s == 4:
+                weighted[s] = placed([P, S], F32, "weighted%d" % s, (14 + s) * UNIT)
+            else:
+                weighted[s] = held([P, S], F32, "weighted%d" % s)
             nc.gpsimd.tensor_tensor(weighted[s][:], neg_h[s], wgt[:], ALU.mult)
 
         def scatter(s):
@@ -291,35 +296,27 @@ def tile_list_stowage_bay_score_kernel(
                 out=acc[:, slot * P : (slot + 1) * P], lhsT=src, rhs=ident[:], is_transpose=True, start=start, stop=stop
             )
 
-        def subtract_pair(k, letters, pages_first):
-            acc = [bank(letter) for letter in letters]
+        sums = {}
 
-            def turn_limits(opens):
-                for c in range(NCH):
-                    for slot in range(4):
-                        mb, e = divmod(slot, 2)
-                        m0 = c * CH + mb * P
-                        src = lim_t[k][:, e, m0 : m0 + P]
-                        turn(acc[c], slot, src, opens and slot == 0, not opens and slot == 3)
+        def turn_limits(k, opens):
+            for c in range(NCH):
+                for slot in range(4):
+                    mb, e = divmod(slot, 2)
+                    m0 = c * CH + mb * P
+                    turn(sums[k][c], slot, lim_t[k][:, e, m0 : m0 + P], opens and slot == 0, False)
 
-            def turn_pages(opens):
-                for e in range(2):
-                    for c in range(NCH):
-                        for mb in range(2):
-                            slot = 2 * mb + e
-                            m0 = c * CH + mb * P
-                            src = pages[(2 * k + e) % PAGES][:, m0 : m0 + P]
-                            turn(acc[c], slot, src, opens and slot == 0, not opens and slot == 3)
+        def turn_page(s, opens):
+            k, e = divmod(s, 2)
+            for c in range(NCH):
+                for mb in range(2):
+                    slot = 2 * mb + e
+                    m0 = c * CH + mb * P
+                    turn(sums[k][c], slot, pages[s % PAGES][:, m0 : m0 + P], opens and slot == 0, slot == 3)
 
-            if pages_first:
-                turn_pages(True)
-                turn_limits(False)
-            else:
-                turn_limits(True)
-                turn_pages(False)
+        def round_pair(k):
             for c in range(NCH):
                 nc.scalar.copy(
-                    out=z_t_pairs(c)[:, :, k % 2], in_=acc[c][:].rearrange("m (mb e q) -> m mb q e", mb=2, e=2)
+                    out=z_t_pairs(c)[:, :, k % 2], in_=sums[k][c][:].rearrange("m (mb e q) -> m mb q e", mb=2, e=2)
                 )
 
         def turn_back(acc, c, u):
@@ -345,7 +342,7 @@ def tile_list_stowage_bay_score_kernel(
         scatter_fused(1)
 
         pair2_span = placed([P, 4 * PASS], BF16, "pair2_span", UNIT - 64)
-        pair3_rounded = held([P, 4 * PASS], BF16, "pair3_rounded")
+        pair3_rounded = placed([P, 4 * PASS], BF16, "pair3_rounded", 18 * UNIT)
         w2_second = [pair2_span[:, 0 : 4 * PASS], pair3_rounded[:]]
         for u in range(2):
             for a in range(2):
@@ -355,7 +352,7 @@ def tile_list_stowage_bay_score_kernel(
             if u == 0:
                 words = held([P, PASS], U32, "second_w0")
             else:
-                words = placed([P, PASS], U32, "second_w1", 15 * UNIT)
+                words = placed([P, PASS], U32, "second_w1", 14 * UNIT)
             scales = held([P, PASS], U8, "second_s%d" % u)
             nc.vector.quantize_mx(out=words[:].bitcast(FP8X4), scales=scales[:], in_=w2_second[u])
             for a in range(2):
@@ -369,15 +366,25 @@ def tile_list_stowage_bay_score_kernel(
         quantize_second(0)
         larger(1, placed([P, 2, S], F32, "neg_h1", 0))
         second_products(2, "EF")
-        larger(2, held([P, 2, S], F32, "neg_h2"))
-        for s in range(2, 5):
-            weigh(s)
+        larger_one(4, held([P, S], F32, "neg_h4")[:])
+        halves = [held([P, S // 2], F32, "weighted2%d" % h) for h in range(2)]
+        for h in range(2):
+            cols = slice(h * S // 2, (h + 1) * S // 2)
+            nc.gpsimd.tensor_tensor(halves[h][:], neg_h[2][:, cols], wgt[:, cols], ALU.mult)
+        weigh(3)
         first_product(6)
         first_product(7)
-        subtract_pair(0, "CDAB", True)
-        scatter(2)
+        sums[0] = [bank(letter) for letter in "CDAB"]
+        turn_page(0, True)
+        turn_limits(0, False)
+        turn_page(1, False)
+        round_pair(0)
+        for h in range(2):
+            nc.vector.tensor_copy(pages[2][:].indirect(idx2[:, 16 * h : 16 * (h + 1)]), halves[h][:])
         quantize_second(1)
-        weigh(5, tag="pair3_rounded")
+        weigh(4)
+        larger_one(5, placed([P, S], F32, "neg_h5", 19 * UNIT)[:])
+        weigh(5)
         scatter(3)
 
         second_products(3, "GH")
@@ -393,16 +400,23 @@ def tile_list_stowage_bay_score_kernel(
             neg_h[s] = held([P, S], F32, "neg_h%d" % s, tag="gap%d" % s)[:]
             nc.gpsimd.tensor_tensor(neg_h[s], neg_d1[s], excess[:], ALU.subtract)
             weigh(s)
-        subtract_pair(1, "CDAB", False)
+        for k, letters in ((1, "CDAB"), (2, "EFGH")):
+            sums[k] = [bank(letter) for letter in letters]
+            turn_limits(k, True)
+        turn_page(2, False)
+        turn_page(3, False)
+        round_pair(1)
         z0 = [held([P, 4 * CH], BF16, "z0%d" % c) for c in range(NCH)]
         for c in range(NCH):
-            acc = bank("AB"[c % 2])
+            acc = bank("CD"[c % 2])
             for u in range(2):
                 turn_back(acc, c, u)
             empty_turned(acc, 0, CH, z0[c][:])
         scatter(4)
         scatter(5)
-        subtract_pair(2, "EFGH", False)
+        turn_page(4, False)
+        turn_page(5, False)
+        round_pair(2)
         z0_codes = {}
 
         def quantize_z0(c, tag=None, offset=None):

@@ -21,6 +21,8 @@ P = 128
 PASS = 512
 CH = 256
 NCH = T2 // CH
+FIRST_PART = 320
+PAGE_OF = (0, 1, 2, 0, 1, 0, 2, 1)
 PAGES = 3
 UNIT = 2048
 
@@ -104,7 +106,10 @@ def tile_list_stowage_bay_score_kernel(
 
         def load_lim(k):
             b, u = divmod(k, 2)
-            lim_t[k] = held([P, 2, T2], F32, "lim%d" % k)
+            if k == 0:
+                lim_t[k] = placed([P, 2, T2], F32, "lim0", 22 * UNIT)
+            else:
+                lim_t[k] = held([P, 2, T2], F32, "lim%d" % k)
             nc.sync.dma_start(
                 out=lim_t[k][:],
                 in_=lim[PASS * b : PASS * (b + 1), :].rearrange("(p i) m -> p i m", i=4)[:, 2 * u : 2 * u + 2, :],
@@ -157,8 +162,8 @@ def tile_list_stowage_bay_score_kernel(
         load_w2(1, 0)
         load_w2(1, 1)
         load_lim(0)
-        load_lim(2)
         load_lim(1)
+        load_lim(2)
         load_scales(w3_s, w3_scales)
         load_lim(3)
         w3_w = held([P, 2 * N], I32, "w3_w")
@@ -187,7 +192,7 @@ def tile_list_stowage_bay_score_kernel(
 
         def round_w2(dst, b, a, u):
             nc.scalar.activation(
-                dst.rearrange("p (e m j) -> p m j e", e=2, j=4),
+                dst,
                 w2_raw[(b, a)][:].rearrange("p j (m i) -> p m j i", i=4)[:, :, :, 2 * u : 2 * u + 2],
                 ACT.Copy,
             )
@@ -223,7 +228,7 @@ def tile_list_stowage_bay_score_kernel(
                 nc.vector.quantize_mx(out=words[:].bitcast(FP8X4), scales=scales[:], in_=w2_last[e][:])
                 w2_codes[(0, 1)].append((words[:], scales[:]))
 
-        round_w2(w2_first[(0, 0)][:], 0, 0, 0)
+        round_w2(w2_first[(0, 0)][:].rearrange("p (e m j) -> p m j e", e=2, j=4), 0, 0, 0)
         nc.vector.tensor_copy(
             out=w2_first[(0, 1)][:].rearrange("p (e m j) -> p m j e", e=2, j=4),
             in_=w2_raw[(0, 0)][:].rearrange("p j (m i) -> p m j i", i=4)[:, :, :, 2:4],
@@ -272,24 +277,28 @@ def tile_list_stowage_bay_score_kernel(
                 larger_one(2 * k + e, both[:, e, :])
 
         def scatter_fused(s):
-            nc.vector.tensor_tensor(pages[s % PAGES][:].indirect(idx2[:]), neg_h[s], wgt[:], ALU.mult)
+            nc.vector.tensor_tensor(pages[PAGE_OF[s]][:].indirect(idx2[:]), neg_h[s], wgt[:], ALU.mult)
 
         weighted = {}
 
-        def weigh(s):
-            if s == 4:
-                weighted[s] = placed([P, S], F32, "weighted%d" % s, (14 + s) * UNIT)
+        def weigh(s, offset=None):
+            if offset:
+                weighted[s] = placed([P, S], F32, "weighted%d" % s, offset)
             else:
                 weighted[s] = held([P, S], F32, "weighted%d" % s)
             nc.gpsimd.tensor_tensor(weighted[s][:], neg_h[s], wgt[:], ALU.mult)
 
         def scatter(s):
-            nc.vector.tensor_copy(pages[s % PAGES][:].indirect(idx2[:]), weighted[s][:])
+            nc.vector.tensor_copy(pages[PAGE_OF[s]][:].indirect(idx2[:]), weighted[s][:])
 
-        z_t = [placed([P, 512], F32, "z_t%d" % c, (2 + c) * UNIT) for c in range(NCH)]
+        z_t = {}
 
-        def z_t_pairs(c):
-            return z_t[c][:].bitcast(BF16).rearrange("m (mb u q e) -> m mb u q e", mb=2, u=2, e=2)
+        def place_z_t(u, unit):
+            for c in range(NCH):
+                z_t[(u, c)] = placed([P, CH], F32, "z_t%d%d" % (unit, c), unit * UNIT + c * UNIT // 2)
+
+        def z_t_pairs(u, c):
+            return z_t[(u, c)][:].bitcast(BF16).rearrange("m (mb q e) -> m mb q e", mb=2, e=2)
 
         def turn(acc, slot, src, start, stop):
             nc.tensor.matmul(
@@ -305,24 +314,25 @@ def tile_list_stowage_bay_score_kernel(
                     m0 = c * CH + mb * P
                     turn(sums[k][c], slot, lim_t[k][:, e, m0 : m0 + P], opens and slot == 0, False)
 
-        def turn_page(s, opens):
+        def turn_page(s, opens, closes):
             k, e = divmod(s, 2)
             for c in range(NCH):
                 for mb in range(2):
                     slot = 2 * mb + e
                     m0 = c * CH + mb * P
-                    turn(sums[k][c], slot, pages[s % PAGES][:, m0 : m0 + P], opens and slot == 0, slot == 3)
+                    turn(sums[k][c], slot, pages[PAGE_OF[s]][:, m0 : m0 + P], opens and slot == 0, closes and mb == 1)
 
         def round_pair(k):
             for c in range(NCH):
                 nc.scalar.copy(
-                    out=z_t_pairs(c)[:, :, k % 2], in_=sums[k][c][:].rearrange("m (mb e q) -> m mb q e", mb=2, e=2)
+                    out=z_t_pairs(k % 2, c), in_=sums[k][c][:].rearrange("m (mb e q) -> m mb q e", mb=2, e=2)
                 )
 
         def turn_back(acc, c, u):
             for mb in range(2):
-                w0 = (2 * mb + u) * P
-                nc.tensor.transpose(acc[:, u * CH + mb * P : u * CH + (mb + 1) * P], z_t[c][:, w0 : w0 + P], ident[:])
+                nc.tensor.transpose(
+                    acc[:, u * CH + mb * P : u * CH + (mb + 1) * P], z_t[(u, c)][:, mb * P : (mb + 1) * P], ident[:]
+                )
 
         def empty_turned(acc, m0, m1, dst):
             nc.scalar.copy(
@@ -342,21 +352,27 @@ def tile_list_stowage_bay_score_kernel(
         scatter_fused(1)
 
         pair2_span = placed([P, 4 * PASS], BF16, "pair2_span", UNIT - 64)
-        pair3_rounded = placed([P, 4 * PASS], BF16, "pair3_rounded", 18 * UNIT)
-        w2_second = [pair2_span[:, 0 : 4 * PASS], pair3_rounded[:]]
+        pair3_span = placed([P, 8 * PASS], BF16, "pair3_span", 18 * UNIT)
+        w2_second = [pair2_span[:, 0 : 4 * PASS], pair3_span[:, 0 : 4 * PASS]]
         for u in range(2):
             for a in range(2):
-                round_w2(w2_second[u][:, 2 * PASS * a : 2 * PASS * (a + 1)], 1, a, u)
+                round_w2(w2_second[u].rearrange("p (e a m j) -> p a m j e", e=2, a=2, j=4)[:, a], 1, a, u)
 
         def quantize_second(u):
             if u == 0:
-                words = held([P, PASS], U32, "second_w0")
+                words = held([P, PASS], U32, "second_w0")[:]
+                scales = held([P, PASS], U8, "second_s0")
             else:
-                words = placed([P, PASS], U32, "second_w1", 14 * UNIT)
-            scales = held([P, PASS], U8, "second_s%d" % u)
-            nc.vector.quantize_mx(out=words[:].bitcast(FP8X4), scales=scales[:], in_=w2_second[u])
+                words = placed([P, PASS + 32], U32, "second_w1", 2 * UNIT + UNIT // 2 - 64)[:, 0:PASS]
+                scales = placed([P, PASS], U8, "second_s1", 13 * UNIT)
+            parts = 2 - u
+            for part in range(parts):
+                lo, hi = part * PASS // parts, (part + 1) * PASS // parts
+                nc.vector.quantize_mx(
+                    out=words[:, lo:hi].bitcast(FP8X4), scales=scales[:, lo:hi], in_=w2_second[u][:, 4 * lo : 4 * hi]
+                )
             for a in range(2):
-                cols = [slice(P * (2 * a + e), P * (2 * a + e + 1)) for e in range(2)]
+                cols = [slice(P * (2 * e + a), P * (2 * e + a + 1)) for e in range(2)]
                 w2_codes[(2 + u, a)] = [(words[:, col], scales[:, col]) for col in cols]
 
         for s in range(4, 8):
@@ -366,56 +382,79 @@ def tile_list_stowage_bay_score_kernel(
         quantize_second(0)
         larger(1, placed([P, 2, S], F32, "neg_h1", 0))
         second_products(2, "EF")
-        larger_one(4, held([P, S], F32, "neg_h4")[:])
-        halves = [held([P, S // 2], F32, "weighted2%d" % h) for h in range(2)]
-        for h in range(2):
-            cols = slice(h * S // 2, (h + 1) * S // 2)
-            nc.gpsimd.tensor_tensor(halves[h][:], neg_h[2][:, cols], wgt[:, cols], ALU.mult)
-        weigh(3)
+        larger_one(4, placed([P, S], F32, "neg_h4", 4 * UNIT + UNIT // 2)[:])
+        first_part = held([P, FIRST_PART], F32, "first_part", tag="w2_raw11")
+        nc.gpsimd.tensor_tensor(first_part[:], neg_h[2][:, 0:FIRST_PART], wgt[:, 0:FIRST_PART], ALU.mult)
+        quantize_second(1)
         first_product(6)
         first_product(7)
-        sums[0] = [bank(letter) for letter in "CDAB"]
-        turn_page(0, True)
-        turn_limits(0, False)
-        turn_page(1, False)
-        round_pair(0)
-        for h in range(2):
-            nc.vector.tensor_copy(pages[2][:].indirect(idx2[:, 16 * h : 16 * (h + 1)]), halves[h][:])
-        quantize_second(1)
-        weigh(4)
-        larger_one(5, placed([P, S], F32, "neg_h5", 19 * UNIT)[:])
-        weigh(5)
-        scatter(3)
 
+        neg_d2, gap, excess = {}, {}, {}
+
+        def empty_second(s):
+            neg_d2[s] = held([P, S], F32, "neg_d2%d" % s)
+            nc.scalar.activation(neg_d2[s][:], d2[s][:], ACT.Copy, scale=-1.0)
+
+        def take_gap(s, dst):
+            gap[s] = dst
+            nc.gpsimd.tensor_tensor(gap[s], neg_d1[s], neg_d2[s][:], ALU.subtract)
+
+        def take_excess(s, dst):
+            excess[s] = dst
+            nc.scalar.activation(excess[s][:], gap[s], ACT.Relu)
+
+        def take_larger(s, dst):
+            neg_h[s] = dst[:]
+            nc.gpsimd.tensor_tensor(neg_h[s], neg_d1[s], excess[s][:], ALU.subtract)
+
+        empty_second(5)
         second_products(3, "GH")
-        gap = {}
-        for s in range(6, 8):
-            neg_d2 = held([P, S], F32, "neg_d2%d" % s)
-            nc.scalar.activation(neg_d2[:], d2[s][:], ACT.Copy, scale=-1.0)
-            gap[s] = held([P, S], F32, "gap%d" % s)
-            nc.gpsimd.tensor_tensor(gap[s][:], neg_d1[s], neg_d2[:], ALU.subtract)
-        for s in range(6, 8):
-            excess = held([P, S], F32, "excess%d" % s, tag="neg_d2%d" % s)
-            nc.scalar.activation(excess[:], gap[s][:], ACT.Relu)
-            neg_h[s] = held([P, S], F32, "neg_h%d" % s, tag="gap%d" % s)[:]
-            nc.gpsimd.tensor_tensor(neg_h[s], neg_d1[s], excess[:], ALU.subtract)
-            weigh(s)
-        for k, letters in ((1, "CDAB"), (2, "EFGH")):
+        empty_second(6)
+        empty_second(7)
+        nc.vector.tensor_copy(pages[2][:].indirect(idx2[:, 0 : FIRST_PART // 16]), first_part[:])
+        weigh(3, 18 * UNIT)
+        take_gap(5, placed([P, S], F32, "gap5", 19 * UNIT + UNIT // 2)[:])
+        take_excess(5, held([P, S], F32, "excess5", tag="neg_d25"))
+        last_part = placed([P, S - FIRST_PART], F32, "last_part", 19 * UNIT)
+        nc.gpsimd.tensor_tensor(last_part[:], neg_h[2][:, FIRST_PART:S], wgt[:, FIRST_PART:S], ALU.mult)
+        place_z_t(0, 2)
+        sums[0] = [bank(letter) for letter in "CDAB"]
+        turn_page(0, True, False)
+        turn_limits(0, False)
+        turn_page(1, False, True)
+        weigh(4, 21 * UNIT + UNIT // 2)
+        round_pair(0)
+        scatter(3)
+        nc.vector.tensor_copy(pages[2][:].indirect(idx2[:, FIRST_PART // 16 : S // 16]), last_part[:])
+        gap6_span = placed([P, S + 32], F32, "gap6_span", 4 * UNIT + UNIT // 2 - 64)
+        take_gap(6, gap6_span[:, 0:S])
+        take_excess(6, placed([P, S], F32, "excess6", 8 * UNIT + UNIT // 2))
+        place_z_t(1, 4)
+        take_larger(5, placed([P, S], F32, "neg_h5", 23 * UNIT))
+        weigh(5)
+        take_larger(6, held([P, S], F32, "neg_h6"))
+        weigh(6)
+        gap7_span = placed([P, S + 32], F32, "gap7_span", 8 * UNIT + UNIT // 2 - 64)
+        take_gap(7, gap7_span[:, 0:S])
+        for k, letters in ((1, "EFGH"), (2, "CDAB")):
             sums[k] = [bank(letter) for letter in letters]
             turn_limits(k, True)
-        turn_page(2, False)
-        turn_page(3, False)
+        turn_page(3, False, False)
+        turn_page(2, False, True)
         round_pair(1)
         z0 = [held([P, 4 * CH], BF16, "z0%d" % c) for c in range(NCH)]
         for c in range(NCH):
-            acc = bank("CD"[c % 2])
+            acc = bank("EF"[c % 2])
             for u in range(2):
                 turn_back(acc, c, u)
             empty_turned(acc, 0, CH, z0[c][:])
+        take_excess(7, placed([P, S], F32, "excess7", 3 * UNIT))
+        take_larger(7, held([P, S], F32, "neg_h7"))
+        place_z_t(0, 8)
         scatter(4)
         scatter(5)
-        turn_page(4, False)
-        turn_page(5, False)
+        turn_page(4, False, False)
+        turn_page(5, False, True)
         round_pair(2)
         z0_codes = {}
 
@@ -451,21 +490,21 @@ def tile_list_stowage_bay_score_kernel(
                 score(0, c, n, 0, CH, words[:], scales[:], n % 2 == 0, False)
 
         scatter(6)
-        quantize_z0(0, tag="gap7")
+        quantize_z0(0, offset=3 * UNIT)
 
-        six = [bank(letter) for letter in "ABCD"]
+        six = [bank(letter) for letter in "GHEF"]
         blocks = T2 // P
         for blk in range(blocks):
             turn(six[blk // 2], blk % 2, lim_t[3][:, 0, blk * P : (blk + 1) * P], blk % 2 == 0, False)
-        back = [bank(letter) for letter in "EFGH"]
+        back = [bank(letter) for letter in "CDAB"]
         for c in range(NCH):
             turn_back(back[c], c, 0)
         for blk in range(blocks):
-            turn(six[blk // 2], blk % 2, pages[6 % PAGES][:, blk * P : (blk + 1) * P], False, blk % 2 == 1)
+            turn(six[blk // 2], blk % 2, pages[PAGE_OF[6]][:, blk * P : (blk + 1) * P], False, blk % 2 == 1)
 
         def round_six(c):
             nc.scalar.copy(
-                out=z_t_pairs(c)[:, :, 1, :, 0],
+                out=z_t_pairs(1, c)[:, :, :, 0],
                 in_=six[c][:, 0:CH].rearrange("m (mb q) -> m mb q", mb=2),
             )
 
@@ -480,8 +519,8 @@ def tile_list_stowage_bay_score_kernel(
             if c == 0:
                 round_six(2)
                 round_six(3)
-        scatter(7)
-        first_score(0, "AB")
+        scatter_fused(7)
+        first_score(0, "GH")
 
         for c in range(NCH):
             for h in range(2):
@@ -489,7 +528,7 @@ def tile_list_stowage_bay_score_kernel(
                 nc.vector.tensor_tensor(
                     z1[(c, h)][:].rearrange("p (m i) -> p m i", i=4)[:, :, 3],
                     lim_t[3][:, 1, m0 : m0 + P],
-                    pages[7 % PAGES][:, m0 : m0 + P],
+                    pages[PAGE_OF[7]][:, m0 : m0 + P],
                     ALU.add,
                 )
             z1_w = held([P, CH], U32, "z1_w%d" % c)
@@ -503,12 +542,12 @@ def tile_list_stowage_bay_score_kernel(
                 score(1, c, n, 0, CH, z1_w[:], z1_s[:], False, n == 3)
             if c + 1 < NCH:
                 quantize_z0(c + 1, tag="z1_%d0" % c)
-                first_score(c + 1, ("CD", "EF", "GH")[c])
+                first_score(c + 1, ("EF", "CD", "AB")[c])
             if c < 2:
                 z1[(NCH - 1, c)] = held([P, 4 * P], BF16, "z1_last%d" % c, tag="z1_%d1" % c)
                 empty_turned(back[NCH - 1], c * P, (c + 1) * P, z1[(NCH - 1, c)][:])
             if c == 0:
-                res = placed([P, 2, 2 * CH], F32, "res0", 5 * UNIT)
+                res = placed([P, 2, 2 * CH], F32, "res0", 5 * UNIT + UNIT // 2)
             else:
                 res = held([P, 2, 2 * CH], F32, "res%d" % c)
             for hf in range(2):

@@ -22,6 +22,7 @@ PASS = 512
 CH = 256
 NCH = T2 // CH
 FIRST_PART = 320
+REST = S - FIRST_PART
 PAGE_OF = (0, 1, 2, 0, 1, 0, 2, 1)
 PAGES = 3
 UNIT = 2048
@@ -104,16 +105,21 @@ def tile_list_stowage_bay_score_kernel(
 
         lim_t = {}
 
+        def lim_rows(b):
+            return lim[PASS * b : PASS * (b + 1), :].rearrange("(p i) m -> p i m", i=4)
+
         def load_lim(k):
             b, u = divmod(k, 2)
-            if k == 0:
-                lim_t[k] = placed([P, 2, T2], F32, "lim0", 22 * UNIT)
-            else:
-                lim_t[k] = held([P, 2, T2], F32, "lim%d" % k)
-            nc.sync.dma_start(
-                out=lim_t[k][:],
-                in_=lim[PASS * b : PASS * (b + 1), :].rearrange("(p i) m -> p i m", i=4)[:, 2 * u : 2 * u + 2, :],
-            )
+            both = held([P, 2, T2], F32, "lim%d" % k)
+            nc.sync.dma_start(out=both[:], in_=lim_rows(b)[:, 2 * u : 2 * u + 2, :])
+            for e in range(2):
+                for c in range(NCH):
+                    lim_t[(2 * k + e, c)] = both[:, e, c * CH : (c + 1) * CH]
+
+        def load_lim_chunks(s, chunks, tile):
+            nc.sync.dma_start(out=tile[:], in_=lim_rows(s // 4)[:, s % 4, chunks[0] * CH : (chunks[-1] + 1) * CH])
+            for place, c in enumerate(chunks):
+                lim_t[(s, c)] = tile[:, place * CH : (place + 1) * CH]
 
         idx = lists.tile([P, S // 16], U16, name="idx")
         idx2 = lists.tile([P, S // 16], U16, name="idx2")
@@ -157,11 +163,15 @@ def tile_list_stowage_bay_score_kernel(
         move_rows(w1_s[1], w1_s[0])
 
         nc.sync.dma_start(idx2[:], offs2)
-        wgt = held([P, S], F32, "wgt")
-        nc.sync.dma_start(out=wgt[:], in_=wgs)
+        wgt_run = held([P, REST + S], F32, "wgt_run")
+        wgt = wgt_run[:, REST : REST + S]
+        nc.sync.dma_start(out=wgt, in_=wgs)
         load_w2(1, 0)
         load_w2(1, 1)
-        load_lim(0)
+        load_lim_chunks(0, (0, 1, 2, 3), held([P, T2], F32, "lim_of0"))
+        load_lim_chunks(1, (0, 1), placed([P, 2 * CH], F32, "lim_of1a", 22 * UNIT))
+        load_lim_chunks(1, (2, 3), held([P, 2 * CH], F32, "lim_of1b"))
+        nc.sync.dma_start(out=wgt_run[:, 0:REST], in_=wgs[:, FIRST_PART:S])
         load_lim(1)
         load_lim(2)
         load_scales(w3_s, w3_scales)
@@ -277,19 +287,16 @@ def tile_list_stowage_bay_score_kernel(
                 larger_one(2 * k + e, both[:, e, :])
 
         def scatter_fused(s):
-            nc.vector.tensor_tensor(pages[PAGE_OF[s]][:].indirect(idx2[:]), neg_h[s], wgt[:], ALU.mult)
+            nc.vector.tensor_tensor(pages[PAGE_OF[s]][:].indirect(idx2[:]), neg_h[s], wgt, ALU.mult)
 
         weighted = {}
 
-        def weigh(s, offset=None):
-            if offset:
-                weighted[s] = placed([P, S], F32, "weighted%d" % s, offset)
-            else:
-                weighted[s] = held([P, S], F32, "weighted%d" % s)
-            nc.gpsimd.tensor_tensor(weighted[s][:], neg_h[s], wgt[:], ALU.mult)
+        def weigh(s, dst):
+            weighted[s] = dst[:]
+            nc.gpsimd.tensor_tensor(weighted[s], neg_h[s], wgt, ALU.mult)
 
         def scatter(s):
-            nc.vector.tensor_copy(pages[PAGE_OF[s]][:].indirect(idx2[:]), weighted[s][:])
+            nc.vector.tensor_copy(pages[PAGE_OF[s]][:].indirect(idx2[:]), weighted[s])
 
         z_t = {}
 
@@ -307,12 +314,11 @@ def tile_list_stowage_bay_score_kernel(
 
         sums = {}
 
-        def turn_limits(k, opens):
-            for c in range(NCH):
-                for slot in range(4):
-                    mb, e = divmod(slot, 2)
-                    m0 = c * CH + mb * P
-                    turn(sums[k][c], slot, lim_t[k][:, e, m0 : m0 + P], opens and slot == 0, False)
+        def turn_limits(s, opens, chunks=range(NCH)):
+            k, e = divmod(s, 2)
+            for c in chunks:
+                for mb in range(2):
+                    turn(sums[k][c], 2 * mb + e, lim_t[(s, c)][:, mb * P : (mb + 1) * P], opens and mb == 0, False)
 
         def turn_page(s, opens, closes):
             k, e = divmod(s, 2)
@@ -360,10 +366,10 @@ def tile_list_stowage_bay_score_kernel(
 
         def quantize_second(u):
             if u == 0:
-                words = held([P, PASS], U32, "second_w0")[:]
+                words = placed([P, PASS], U32, "second_w0", 22 * UNIT)[:]
                 scales = held([P, PASS], U8, "second_s0")
             else:
-                words = placed([P, PASS + 32], U32, "second_w1", 2 * UNIT + UNIT // 2 - 64)[:, 0:PASS]
+                words = held([P, PASS], U32, "second_w1")[:]
                 scales = placed([P, PASS], U8, "second_s1", 13 * UNIT)
             parts = 2 - u
             for part in range(parts):
@@ -375,82 +381,85 @@ def tile_list_stowage_bay_score_kernel(
                 cols = [slice(P * (2 * e + a), P * (2 * e + a + 1)) for e in range(2)]
                 w2_codes[(2 + u, a)] = [(words[:, col], scales[:, col]) for col in cols]
 
+        late_d1 = placed([P, 4 * S], F32, "late_d1", 14 * UNIT)
         for s in range(4, 8):
-            neg_d1[s] = placed([P, S], F32, "late_d1%d" % s, (s + 10) * UNIT)[:]
+            neg_d1[s] = late_d1[:, (s - 4) * S : (s - 3) * S]
         first_product(4)
         first_product(5)
-        quantize_second(0)
-        larger(1, placed([P, 2, S], F32, "neg_h1", 0))
-        second_products(2, "EF")
-        larger_one(4, placed([P, S], F32, "neg_h4", 4 * UNIT + UNIT // 2)[:])
-        first_part = held([P, FIRST_PART], F32, "first_part", tag="w2_raw11")
-        nc.gpsimd.tensor_tensor(first_part[:], neg_h[2][:, 0:FIRST_PART], wgt[:, 0:FIRST_PART], ALU.mult)
-        quantize_second(1)
-        first_product(6)
-        first_product(7)
-
-        neg_d2, gap, excess = {}, {}, {}
-
-        def empty_second(s):
-            neg_d2[s] = held([P, S], F32, "neg_d2%d" % s)
-            nc.scalar.activation(neg_d2[s][:], d2[s][:], ACT.Copy, scale=-1.0)
-
-        def take_gap(s, dst):
-            gap[s] = dst
-            nc.gpsimd.tensor_tensor(gap[s], neg_d1[s], neg_d2[s][:], ALU.subtract)
-
-        def take_excess(s, dst):
-            excess[s] = dst
-            nc.scalar.activation(excess[s][:], gap[s], ACT.Relu)
-
-        def take_larger(s, dst):
-            neg_h[s] = dst[:]
-            nc.gpsimd.tensor_tensor(neg_h[s], neg_d1[s], excess[s][:], ALU.subtract)
-
-        empty_second(5)
-        second_products(3, "GH")
-        empty_second(6)
-        empty_second(7)
-        nc.vector.tensor_copy(pages[2][:].indirect(idx2[:, 0 : FIRST_PART // 16]), first_part[:])
-        weigh(3, 18 * UNIT)
-        take_gap(5, placed([P, S], F32, "gap5", 19 * UNIT + UNIT // 2)[:])
-        take_excess(5, held([P, S], F32, "excess5", tag="neg_d25"))
-        last_part = placed([P, S - FIRST_PART], F32, "last_part", 19 * UNIT)
-        nc.gpsimd.tensor_tensor(last_part[:], neg_h[2][:, FIRST_PART:S], wgt[:, FIRST_PART:S], ALU.mult)
-        place_z_t(0, 2)
         sums[0] = [bank(letter) for letter in "CDAB"]
         turn_page(0, True, False)
         turn_limits(0, False)
+        turn_limits(1, False, (0, 1))
+        quantize_second(0)
+        neg_h324 = placed([P, 3 * S], F32, "neg_h324", 0)
+        larger_one(2, neg_h324[:, S : 2 * S])
+        larger_one(3, neg_h324[:, 0:S])
+        second_products(2, "EF")
+        larger_one(4, neg_h324[:, 2 * S : 3 * S])
+        first_part = held([P, FIRST_PART], F32, "first_part", tag="w2_raw11")
+        nc.gpsimd.tensor_tensor(first_part[:], neg_h[2][:, 0:FIRST_PART], wgt[:, 0:FIRST_PART], ALU.mult)
+        quantize_second(1)
+        turn_limits(1, False, (2, 3))
         turn_page(1, False, True)
-        weigh(4, 21 * UNIT + UNIT // 2)
+
+        def empty_second(s, dst):
+            nc.scalar.activation(dst, d2[s][:], ACT.Copy, scale=-1.0)
+
+        neg_d25 = held([P, S], F32, "neg_d25")
+        taken = {s: held([P, 2 * S], F32, "taken%d" % s) for s in (5, 6)}
+        empty_second(5, neg_d25[:])
+        place_z_t(0, 6)
         round_pair(0)
+        first_product(6)
+        first_product(7)
+        second_products(3, "GH")
+        empty_second(6, taken[5][:, S : 2 * S])
+        empty_second(7, taken[6][:, S : 2 * S])
+        nc.vector.tensor_copy(pages[2][:].indirect(idx2[:, 0 : FIRST_PART // 16]), first_part[:])
+        weigh(3, placed([P, S], F32, "weighted3", 18 * UNIT))
+        gap5 = placed([P, S], F32, "gap5", 19 * UNIT)
+        nc.gpsimd.tensor_tensor(gap5[:], neg_d1[5], neg_d25[:], ALU.subtract)
+        nc.scalar.activation(taken[5][:, 0:S], gap5[:], ACT.Relu)
+        weighted24 = placed([P, REST + S], F32, "weighted24", 20 * UNIT)
+        nc.gpsimd.tensor_tensor(weighted24[:], neg_h324[:, S + FIRST_PART : 3 * S], wgt_run[:], ALU.mult)
+        weighted[4] = weighted24[:, REST : REST + S]
         scatter(3)
-        nc.vector.tensor_copy(pages[2][:].indirect(idx2[:, FIRST_PART // 16 : S // 16]), last_part[:])
-        gap6_span = placed([P, S + 32], F32, "gap6_span", 4 * UNIT + UNIT // 2 - 64)
-        take_gap(6, gap6_span[:, 0:S])
-        take_excess(6, placed([P, S], F32, "excess6", 8 * UNIT + UNIT // 2))
+        nc.vector.tensor_copy(pages[2][:].indirect(idx2[:, FIRST_PART // 16 : S // 16]), weighted24[:, 0:REST])
         place_z_t(1, 4)
-        take_larger(5, placed([P, S], F32, "neg_h5", 23 * UNIT))
-        weigh(5)
-        take_larger(6, held([P, S], F32, "neg_h6"))
-        weigh(6)
-        gap7_span = placed([P, S + 32], F32, "gap7_span", 8 * UNIT + UNIT // 2 - 64)
-        take_gap(7, gap7_span[:, 0:S])
-        for k, letters in ((1, "EFGH"), (2, "CDAB")):
-            sums[k] = [bank(letter) for letter in letters]
-            turn_limits(k, True)
+
+        def take_off(s, dst):
+            nc.gpsimd.tensor_tensor(dst[:], late_d1[:, (s - 4) * S : (s - 2) * S], taken[s][:], ALU.subtract)
+            neg_h[s] = dst[:, 0:S]
+            return dst[:, S : 2 * S]
+
+        gap6 = take_off(5, held([P, 2 * S], F32, "left5"))
+        nc.scalar.activation(taken[6][:, 0:S], gap6, ACT.Relu)
+        weigh(5, held([P, S], F32, "weighted5"))
+        gap7 = take_off(6, placed([P, 2 * S], F32, "left6", 8 * UNIT))
+        weigh(6, held([P, S], F32, "weighted6"))
+        sums[1] = [bank(letter) for letter in "EFGH"]
+        turn_limits(2, True)
+        turn_limits(3, False)
+        back = [bank(letter) for letter in "CDAB"]
+        for c in range(NCH):
+            turn_back(back[c], c, 0)
         turn_page(3, False, False)
         turn_page(2, False, True)
         round_pair(1)
         z0 = [held([P, 4 * CH], BF16, "z0%d" % c) for c in range(NCH)]
         for c in range(NCH):
-            acc = bank("EF"[c % 2])
-            for u in range(2):
-                turn_back(acc, c, u)
-            empty_turned(acc, 0, CH, z0[c][:])
-        take_excess(7, placed([P, S], F32, "excess7", 3 * UNIT))
-        take_larger(7, held([P, S], F32, "neg_h7"))
+            turn_back(back[c], c, 1)
+            empty_turned(back[c], 0, CH, z0[c][:])
+        excess7 = placed([P, S], F32, "excess7", 5 * UNIT)
+        nc.scalar.activation(excess7[:], gap7, ACT.Relu)
+        neg_h[7] = held([P, S], F32, "neg_h7")[:]
+        nc.gpsimd.tensor_tensor(neg_h[7], neg_d1[7], excess7[:], ALU.subtract)
+        for c in range(NCH):
+            z_t[(1, c)] = z_t[(0, c)]
         place_z_t(0, 8)
+        sums[2] = [bank(letter) for letter in "EFGH"]
+        turn_limits(4, True)
+        turn_limits(5, False)
         scatter(4)
         scatter(5)
         turn_page(4, False, False)
@@ -490,13 +499,13 @@ def tile_list_stowage_bay_score_kernel(
                 score(0, c, n, 0, CH, words[:], scales[:], n % 2 == 0, False)
 
         scatter(6)
-        quantize_z0(0, offset=3 * UNIT)
+        quantize_z0(0, offset=5 * UNIT)
 
-        six = [bank(letter) for letter in "GHEF"]
+        six = [bank(letter) for letter in "CDAB"]
         blocks = T2 // P
         for blk in range(blocks):
-            turn(six[blk // 2], blk % 2, lim_t[3][:, 0, blk * P : (blk + 1) * P], blk % 2 == 0, False)
-        back = [bank(letter) for letter in "CDAB"]
+            turn(six[blk // 2], blk % 2, lim_t[(6, blk // 2)][:, blk % 2 * P : (blk % 2 + 1) * P], blk % 2 == 0, False)
+        back = [bank(letter) for letter in "EFGH"]
         for c in range(NCH):
             turn_back(back[c], c, 0)
         for blk in range(blocks):
@@ -520,14 +529,14 @@ def tile_list_stowage_bay_score_kernel(
                 round_six(2)
                 round_six(3)
         scatter_fused(7)
-        first_score(0, "GH")
+        first_score(0, "CD")
 
         for c in range(NCH):
             for h in range(2):
                 m0 = c * CH + h * P
                 nc.vector.tensor_tensor(
                     z1[(c, h)][:].rearrange("p (m i) -> p m i", i=4)[:, :, 3],
-                    lim_t[3][:, 1, m0 : m0 + P],
+                    lim_t[(7, c)][:, h * P : (h + 1) * P],
                     pages[PAGE_OF[7]][:, m0 : m0 + P],
                     ALU.add,
                 )
@@ -542,12 +551,12 @@ def tile_list_stowage_bay_score_kernel(
                 score(1, c, n, 0, CH, z1_w[:], z1_s[:], False, n == 3)
             if c + 1 < NCH:
                 quantize_z0(c + 1, tag="z1_%d0" % c)
-                first_score(c + 1, ("EF", "CD", "AB")[c])
+                first_score(c + 1, ("AB", "EF", "GH")[c])
             if c < 2:
                 z1[(NCH - 1, c)] = held([P, 4 * P], BF16, "z1_last%d" % c, tag="z1_%d1" % c)
                 empty_turned(back[NCH - 1], c * P, (c + 1) * P, z1[(NCH - 1, c)][:])
             if c == 0:
-                res = placed([P, 2, 2 * CH], F32, "res0", 5 * UNIT + UNIT // 2)
+                res = placed([P, 2, 2 * CH], F32, "res0", 7 * UNIT + UNIT // 2)
             else:
                 res = held([P, 2, 2 * CH], F32, "res%d" % c)
             for hf in range(2):

@@ -21,7 +21,7 @@ P = 128
 PASS = 512
 CH = 256
 NCH = T2 // CH
-FIRST_PART = 320
+FIRST_PART = 256
 REST = S - FIRST_PART
 PAGE_OF = (0, 1, 2, 0, 1, 0, 2, 1)
 PAGES = 3
@@ -117,7 +117,7 @@ def tile_list_stowage_bay_score_kernel(
                     lim_t[(2 * k + e, c)] = both[:, e, c * CH : (c + 1) * CH]
 
         def load_lim_chunks(s, chunks, tile):
-            nc.sync.dma_start(out=tile[:], in_=lim_rows(s // 4)[:, s % 4, chunks[0] * CH : (chunks[-1] + 1) * CH])
+            nc.sync.dma_start(out=tile, in_=lim_rows(s // 4)[:, s % 4, chunks[0] * CH : (chunks[-1] + 1) * CH])
             for place, c in enumerate(chunks):
                 lim_t[(s, c)] = tile[:, place * CH : (place + 1) * CH]
 
@@ -164,14 +164,14 @@ def tile_list_stowage_bay_score_kernel(
 
         nc.sync.dma_start(idx2[:], offs2)
         wgt_run = held([P, REST + S], F32, "wgt_run")
-        wgt = wgt_run[:, REST : REST + S]
+        wgt = wgt_run[:, 0:S]
         nc.sync.dma_start(out=wgt, in_=wgs)
         load_w2(1, 0)
         load_w2(1, 1)
-        load_lim_chunks(0, (0, 1, 2, 3), held([P, T2], F32, "lim_of0"))
-        load_lim_chunks(1, (0, 1), placed([P, 2 * CH], F32, "lim_of1a", 22 * UNIT))
-        load_lim_chunks(1, (2, 3), held([P, 2 * CH], F32, "lim_of1b"))
-        nc.sync.dma_start(out=wgt_run[:, 0:REST], in_=wgs[:, FIRST_PART:S])
+        load_lim_chunks(0, (0, 1, 2, 3), held([P, T2], F32, "lim_of0")[:])
+        load_lim_chunks(1, (0, 1), placed([P, 5 * S], F32, "lim_span", 23 * UNIT)[:, 0 : 2 * CH])
+        load_lim_chunks(1, (2, 3), held([P, 2 * CH], F32, "lim_of1b")[:])
+        nc.sync.dma_start(out=wgt_run[:, S : S + REST], in_=wgs[:, 0:REST])
         load_lim(1)
         load_lim(2)
         load_scales(w3_s, w3_scales)
@@ -357,20 +357,20 @@ def tile_list_stowage_bay_score_kernel(
         second_products(1, "GH")
         scatter_fused(1)
 
-        pair2_span = placed([P, 4 * PASS], BF16, "pair2_span", UNIT - 64)
-        pair3_span = placed([P, 8 * PASS], BF16, "pair3_span", 18 * UNIT)
-        w2_second = [pair2_span[:, 0 : 4 * PASS], pair3_span[:, 0 : 4 * PASS]]
+        pair2_rounded = held([P, 4 * PASS], BF16, "pair2_rounded")
+        pair3_span = placed([P, 4 * PASS], BF16, "pair3_span", 18 * UNIT)
+        w2_second = [pair2_rounded[:], pair3_span[:, 0 : 4 * PASS]]
         for u in range(2):
             for a in range(2):
                 round_w2(w2_second[u].rearrange("p (e a m j) -> p a m j e", e=2, a=2, j=4)[:, a], 1, a, u)
 
         def quantize_second(u):
             if u == 0:
-                words = placed([P, PASS], U32, "second_w0", 22 * UNIT)[:]
+                words = placed([P, PASS], U32, "second_w0", 23 * UNIT)[:]
                 scales = held([P, PASS], U8, "second_s0")
             else:
-                words = held([P, PASS], U32, "second_w1")[:]
-                scales = placed([P, PASS], U8, "second_s1", 13 * UNIT)
+                words = placed([P, PASS], U32, "second_w1", 27 * UNIT)[:]
+                scales = held([P, PASS], U8, "second_s1")
             parts = 2 - u
             for part in range(parts):
                 lo, hi = part * PASS // parts, (part + 1) * PASS // parts
@@ -391,16 +391,14 @@ def tile_list_stowage_bay_score_kernel(
         turn_limits(0, False)
         turn_limits(1, False, (0, 1))
         quantize_second(0)
-        neg_h324 = placed([P, 3 * S], F32, "neg_h324", 0)
-        larger_one(2, neg_h324[:, S : 2 * S])
-        larger_one(3, neg_h324[:, 0:S])
-        second_products(2, "EF")
-        larger_one(4, neg_h324[:, 2 * S : 3 * S])
-        first_part = held([P, FIRST_PART], F32, "first_part", tag="w2_raw11")
-        nc.gpsimd.tensor_tensor(first_part[:], neg_h[2][:, 0:FIRST_PART], wgt[:, 0:FIRST_PART], ALU.mult)
+        neg_h423 = placed([P, 3 * S], F32, "neg_h423", 24 * UNIT)
+        larger_one(2, neg_h423[:, S : 2 * S])
         quantize_second(1)
-        turn_limits(1, False, (2, 3))
-        turn_page(1, False, True)
+        larger_one(3, neg_h423[:, 2 * S : 3 * S])
+        second_products(2, "EF")
+        larger_one(4, neg_h423[:, 0:S])
+        first_part = placed([P, FIRST_PART], F32, "first_part", 18 * UNIT)
+        nc.gpsimd.tensor_tensor(first_part[:], neg_h[2][:, REST:S], wgt[:, REST:S], ALU.mult)
 
         def empty_second(s, dst):
             nc.scalar.activation(dst, d2[s][:], ACT.Copy, scale=-1.0)
@@ -408,23 +406,25 @@ def tile_list_stowage_bay_score_kernel(
         neg_d25 = held([P, S], F32, "neg_d25")
         taken = {s: held([P, 2 * S], F32, "taken%d" % s) for s in (5, 6)}
         empty_second(5, neg_d25[:])
-        place_z_t(0, 6)
-        round_pair(0)
         first_product(6)
         first_product(7)
         second_products(3, "GH")
         empty_second(6, taken[5][:, S : 2 * S])
+        nc.vector.tensor_copy(pages[2][:].indirect(idx2[:, REST // 16 : S // 16]), first_part[:])
+        weigh(3, placed([P, S], F32, "weighted3", 19 * UNIT))
+        gap5 = neg_h[3]
+        nc.gpsimd.tensor_tensor(gap5, neg_d1[5], neg_d25[:], ALU.subtract)
+        nc.scalar.activation(taken[5][:, 0:S], gap5, ACT.Relu)
         empty_second(7, taken[6][:, S : 2 * S])
-        nc.vector.tensor_copy(pages[2][:].indirect(idx2[:, 0 : FIRST_PART // 16]), first_part[:])
-        weigh(3, placed([P, S], F32, "weighted3", 18 * UNIT))
-        gap5 = placed([P, S], F32, "gap5", 19 * UNIT)
-        nc.gpsimd.tensor_tensor(gap5[:], neg_d1[5], neg_d25[:], ALU.subtract)
-        nc.scalar.activation(taken[5][:, 0:S], gap5[:], ACT.Relu)
-        weighted24 = placed([P, REST + S], F32, "weighted24", 20 * UNIT)
-        nc.gpsimd.tensor_tensor(weighted24[:], neg_h324[:, S + FIRST_PART : 3 * S], wgt_run[:], ALU.mult)
-        weighted[4] = weighted24[:, REST : REST + S]
+        weighted24 = held([P, REST + S], F32, "weighted24", tag="neg_d25")
+        nc.gpsimd.tensor_tensor(weighted24[:], neg_h423[:, 0 : S + REST], wgt_run[:], ALU.mult)
+        weighted[4] = weighted24[:, 0:S]
+        turn_limits(1, False, (2, 3))
+        turn_page(1, False, True)
+        place_z_t(0, 6)
+        round_pair(0)
         scatter(3)
-        nc.vector.tensor_copy(pages[2][:].indirect(idx2[:, FIRST_PART // 16 : S // 16]), weighted24[:, 0:REST])
+        nc.vector.tensor_copy(pages[2][:].indirect(idx2[:, 0 : REST // 16]), weighted24[:, S : S + REST])
         place_z_t(1, 4)
 
         def take_off(s, dst):

from contextlib import ExitStack

import concourse.mybir as mybir
from concourse.masks import make_identity

K, T, S, T2, H, N = 1024, 2048, 512, 1024, 1024, 512
FLOPS = 2 * (2 * K * H * S + H * N * T2)

F32 = mybir.dt.float32
BF16 = mybir.dt.bfloat16
I32 = mybir.dt.int32
U32 = mybir.dt.uint32
U16 = mybir.dt.uint16
U8 = mybir.dt.uint8
FP8X4 = mybir.dt.float8_e4m3fn_x4
FP4X4 = mybir.dt.float4_e2m1fn_x4
ALU = mybir.AluOpType
ACT = mybir.ActivationFunctionType

P = 128
PASS = 512
CH = 256
NCH = T2 // CH
FIRST_PART = 256
REST = S - FIRST_PART
PAGE_OF = (0, 1, 2, 0, 1, 0, 2, 1)
PAGES = 3
UNIT = 2048


def tile_list_stowage_bay_score_kernel(
    tc, tab_words, tab_scales, offs, w1_words, w1_scales, w2, offs2, wgs, lim, w3_words, w3_scales, out
):
    nc = tc.nc
    with ExitStack() as ctx:
        lists = ctx.enter_context(tc.tile_pool(name="lists", bufs=1))
        keep = ctx.enter_context(tc.tile_pool(name="keep", bufs=1))
        shared = ctx.enter_context(tc.tile_pool(name="shared", bufs=1))
        psum = ctx.enter_context(tc.psum_pool(name="psum", bufs=1))

        def held(shape, dtype, name, tag=None):
            return keep.tile(shape, dtype, name=name, tag=tag or name, align_bytes=64)

        def placed(shape, dtype, name, offset):
            return shared.tile(shape, dtype, name=name, offset=offset, align_bytes=64)

        def bank(letter):
            return psum.tile([P, 512], F32, name="bank", tag=letter)

        tab_s = held([P, 2 * T], U8, "tab_s")
        w1_s_raw = held([P, H], U8, "w1_s_raw")
        w3_s = held([P, 2 * N], U8, "w3_s")
        moved_s = held([P, 2 * S], U8, "moved_s")
        w1_s = [held([P, H], U8, "w1_s%d" % b) for b in range(2)]
        for scale_tile in (tab_s, w1_s_raw, moved_s, w1_s[1], w3_s):
            nc.vector.memset(scale_tile[:].bitcast(I32), 0)

        pages = [held([P, T2], F32, "page%d" % i) for i in range(PAGES)]
        for page in pages:
            nc.vector.memset(page[:].bitcast(I32), 0)
        ident = held([P, P], F32, "ident")
        make_identity(nc, ident[:])

        def load_scales(tile, src):
            for r in range(4):
                nc.sync.dma_start(
                    out=tile[r:P:32, :].bitcast(I32).rearrange("q (a c) -> q a c", a=2),
                    in_=src[:, r:16:4, :].rearrange("a q c -> q a c").bitcast(I32),
                )

        def load_spread(tile, src):
            nc.sync.dma_start(
                out=tile[4:P:8, :].bitcast(I32).rearrange("q (a c) -> q a c", a=2),
                in_=src.rearrange("a q c -> q a c").bitcast(I32),
            )

        def move_rows(dst, src):
            for r in range(4):
                nc.sync.dma_start(out=dst[r:P:32, :].bitcast(I32), in_=src[8 * r + 4 : P : 32, :].bitcast(I32))

        tab_w = [held([P, T], I32, "tab_w%d" % a) for a in range(2)]

        def load_table(a):
            nc.sync.dma_start(out=tab_w[a][:], in_=tab_words[a].rearrange("p t i -> p (t i)").bitcast(I32))

        w1_w_raw = [held([P, H // 2], I32, "w1_w_raw%d" % b) for b in range(2)]

        def load_w1(b):
            nc.sync.dma_start(
                out=w1_w_raw[b][:].rearrange("p (a c) -> p a c", a=2),
                in_=w1_words[:, :, H * b : H * (b + 1)].rearrange("a p c -> p a c").bitcast(I32),
            )

        def w2_block(b, a):
            return w2[PASS * a : PASS * (a + 1), PASS * b : PASS * (b + 1)].rearrange("(p j) c -> p j c", j=4)

        w2_raw = {}

        def load_w2(b, a):
            if a == 0:
                w2_raw[(b, a)] = placed([P, 4, PASS], F32, "w2_raw%d0" % b, (10 + 4 * b) * UNIT)
            else:
                w2_raw[(b, a)] = held([P, 4, PASS], F32, "w2_raw%d%d" % (b, a))
            nc.sync.dma_start(out=w2_raw[(b, a)][:], in_=w2_block(b, a))

        lim_t = {}

        def lim_rows(b):
            return lim[PASS * b : PASS * (b + 1), :].rearrange("(p i) m -> p i m", i=4)

        def load_lim(k):
            b, u = divmod(k, 2)
            both = held([P, 2, T2], F32, "lim%d" % k)
            nc.sync.dma_start(out=both[:], in_=lim_rows(b)[:, 2 * u : 2 * u + 2, :])
            for e in range(2):
                for c in range(NCH):
                    lim_t[(2 * k + e, c)] = both[:, e, c * CH : (c + 1) * CH]

        def load_lim_chunks(s, chunks, tile):
            nc.sync.dma_start(out=tile, in_=lim_rows(s // 4)[:, s % 4, chunks[0] * CH : (chunks[-1] + 1) * CH])
            for place, c in enumerate(chunks):
                lim_t[(s, c)] = tile[:, place * CH : (place + 1) * CH]

        idx = lists.tile([P, S // 16], U16, name="idx")
        idx2 = lists.tile([P, S // 16], U16, name="idx2")
        load_table(0)
        nc.sync.dma_start(idx[:], offs)
        load_spread(tab_s, tab_scales)
        load_w1(0)
        load_table(1)
        load_scales(w1_s_raw, w1_scales[:, :, 0:PASS])
        load_spread(w1_s_raw, w1_scales[:, :, PASS:H])
        load_w2(0, 0)
        picked_s = held([P, 2 * S], U8, "picked_s")
        for a in range(2):
            nc.vector.tensor_copy(picked_s[:, a * S : (a + 1) * S], tab_s[:, a * T : (a + 1) * T].indirect(idx[:]))
        move_rows(moved_s, picked_s)
        v_s = [moved_s[:, a * S : (a + 1) * S] for a in range(2)]
        w2_rows = [held([P, 2, PASS], F32, "w2_rows%d" % v) for v in range(2)]
        for v in range(2):
            nc.sync.dma_start(out=w2_rows[v][:], in_=w2_block(0, 1)[:, 2 * v : 2 * v + 2, :])
        load_w1(1)

        w1_w = {}

        def order_w1_words(copy, b, a, tag=None):
            w1_w[(b, a)] = held([P, H], U8, "w1_w%d%d" % (b, a), tag=tag)
            copy(
                out=w1_w[(b, a)][:].bitcast(U16).rearrange("p (i m) -> p i m", i=4),
                in_=w1_w_raw[b][:].bitcast(U16).rearrange("p (a m i) -> p a i m", a=2, i=4)[:, a],
            )

        v_w = [held([P, S], U32, "v_w0", tag="tab_s"), None]
        nc.vector.tensor_copy(v_w[0][:], tab_w[0][:].bitcast(U32).indirect(idx[:]))
        for a in range(2):
            order_w1_words(nc.scalar.copy, 0, a)
        nc.vector.tensor_copy(
            out=w1_s[0][:].rearrange("p (a i m) -> p a i m", a=2, i=4),
            in_=w1_s_raw[:].rearrange("p (a m i) -> p a i m", a=2, i=4),
        )
        v_w[1] = held([P, S], U32, "v_w1", tag="w1_s_raw")
        nc.vector.tensor_copy(v_w[1][:], tab_w[1][:].bitcast(U32).indirect(idx[:]))
        move_rows(w1_s[1], w1_s[0])

        nc.sync.dma_start(idx2[:], offs2)
        wgt_run = held([P, REST + S], F32, "wgt_run")
        wgt = wgt_run[:, 0:S]
        nc.sync.dma_start(out=wgt, in_=wgs)
        load_w2(1, 0)
        load_w2(1, 1)
        load_lim_chunks(0, (0, 1, 2, 3), held([P, T2], F32, "lim_of0")[:])
        load_lim_chunks(1, (0, 1), placed([P, 5 * S], F32, "lim_span", 23 * UNIT)[:, 0 : 2 * CH])
        load_lim_chunks(1, (2, 3), held([P, 2 * CH], F32, "lim_of1b")[:])
        nc.sync.dma_start(out=wgt_run[:, S : S + REST], in_=wgs[:, 0:REST])
        load_lim(1)
        load_lim(2)
        load_scales(w3_s, w3_scales)
        load_lim(3)
        w3_w = held([P, 2 * N], I32, "w3_w")
        nc.sync.dma_start(
            out=w3_w[:].rearrange("p (b c) -> p b c", b=2),
            in_=w3_words.rearrange("b p c i -> p b (c i)").bitcast(I32),
        )

        neg_d1 = {}

        def first_product(s):
            b, i = divmod(s, 4)
            d1 = bank("GHEFEFGH"[s])
            for a in range(2):
                col = a * PASS + i * P
                nc.tensor.matmul_mx(
                    out=d1[:],
                    lhsT=w1_w[(b, a)][:, 2 * i * P : 2 * (i + 1) * P].bitcast(FP4X4),
                    lhsT_scale=w1_s[b][:, col : col + P],
                    rhs=v_w[a][:].bitcast(FP8X4),
                    rhs_scale=v_s[a],
                    start=(a == 0),
                    stop=(a == 1),
                )
            nc.scalar.activation(neg_d1[s], d1[:], ACT.Copy, scale=-1.0)

        def round_w2(dst, b, a, u):
            nc.scalar.activation(
                dst,
                w2_raw[(b, a)][:].rearrange("p j (m i) -> p m j i", i=4)[:, :, :, 2 * u : 2 * u + 2],
                ACT.Copy,
            )

        w2_first = {au: held([P, 2 * PASS], BF16, "w2_first%d%d" % au) for au in ((0, 0), (0, 1), (1, 1))}
        w2_last = [held([P, PASS], BF16, "w2_last%d" % e) for e in range(2)]
        w2_codes = {}

        def round_w2_rows(v, u):
            src = w2_rows[v][:].rearrange("p j (m i) -> p m i j", i=4)[:, :, 2 * u : 2 * u + 2, :]
            if u == 0:
                for e in range(2):
                    dst = w2_last[e][:].rearrange("p (m j) -> p m j", j=4)[:, :, 2 * v : 2 * v + 2]
                    nc.vector.tensor_copy(out=dst, in_=src[:, :, e, :])
                return
            dst = w2_first[(1, u)][:].rearrange("p (e m j) -> p m e j", e=2, j=4)[:, :, :, 2 * v : 2 * v + 2]
            nc.scalar.activation(dst, src, ACT.Copy)

        def quantize_first(a, u):
            if (a, u) == (1, 1):
                words = placed([P, 2 * P], U32, "first_w11", 11 * UNIT)
            else:
                words = held([P, 2 * P], U32, "first_w%d%d" % (a, u))
            scales = held([P, 2 * P], U8, "first_s%d%d" % (a, u))
            nc.vector.quantize_mx(out=words[:].bitcast(FP8X4), scales=scales[:], in_=w2_first[(a, u)][:])
            w2_codes[(u, a)] = [(words[:, e * P : (e + 1) * P], scales[:, e * P : (e + 1) * P]) for e in range(2)]

        def quantize_last():
            w2_codes[(0, 1)] = []
            for e in range(2):
                words = held([P, P], U32, "last_w%d" % e)
                scales = held([P, P], U8, "last_s%d" % e)
                nc.vector.quantize_mx(out=words[:].bitcast(FP8X4), scales=scales[:], in_=w2_last[e][:])
                w2_codes[(0, 1)].append((words[:], scales[:]))

        round_w2(w2_first[(0, 0)][:].rearrange("p (e m j) -> p m j e", e=2, j=4), 0, 0, 0)
        nc.vector.tensor_copy(
            out=w2_first[(0, 1)][:].rearrange("p (e m j) -> p m j e", e=2, j=4),
            in_=w2_raw[(0, 0)][:].rearrange("p j (m i) -> p m j i", i=4)[:, :, :, 2:4],
        )
        for s in range(4):
            neg_d1[s] = placed([P, S], F32, "early_d1%d" % s, (10 + s) * UNIT)[:]
        first_product(0)
        first_product(1)
        quantize_first(0, 1)
        round_w2_rows(0, 0)
        quantize_first(0, 0)
        round_w2_rows(0, 1)
        round_w2_rows(1, 0)
        quantize_last()
        round_w2_rows(1, 1)

        d2 = {}

        def second_products(k, letters):
            for e in range(2):
                d2[2 * k + e] = bank(letters[e])
            passes = (1, 0) if k == 1 else (0, 1)
            order = [(a, e) for a in passes for e in range(2)] if k == 0 else [(a, e) for e in range(2) for a in passes]
            for a, e in order:
                words, scales = w2_codes[(k, a)][e]
                nc.tensor.matmul_mx(
                    out=d2[2 * k + e][:],
                    lhsT=words.bitcast(FP8X4),
                    lhsT_scale=scales,
                    rhs=v_w[a][:].bitcast(FP8X4),
                    rhs_scale=v_s[a],
                    start=(a == passes[0]),
                    stop=(a == passes[1]),
                )

        neg_h = {}

        def larger_one(s, dst):
            neg_h[s] = dst
            nc.vector.scalar_tensor_tensor(
                out=neg_h[s], in0=d2[s][:], scalar=-1.0, in1=neg_d1[s], op0=ALU.mult, op1=ALU.min
            )

        def larger(k, both):
            for e in range(2):
                larger_one(2 * k + e, both[:, e, :])

        def scatter_fused(s):
            nc.vector.tensor_tensor(pages[PAGE_OF[s]][:].indirect(idx2[:]), neg_h[s], wgt, ALU.mult)

        weighted = {}

        def weigh(s, dst):
            weighted[s] = dst[:]
            nc.gpsimd.tensor_tensor(weighted[s], neg_h[s], wgt, ALU.mult)

        def scatter(s):
            nc.vector.tensor_copy(pages[PAGE_OF[s]][:].indirect(idx2[:]), weighted[s])

        z_t = {}

        def place_z_t(u, unit):
            for c in range(NCH):
                z_t[(u, c)] = placed([P, CH], F32, "z_t%d%d" % (unit, c), unit * UNIT + c * UNIT // 2)

        def z_t_pairs(u, c):
            return z_t[(u, c)][:].bitcast(BF16).rearrange("m (mb q e) -> m mb q e", mb=2, e=2)

        def turn(acc, slot, src, start, stop):
            nc.tensor.matmul(
                out=acc[:, slot * P : (slot + 1) * P], lhsT=src, rhs=ident[:], is_transpose=True, start=start, stop=stop
            )

        sums = {}

        def turn_limits(s, opens, chunks=range(NCH)):
            k, e = divmod(s, 2)
            for c in chunks:
                for mb in range(2):
                    turn(sums[k][c], 2 * mb + e, lim_t[(s, c)][:, mb * P : (mb + 1) * P], opens and mb == 0, False)

        def turn_page(s, opens, closes):
            k, e = divmod(s, 2)
            for c in range(NCH):
                for mb in range(2):
                    slot = 2 * mb + e
                    m0 = c * CH + mb * P
                    turn(sums[k][c], slot, pages[PAGE_OF[s]][:, m0 : m0 + P], opens and slot == 0, closes and mb == 1)

        def round_pair(k):
            for c in range(NCH):
                nc.scalar.copy(
                    out=z_t_pairs(k % 2, c), in_=sums[k][c][:].rearrange("m (mb e q) -> m mb q e", mb=2, e=2)
                )

        def turn_back(acc, c, u):
            for mb in range(2):
                nc.tensor.transpose(
                    acc[:, u * CH + mb * P : u * CH + (mb + 1) * P], z_t[(u, c)][:, mb * P : (mb + 1) * P], ident[:]
                )

        def empty_turned(acc, m0, m1, dst):
            nc.scalar.copy(
                out=dst.bitcast(F32).rearrange("p (m u) -> p m u", u=2),
                in_=acc[:].rearrange("p (u m) -> p m u", u=2)[:, m0:m1],
            )

        second_products(0, "EF")
        for a in range(2):
            order_w1_words(nc.vector.tensor_copy, 1, a, tag="w2_last%d" % a)
        larger(0, held([P, 2, S], F32, "neg_h0"))
        scatter_fused(0)
        quantize_first(1, 1)
        first_product(2)
        first_product(3)
        second_products(1, "GH")
        scatter_fused(1)

        pair2_rounded = held([P, 4 * PASS], BF16, "pair2_rounded")
        pair3_span = placed([P, 4 * PASS], BF16, "pair3_span", 18 * UNIT)
        w2_second = [pair2_rounded[:], pair3_span[:, 0 : 4 * PASS]]
        for u in range(2):
            for a in range(2):
                round_w2(w2_second[u].rearrange("p (e a m j) -> p a m j e", e=2, a=2, j=4)[:, a], 1, a, u)

        def quantize_second(u):
            if u == 0:
                words = placed([P, PASS], U32, "second_w0", 23 * UNIT)[:]
                scales = held([P, PASS], U8, "second_s0")
            else:
                words = placed([P, PASS], U32, "second_w1", 27 * UNIT)[:]
                scales = held([P, PASS], U8, "second_s1")
            parts = 2 - u
            for part in range(parts):
                lo, hi = part * PASS // parts, (part + 1) * PASS // parts
                nc.vector.quantize_mx(
                    out=words[:, lo:hi].bitcast(FP8X4), scales=scales[:, lo:hi], in_=w2_second[u][:, 4 * lo : 4 * hi]
                )
            for a in range(2):
                cols = [slice(P * (2 * e + a), P * (2 * e + a + 1)) for e in range(2)]
                w2_codes[(2 + u, a)] = [(words[:, col], scales[:, col]) for col in cols]

        late_d1 = placed([P, 4 * S], F32, "late_d1", 14 * UNIT)
        for s in range(4, 8):
            neg_d1[s] = late_d1[:, (s - 4) * S : (s - 3) * S]
        first_product(4)
        first_product(5)
        sums[0] = [bank(letter) for letter in "CDAB"]
        turn_page(0, True, False)
        turn_limits(0, False)
        turn_limits(1, False, (0, 1))
        quantize_second(0)
        neg_h423 = placed([P, 3 * S], F32, "neg_h423", 24 * UNIT)
        larger_one(2, neg_h423[:, S : 2 * S])
        quantize_second(1)
        larger_one(3, neg_h423[:, 2 * S : 3 * S])
        second_products(2, "EF")
        larger_one(4, neg_h423[:, 0:S])
        first_part = placed([P, FIRST_PART], F32, "first_part", 18 * UNIT)
        nc.gpsimd.tensor_tensor(first_part[:], neg_h[2][:, REST:S], wgt[:, REST:S], ALU.mult)

        def empty_second(s, dst):
            nc.scalar.activation(dst, d2[s][:], ACT.Copy, scale=-1.0)

        neg_d25 = held([P, S], F32, "neg_d25")
        taken = {s: held([P, 2 * S], F32, "taken%d" % s) for s in (5, 6)}
        empty_second(5, neg_d25[:])
        first_product(6)
        first_product(7)
        second_products(3, "GH")
        empty_second(6, taken[5][:, S : 2 * S])
        nc.vector.tensor_copy(pages[2][:].indirect(idx2[:, REST // 16 : S // 16]), first_part[:])
        weigh(3, placed([P, S], F32, "weighted3", 19 * UNIT))
        gap5 = neg_h[3]
        nc.gpsimd.tensor_tensor(gap5, neg_d1[5], neg_d25[:], ALU.subtract)
        nc.scalar.activation(taken[5][:, 0:S], gap5, ACT.Relu)
        empty_second(7, taken[6][:, S : 2 * S])
        weighted24 = held([P, REST + S], F32, "weighted24", tag="neg_d25")
        nc.gpsimd.tensor_tensor(weighted24[:], neg_h423[:, 0 : S + REST], wgt_run[:], ALU.mult)
        weighted[4] = weighted24[:, 0:S]
        turn_limits(1, False, (2, 3))
        turn_page(1, False, True)
        place_z_t(0, 6)
        round_pair(0)
        scatter(3)
        nc.vector.tensor_copy(pages[2][:].indirect(idx2[:, 0 : REST // 16]), weighted24[:, S : S + REST])
        place_z_t(1, 4)

        def take_off(s, dst):
            nc.gpsimd.tensor_tensor(dst[:], late_d1[:, (s - 4) * S : (s - 2) * S], taken[s][:], ALU.subtract)
            neg_h[s] = dst[:, 0:S]
            return dst[:, S : 2 * S]

        gap6 = take_off(5, held([P, 2 * S], F32, "left5"))
        nc.scalar.activation(taken[6][:, 0:S], gap6, ACT.Relu)
        weigh(5, held([P, S], F32, "weighted5"))
        gap7 = take_off(6, placed([P, 2 * S], F32, "left6", 8 * UNIT))
        weigh(6, held([P, S], F32, "weighted6"))
        sums[1] = [bank(letter) for letter in "EFGH"]
        turn_limits(2, True)
        turn_limits(3, False)
        back = [bank(letter) for letter in "CDAB"]
        for c in range(NCH):
            turn_back(back[c], c, 0)
        turn_page(3, False, False)
        turn_page(2, False, True)
        round_pair(1)
        z0 = [held([P, 4 * CH], BF16, "z0%d" % c) for c in range(NCH)]
        for c in range(NCH):
            turn_back(back[c], c, 1)
            empty_turned(back[c], 0, CH, z0[c][:])
        excess7 = placed([P, S], F32, "excess7", 5 * UNIT)
        nc.scalar.activation(excess7[:], gap7, ACT.Relu)
        neg_h[7] = held([P, S], F32, "neg_h7")[:]
        nc.gpsimd.tensor_tensor(neg_h[7], neg_d1[7], excess7[:], ALU.subtract)
        for c in range(NCH):
            z_t[(1, c)] = z_t[(0, c)]
        place_z_t(0, 8)
        sums[2] = [bank(letter) for letter in "EFGH"]
        turn_limits(4, True)
        turn_limits(5, False)
        scatter(4)
        scatter(5)
        turn_page(4, False, False)
        turn_page(5, False, True)
        round_pair(2)
        z0_codes = {}

        def quantize_z0(c, tag=None, offset=None):
            if offset is None:
                words = held([P, CH], U32, "z0_w%d" % c, tag=tag)
            else:
                words = placed([P, CH], U32, "z0_w%d" % c, offset)
            scales = held([P, CH], U8, "z0_s%d" % c)
            nc.vector.quantize_mx(out=words[:].bitcast(FP8X4), scales=scales[:], in_=z0[c][:])
            z0_codes[c] = (words, scales)


        y = {}

        def score(b, c, n, lo, hi, codes, scales, start, stop):
            col = b * N + n * P
            nc.tensor.matmul_mx(
                out=y[(c, n // 2)][:, (n % 2) * CH + lo : (n % 2) * CH + hi],
                lhsT=w3_w[:, col : col + P].bitcast(FP8X4),
                lhsT_scale=w3_s[:, col : col + P],
                rhs=codes.bitcast(FP8X4),
                rhs_scale=scales,
                start=start,
                stop=stop,
            )

        def first_score(c, letters):
            words, scales = z0_codes[c]
            for n in range(4):
                if n % 2 == 0:
                    y[(c, n // 2)] = bank(letters[n // 2])
                score(0, c, n, 0, CH, words[:], scales[:], n % 2 == 0, False)

        scatter(6)
        quantize_z0(0, offset=5 * UNIT)

        six = [bank(letter) for letter in "CDAB"]
        blocks = T2 // P
        for blk in range(blocks):
            turn(six[blk // 2], blk % 2, lim_t[(6, blk // 2)][:, blk % 2 * P : (blk % 2 + 1) * P], blk % 2 == 0, False)
        back = [bank(letter) for letter in "EFGH"]
        for c in range(NCH):
            turn_back(back[c], c, 0)
        for blk in range(blocks):
            turn(six[blk // 2], blk % 2, pages[PAGE_OF[6]][:, blk * P : (blk + 1) * P], False, blk % 2 == 1)

        def round_six(c):
            nc.scalar.copy(
                out=z_t_pairs(1, c)[:, :, :, 0],
                in_=six[c][:, 0:CH].rearrange("m (mb q) -> m mb q", mb=2),
            )

        z1 = {(c, h): held([P, 4 * P], BF16, "z1_%d%d" % (c, h)) for c in range(NCH - 1) for h in range(2)}
        round_six(0)
        round_six(1)
        for c in range(NCH):
            turn_back(back[c], c, 1)
            if c + 1 < NCH:
                for h in range(2):
                    empty_turned(back[c], h * P, (h + 1) * P, z1[(c, h)][:])
            if c == 0:
                round_six(2)
                round_six(3)
        scatter_fused(7)
        first_score(0, "CD")

        for c in range(NCH):
            for h in range(2):
                m0 = c * CH + h * P
                nc.vector.tensor_tensor(
                    z1[(c, h)][:].rearrange("p (m i) -> p m i", i=4)[:, :, 3],
                    lim_t[(7, c)][:, h * P : (h + 1) * P],
                    pages[PAGE_OF[7]][:, m0 : m0 + P],
                    ALU.add,
                )
            z1_w = held([P, CH], U32, "z1_w%d" % c)
            z1_s = held([P, CH], U8, "z1_s%d" % c)
            for h in range(2):
                lo, hi = h * P, (h + 1) * P
                nc.vector.quantize_mx(out=z1_w[:, lo:hi].bitcast(FP8X4), scales=z1_s[:, lo:hi], in_=z1[(c, h)][:])
                for n in range(2):
                    score(1, c, n, lo, hi, z1_w[:, lo:hi], z1_s[:, lo:hi], False, h == 1 and n == 1)
            for n in range(2, 4):
                score(1, c, n, 0, CH, z1_w[:], z1_s[:], False, n == 3)
            if c + 1 < NCH:
                quantize_z0(c + 1, tag="z1_%d0" % c)
                first_score(c + 1, ("AB", "EF", "GH")[c])
            if c < 2:
                z1[(NCH - 1, c)] = held([P, 4 * P], BF16, "z1_last%d" % c, tag="z1_%d1" % c)
                empty_turned(back[NCH - 1], c * P, (c + 1) * P, z1[(NCH - 1, c)][:])
            if c == 0:
                res = placed([P, 2, 2 * CH], F32, "res0", 7 * UNIT + UNIT // 2)
            else:
                res = held([P, 2, 2 * CH], F32, "res%d" % c)
            for hf in range(2):
                step = 1 if (c, hf) in ((0, 0), (NCH - 1, 1)) else 2
                for n0 in range(0, 2, step):
                    part = slice(n0 * CH, (n0 + step) * CH)
                    rows = slice(P * (2 * hf + n0), P * (2 * hf + n0 + step))
                    nc.scalar.activation(res[:, hf, part], y[(c, hf)][:, part], ACT.Square)
                    nc.sync.dma_start(
                        out=out[rows, c * CH : (c + 1) * CH].rearrange("(n p) m -> p n m", p=P),
                        in_=res[:, hf, part].rearrange("p (n m) -> p n m", n=step),
                    )
